import numpy as np, ml_dtypes
CORES = [23,119,17,113]
N = 4
BF = ml_dtypes.bfloat16
def gentries(a):
    return np.ascontiguousarray(a.reshape(8, 16, -1).transpose(0, 2, 1)).reshape(8, -1)
def gtable(e):
    e = np.asarray(e); return np.ascontiguousarray(e.reshape(8, -1, 16).transpose(0, 2, 1)).reshape(128, -1).astype(np.int32)
V0, M, RO, H, S = 1664, 128, 3, 2, 2
V = V0 + RO * M
def parts(rng):
    m = rng.integers(0, 256, (N, 8, 12, 16)); c = rng.integers(0, 12, (N, 8, V, 1))
    x = np.clip(np.take_along_axis(m, c, 2) + rng.integers(-60, 61, (N, 8, V, 16)), 0, 255)
    y = rng.integers(0, 257, (N, 8, V0, 16)) * 0.00390625
    nx = np.argsort(rng.random((N, 8, 8, V0)), axis=-1)
    few = np.take_along_axis(rng.integers(0, V0, (N, 8, 6)), rng.integers(0, 6, (N, 8, RO * M)), 2).reshape(N, 8, RO, M)
    st = np.where(rng.random((N, 8, RO, M)) < 0.25, few, rng.integers(0, V0, (N, 8, RO, M)))
    return x, y, nx, st
def pack(x, y, nx, st):
    return {"x": np.ascontiguousarray(x.transpose(0, 1, 3, 2)).reshape(N, 128, V).astype(np.float32).astype(BF),
            "y0": np.ascontiguousarray(y.transpose(0, 1, 3, 2)).reshape(N, 128, V0).astype(np.float32).astype(BF),
            "nx0": np.ascontiguousarray(nx.reshape(N, 64, V0)).astype(np.int32), "st": np.stack([gtable(a.reshape(8, -1)) for a in st])}
def setup_inputs(rng):
    return pack(*parts(rng))
def setup_inputs_spread(rng):
    x, y, nx, st = parts(rng)
    x = (np.exp2(rng.integers(0, 9, (N, 8, V, 1))) * rng.random((N, 8, V, 16))).astype(np.int64)
    y = rng.integers(128, 256, (N, 8, V0, 16)) * np.exp2(-7.0 - rng.integers(1, 4, (N, 8, V0, 1)))
    y = y * (rng.random((N, 8, V0, 1)) > 0.0625)
    u = 4 * rng.integers(32, 64, (N, 2, V0, 16)) + 1; u[:, :, 1::2] += 2
    y[:, 1::4] = u * 0.0001220703125
    nx[:, 1::4, :, 0::2] = 2 * np.argsort(rng.random((N, 2, 8, V0 // 2)), axis=-1) + 1
    nx[:, 1::4, :, 1::2] = 2 * np.argsort(rng.random((N, 2, 8, V0 // 2)), axis=-1)
    st = (V0 * rng.random((N, 8, RO, M)) ** 3).astype(np.int64)
    return pack(x, y, nx, st)
def link(p, a, b):
    i = np.flatnonzero(p == b)[0]; p[i] = p[a]; p[a] = b
def setup_inputs_ends(rng):
    x, y, nx, st = parts(rng); L = V0 - 1
    for q in range(N):
        for g in range(8):
            for k in range(8):
                if k % 4 in (0, 2): link(nx[q, g, k], 0, L)
                if k % 4 in (1, 2): link(nx[q, g, k], L, 0)
                if k % 4 == 3: link(nx[q, g, k], L, L); link(nx[q, g, k], 0, 0)
    pv = np.argsort(nx, axis=-1)
    e = 255 * rng.integers(0, 2, (N, 8, V, 16)); e[:, 1::2] = 255 * rng.integers(0, 2, (N, 4, V, 1))
    n = (rng.random((N, 4, V, 16)) < 0.25) * rng.integers(1, 3, (N, 4, V, 16)); e[:, 0::2] += np.where(e[:, 0::2] > 0, -n, n)
    for q in range(N):
        for g, b in ((3, 0), (5, 255), (7, 0)):
            e[q, g, nx[q, g, :, L]] = b; e[q, g, pv[q, g, :, L]] = b
    e[:, :, 0] = 0; e[:, :, L] = 0
    for v in (V0, V0 + M - 1, V - M, V - 1): e[:, :, v] = 255
    st = np.where(rng.random(st.shape) < 0.8, L * rng.integers(0, 2, st.shape), st); st[..., 0] = 0; st[..., M - 1] = L
    p = np.full((1, 8, 1, 1), 0.5); p[0, 2] = 0.96875; p[0, 7] = 0.96875; p[0, 3] = 0.03125
    y = (rng.random((N, 8, V0, 16)) < p) * 1.0
    return pack(e, y, nx, st)
def corner(rng, c):
    a = np.arange(V0); o = rng.permutation(V0); p = np.arange(V0)
    if c == 0: return a
    if c == 1: return (a + 1) % V0
    if c == 2: return (a - 1) % V0
    if c == 3: return a ^ 1
    if c == 4: return V0 - 1 - a
    if c == 5: p[o] = np.roll(o, -1)
    if c == 6: p[o[0::2]] = o[1::2]; p[o[1::2]] = o[0::2]
    if c == 7: h = o[:V0 // 2]; p[h] = np.roll(h, 1)
    return p
def setup_inputs_corners(rng):
    x, y, nx, st = parts(rng)
    for q in range(N):
        for g in range(8):
            o = rng.permutation(8)
            for k in range(8): nx[q, g, k] = corner(rng, o[k])
        nx[q, q % 8] = np.arange(V0); nx[q, (q + 1) % 8] = corner(rng, 5)
    st = np.where(rng.random(st.shape) < 0.4, rng.choice(np.array([0, 1, V0 - 2, V0 - 1]), st.shape), st)
    same = np.take_along_axis(x, st.reshape(N, 8, RO * M, 1), 2)
    x[:, :, V0:] = np.where(rng.random((N, 8, RO * M, 1)) < 0.3, same, x[:, :, V0:])
    y[:, 4] = 1.0; y[:, 5] = 0.0
    return pack(x, y, nx, st)
def setup_inputs_crowd(rng):
    x, y, nx, st = parts(rng)
    for q in range(N):
        for g in range(8):
            kind = (g + q) % 5; base = rng.integers(0, 256, 16); s = rng.integers(0, V0, 4)
            for t in range(RO):
                odd = (-1, int(rng.integers(0, M)), 0, M - 1, -1)[kind]; alike = np.arange(M) != odd; a = V0 + t * M
                x[q, g, a:a + M][alike] = np.clip(base + rng.integers(-2, 3, 16), 0, 255)
                st[q, g, t][alike] = s[0]
                if kind == 4: st[q, g, t] = s[rng.integers(0, 4, M)]
    return pack(x, y, nx, st)
def setup_inputs_ties(rng):
    x, y, nx, st = parts(rng)
    x = 100 + rng.integers(0, 2, (N, 8, V, 16))
    x[:, 1::2] = np.take_along_axis(rng.integers(0, 256, (N, 4, 3, 16)), rng.integers(0, 3, (N, 4, V, 1)), 2)
    one = 255 - (np.arange(16) == rng.integers(0, 16, (N, V, 1))).astype(np.int64)
    x[:, 2] = np.where(rng.random((N, V, 1)) < 0.3, one, 255); x[:, 2, V0:] = 0
    x[:, 6] = rng.integers(0, 2, (N, V, 16)); x[:, 6, V0:] = 255
    c = rng.integers(0, 3, (N, V, 1))
    x[:, 4] = np.where(c == 0, 0, np.where(c == 1, 255, one)); x[:, 4, V0:] = rng.integers(1, 20, (N, RO * M, 16))
    return pack(x, y, nx, st)
def check_ranges(d):
    bad = []
    w = dict((k, np.asarray(d[k]).astype(np.float64)) for k in ("x", "y0", "nx0", "st"))
    for k, lo, hi in (("x", 0, 255), ("y0", 0, 1), ("nx0", 0, V0 - 1), ("st", 0, V0 - 1)):
        if not (np.min(w[k]) >= lo and np.max(w[k]) <= hi): bad.append("range of " + k)
    if np.any(w["x"] != np.floor(w["x"])): bad.append("x is not whole")
    if np.any((w["y0"] > 0) & (w["y0"] < 2.0 ** -8)): bad.append("y0 is too small and not 0")
    if np.any(np.sort(w["nx0"], axis=-1) != np.arange(V0)): bad.append("a row of nx0 is not a permutation")
    return bad
def dist(a, b):
    return np.add.reduce(np.abs(a - b), axis=-1)
def search(x, nx, pv, xv, p):
    m = np.arange(M)
    for h in range(H):
        w = np.concatenate([nx[:, p], pv[:, p]])
        e = dist(x[w], xv); i = np.argmin(e, axis=0)
        p = np.where(e[i, m] < dist(x[p], xv), w[i, m], p)
    return p
def enter(x, nx, pv, v, b):
    n2 = nx.copy(); p2 = pv.copy()
    for k in range(8):
        c = nx[(k + 1) % 8, b]; f = nx[k, c]; a = pv[k, c]
        ahead = dist(x[c], x[f]) - dist(x[v], x[f]); back = dist(x[c], x[a]) - dist(x[v], x[a])
        tail, first = np.unique(np.where(ahead >= back, c, a), return_index=True)
        w = v[first]; head = nx[k, tail]
        n2[k, v] = v; p2[k, v] = v
        n2[k, tail] = w; n2[k, w] = head; p2[k, head] = w; p2[k, w] = tail
    return n2, p2
def reference(x, y0, nx0, st):
    xs = np.ascontiguousarray(x.astype(np.float32).astype(np.int64).reshape(N, 8, 16, V).transpose(0, 1, 3, 2))
    ys = np.zeros((N, 8, V, 16)); ys[:, :, :V0] = y0.astype(np.float64).reshape(N, 8, 16, V0).transpose(0, 1, 3, 2)
    nx = np.tile(np.arange(V), (N, 8, 8, 1)); nx[..., :V0] = nx0.reshape(N, 8, 8, V0); pv = np.argsort(nx, axis=-1)
    sl = np.stack([gentries(a) for a in st]).astype(np.int64).reshape(N, 8, RO, M)
    for t in range(RO):
        v = V0 + t * M + np.arange(M); have = V0 + (t + 1) * M
        b = np.zeros((N, 8, M), np.int64); got = np.zeros((N, 8, M, 16))
        for r in range(N):
            q = (r + 1 + t) % N
            for g in range(8):
                b[r, g] = search(xs[r, g], nx[r, g], pv[r, g], xs[r, g, v], sl[r, g, t])
                got[r, g] = ys[q, g][search(xs[q, g], nx[q, g], pv[q, g], xs[r, g, v], sl[r, g, t])]
        for r in range(N):
            for g in range(8):
                nx[r, g], pv[r, g] = enter(xs[r, g], nx[r, g], pv[r, g], v, b[r, g])
                y = ys[r, g, :have].copy(); y[v] = got[r, g]
                for s in range(S):
                    y = 0.5 * (1.0 + y) - 0.0625 * np.add.reduce(y[nx[r, g, :, :have]] * y[pv[r, g, :, :have]], axis=0)
                ys[r, g, :have] = y
    return {"y": np.ascontiguousarray(ys.transpose(0, 1, 3, 2)).reshape(N, 128, V).astype(np.float32), "nx": nx.reshape(N, 64, V).astype(np.float32)}

def check_inputs(d):
    bad = list(check_ranges(d))
    if not bad:
        for name, y in reference(**d).items():
            for q in range(N):
                v = np.abs(np.asarray(y[q], np.float64)); s = np.sqrt(np.mean(v * v))
                if v.max() > 3 * s or s < 2.0 ** -2: bad.append('%s of rank %d is uneven or too small' % (name, q))
    return bad

@@ -1,0 +1,606 @@
+from concourse.bass import DstId, RemoteDMATransfer
+from concourse.mybir import AluOpType, AxisListType, ActivationFunctionType
+
+AL = AluOpType
+AF = ActivationFunctionType
+V0, M, RO, V = 1664, 128, 3, 2048
+H = "float16"
+F, B, I, U = "float32", "bfloat16", "int32", "uint16"
+RING = 4096
+NF = 64
+PAR = dict(
+    fold=((0, 2, 4, 6),) * 3, foldl=((0, 2), (0, 2, 4, 6)), eq=("VV", "SS", "SS"),
+    cuts=((0, 512, 1024, 1536, 1792), (0, 512, 1024, 1536, 1920), (0, 512, 1024, 1536, 1792, 2048)),
+    lead=(0.0, 0.0, 0.0),
+    nflat=(5, 5, 99),
+    alead=(0.0, 0.0, 0.0),
+    nsv=4,
+    ev=("S", "S", "SV"), evl=30000.0,
+    sg=("V", "V", "V"), eg=("V", "S", "S"), wg=("S", "S", "S"),
+    CY=1.0, GA=1.55, SCA=3.8, PE=0.52, LAT=90.0, DL=1.0)
+PAR.update({'lead': (0.0, 20000.0, 40000.0), 'evl': 5000.0, 'sg': ('V', 'SVVV', 'SVVV'), 'eg': ('V', 'V', 'V'), 'eq': ('VV', 'VV', 'VV'), 'ev': ('S', 'S', 'VS'), 'fold': ((-1, 1, 3, 5), (-1, 1, 3, 5), (-1, 1, 3, 5)), 'foldl': ((0, 2, 4, 6), (-1, 1, 3, 5)), 'cuts': ((0, 512, 1024, 1536, 1792), (0, 512, 1024, 1536, 1792, 1920), (0, 256, 768, 1280, 1792, 2048)), 'wg': ('V', 'S', 'S'), 'nflat': (6, 6, 99), 'alead': (0.0, 0.0, 0.0)})
+SB = {
+    "flat": (16 * V, F), "ring": (RING, F), "ya": (V, F), "yb": (V, F), "xs": (V, B), "nb": (V, F), "nbp": (V, U),
+    "off": (V, U), "iot": (V, I), "val": (1024, F), "rr": (V, B), "mask": (1032, B), "r8": (1024, B),
+    "wt": (V + 128, B), "sc": (2048, B), "gg": (1024, H), "xcq": (1024, B), "ab": (1024, B), "eq": (1024, B),
+    "sti": (24, I), "stf": (24, I), "xf": (384, B), "xvt": (256, B), "ys": (128, F),
+    "pi": (8, I), "col": (28, F), "ib": (128, B), "ibn": (128, B), "iff": (128, F), "ztop": (160, B), "zbot": (160, B),
+    "z0": (160, B), "z64": (160, B), "zn": (160, B), "selc": (256, B), "sq": (512, B), "b48": (48, B), "b48p": (48, B), "b48n": (48, B),
+    "bias": (384, B), "ru": (32, B), "rf": (32, B), "ro": (32, B), "rom": (256, B), "par": (256, B), "h2": (64, B), "zero": (256, B),
+    "ones": (128, B), "dv": (128, H), "jm": (128, F), "bc": (16, U), "pil": (128, U), "thr": (128, F), "cw": (240, B),
+    "t1": (256, F), "t2": (256, F), "t3": (256, F), "p16": (16, U), "ph": (16, F), "c16": (256, U), "pd": (256, H),
+    "mm": (16, F), "stay": (16, F), "oh": (256, B), "oht": (256, B), "sel": (256, H),
+    "nbb": (128, H), "cq": (64, U), "fa": (128, U), "brep": (128, H), "nbrep": (128, H), "oo": (128, H), "rl": (8, U),
+    "ind": (384, B), "dw": (128, B), "fam": (256, H), "ot": (256, H), "o16": (64, U), "b16": (64, U), "wts": (128, B),
+    "wrow": (128, B), "zz": (256, H), "sl": (128, U), "thh": (128, H),
+}
+ALIAS = {"ni": ("iot", 256, 832), "gw": ("xcq", 0, 1024), "sc2": ("wt", 0, 1024)}
+SCRATCH = dict((k, ("sbuf", [128, n], d)) for k, (n, d) in SB.items())
+for _b in range(8):
+    SCRATCH["ps%d" % _b] = ("psum", [128, 512], F)
+SEMAPHORES = ["cV", "cS", "cP", "cG", "sent"] + ["d%d" % i for i in range(48)] + ["f%d" % i for i in range(NF)] + [k + str(t) for k in ("ax", "as", "ay") for t in range(RO)]
+
+MAGIC = 12582912.0
+MAGIC64 = 805306368.0
+
+
+def start_masks(T, topo, rank):
+    me = T.cores[rank]
+    eng = [topo.engines(me, T.cores[(rank + 1 + t) % len(T.cores)]) for t in range(RO)]
+    least = min(len(e) for e in eng)
+    narrow = [t for t in range(RO) if len(eng[t]) == least]
+    share = 1
+    while share * 2 * len(narrow) <= least:
+        share *= 2
+    used, out = [], [None] * RO
+    for t in narrow + [t for t in range(RO) if t not in narrow]:
+        free = [e for e in eng[t] if e not in used]
+        n = share
+        if t not in narrow:
+            while n * 2 <= len(free):
+                n *= 2
+        out[t] = free[:n]
+        used += out[t]
+    return out
+
+
+def build(g, core, T, topo):
+    rank = T.rank_of(core)
+    n = len(T.cores)
+    ops = []
+    nsem = [0]
+    vec, act, pe = g.vector, g.scalar, g.tensor
+    CY, GA, SCA, PE, DL = PAR["CY"], PAR["GA"], PAR["SCA"], PAR["PE"], PAR["DL"]
+
+    def A(name, a=0, b=None, s=1, p=None):
+        if name in ALIAS:
+            name, o, w = ALIAS[name]
+            a, b = a + o, (w if b is None else b) + o
+        t = T[name]
+        b = SB.get(name, (512, F))[0] if b is None else b
+        cs = slice(a, b, s) if s > 1 else slice(a, b)
+        return (t[slice(None) if p is None else p, cs], name, a, b, (b - a + s - 1) // s)
+
+    def IN(win, off):
+        return (win[0].indirect(off[0]), win[1], win[2], win[3], win[4], off)
+
+    def op(eng, fn, dur, rd, wr, kind="c", lat=0.0, sem=None, cnt=0, after=()):
+        r = [x[1:4] for x in rd if isinstance(x, tuple)] + [x[5][1:4] for x in list(rd) + list(wr) if isinstance(x, tuple) and len(x) > 5]
+        ops.append(dict(eng=eng, fn=fn, dur=dur, rd=sorted(set(r)), wr=sorted(set(x[1:4] for x in wr)), kind=kind, lat=lat, sem=sem, cnt=cnt, after=list(after)))
+        return len(ops) - 1
+
+    def two(*xs):
+        return all(SB.get(x[1], (0, F))[1] in (B, H, U) for x in xs)
+
+    def cost(out, a, per):
+        if len(out) > 5:
+            return 50 + 16 * out[5][4] * SCA * CY
+        if len(a) > 5:
+            return 55 + out[4] * GA * CY
+        return 30 + max(64, out[4] * per) * CY
+
+    def ap(x):
+        return x[0] if isinstance(x, tuple) else x
+
+    def cp(out, a):
+        return op("V", lambda: vec.tensor_copy(out[0], a[0]), cost(out, a, .5 if two(out, a) else 1), [a], [out])
+
+    def tt(out, a, b, o, **k):
+        per = 1 if (a[1][:2] == "ps" or b[1][:2] == "ps") else 2
+        return op("V", lambda: vec.tensor_tensor(out[0], a[0], b[0], o), cost(out, a, per), [a, b], [out], **k)
+
+    def ts(out, a, s1, o1, s2=None, o2=None):
+        if o2 is None:
+            fn = lambda: vec.tensor_scalar(out[0], a[0], ap(s1), None, o1)
+        else:
+            fn = lambda: vec.tensor_scalar(out[0], a[0], ap(s1), ap(s2), o1, o2)
+        return op("V", fn, cost(out, a, .5 if two(out, a) else 1), [a, s1, s2], [out])
+
+    def ms(out, c):
+        return op("V", lambda: vec.memset(out[0], c), cost(out, out, .5 if two(out) else 1), [], [out])
+
+    def tr(out, a):
+        return op("V", lambda: vec.transpose(out[0], a[0]), cost(out, a, .5 if two(out) else 1), [a], [out])
+
+    def ac(out, a, f=AF.Identity, extra=0.0, after=(), **k):
+        kw = dict((x, ap(y)) for x, y in k.items())
+        return op("S", lambda: act.activation(out[0], a[0], f, **kw), cost(out, a, 1) + 15 + extra, [a] + list(k.values()), [out], after=after)
+
+    def gat(e, out, a):
+        return cp(out, a) if e == "V" else ac(out, a)
+
+    def mm(calls):
+        def fn():
+            for c in calls:
+                r = pe.matmul(c[0][0], c[1][0], c[2][0], c[3], c[4])
+            return r
+        d = 60 + sum(max(64, c[2][4]) * (4 if SB[c[2][1]][1] == F else 1) * PE for c in calls)
+        return op("P", fn, d, [x for c in calls for x in c[1:3]], [c[0] for c in calls])
+
+    def acc(out, pairs):
+        return [(out, l, r, i == 0, i == len(pairs) - 1) for i, (l, r) in enumerate(pairs)]
+
+    def iota(out, pat, base=0, cm=0):
+        if SB[out[1]][1] == I:
+            fn = lambda: g.iota(out[0], pat, base, cm)
+        else:
+            fn = lambda: g.iota(out[0], pat, base, cm, allow_small_or_imprecise_dtypes=True)
+        return op("G", fn, 150 + 2 * out[4] * CY, [], [out])
+
+    def asel(out, a, pat, base, cm):
+        return op("G", lambda: g.affine_select(out[0], a[0], pat, AL.is_equal, 0.0, base, cm), 190 + 2 * out[4] * CY, [a], [out])
+
+    def dma(eng, pairs, lat, **k):
+        sem = T.sem["d%d" % nsem[0]]
+        nsem[0] += 1
+        q = {"G": g, "Y": g.sync, "S": act}[eng]
+
+        def fn():
+            for o, i in pairs:
+                q.dma_start(ap(o), ap(i), **k).then_inc(sem, 16)
+        return op(eng, fn, (900 if eng == "G" else 70) * len(pairs) * DL, [i for o, i in pairs], [o for o, i in pairs if isinstance(o, tuple)],
+                  kind="d", lat=lat * DL, sem=sem, cnt=16 * len(pairs))
+
+    folds = []
+
+    def fold_dma(out, a):
+        i = len(folds)
+        sem = T.sem["f%d" % (i % NF)]
+        op("G", lambda: g.dma_start(out[0], a[0], accum_op=AL.add).then_inc(sem, 16), 900 * DL, [a, out], [out], kind="d",
+           lat=(1800 + 1.7 * out[4]) * DL, sem=sem, cnt=16 * (i // NF + 1))
+        ops[-1].update(key="f%d" % (i % NF), cons=len(ops), hard=[folds[i - NF] + 1] if i >= NF else [])
+        folds.append(len(ops) - 1)
+
+    sent = [0]
+
+    def arrive(name, cnt, reg, after):
+        return op("R", None, 0.0, [], [reg], kind="r", lat=2000.0 * DL, sem=T.sem[name], cnt=cnt, after=[after])
+
+    def row(s):
+        return slice(s, 128, 16)
+
+    def Z(name, b):
+        return A(name, 16 - b, 144 - b)
+
+    Y0, Y1, Y2, D0, D1, K, TT, X = ["ps%d" % i for i in range(8)]
+    IB = A("ib")
+
+    dma("Y", [(A("ni", 104 * k, 104 * k + 104), T.nx0[k::8, :]) for k in range(4)], 2200)
+    dma("S", [(A("ni", 104 * k, 104 * k + 104), T.nx0[k::8, :]) for k in range(4, 8)], 2200)
+    dma("Y", [(A("xs"), T.x[:])], 3000)
+    dma("Y", [(A("sti"), T.st[:])], 2200)
+    vali = A("ring", 0, V0)
+    iota(vali, [[1, 104], [104, 16]], 64)
+    iota(A("pi", 0, 1), [[0, 1]], 0, 1)
+    iota(A("iot", 0, 256), [[1, 256]])
+    ms(A("rr"), 1.0)
+    ms(A("nb", V0, V), 0.0)
+    cp(A("nbp", 416, 832), A("ni", 416, 832))
+    cp(A("nbp", 0, 416), A("ni", 0, 416))
+    for k in range(8):
+        w = IN(A("flat", (8 + k) * V, (8 + k) * V + V0), A("nbp", 104 * k, 104 * k + 104))
+        if k < PAR["nsv"]:
+            cp(w, vali)
+        else:
+            ac(w, vali, AF.Silu, extra=1500.0 if k == PAR["nsv"] else 0.0)
+        dma("Y", [(A("nb", 0, V0, p=row(8 + k)), A("flat", (8 + k) * V, (8 + k) * V + V0, p=row(8 + k)))], 2300)
+        ops[-1]["wr"] = [("nb%d" % (8 + k), 0, 1)]
+    cp(A("ring", 2048, 2048 + 832), A("ni"))
+    dma("Y", [(A("nb", 0, V0, p=row(k)), A("ring", 2048 + 104 * k, 2152 + 104 * k)) for k in range(8)], 2500)
+    ops[-1]["wr"] = [("nb0", 0, 1)]
+    dma("G", [(A("ya", 0, V0), T.y0[:])], 4000)
+
+    mk = start_masks(T, topo, rank)
+    for name, src, dst, w0, w in (("ax", "xs", "xf", V0, M), ("as", "sti", "stf", 0, 8)):
+        trs = []
+        for t in range(RO):
+            rid, pid, _ = topo.addr(T.cores[(rank + 1 + t) % n])
+            trs.append(RemoteDMATransfer(dst_ids=[DstId(rid=rid, pnc=pid)], dma_engine_mask=sum(1 << e for e in mk[t]), remote_sem=T.sem[name + str(t)],
+                                         src=A(src, w0 + w * t, w0 + w * t + w)[0], dst=A(dst, w * t, w * t + w)[0]))
+        sent[0] += sum(len(m) for m in mk)
+        s = op("G", (lambda trs=trs: g.remote_dma_fused(trs, local_sem=T.sem.sent)), 2500, [A(src, w0, w0 + RO * w)], [], kind="x", lat=3000.0)
+        for t in range(RO):
+            arrive(name + str(t), len(start_masks(T, topo, (rank - 1 - t) % n)[t]), A(dst, w * t, w * t + w), s)
+
+    def C(i):
+        return A("col", i, i + 1)
+    P_, P16, P8, GB, P1, PH, T0, TOP, BOT, FST, GB16, T1, IDX, SV, OFC, P256, WC, TC, SW = [C(i) for i in range(19)]
+    for i, (c, o) in enumerate(((15, AL.bitwise_and), (7, AL.bitwise_and), (112, AL.bitwise_and), (1, AL.bitwise_and), (1, AL.arith_shift_right))):
+        ts(A("pi", i + 1, i + 2), A("pi", 0, 1), c, o)
+    cp(A("col", 0, 6), A("pi", 0, 6))
+    ts(TOP, P16, 8.0, AL.is_lt)
+    ts(BOT, P16, 8.0, AL.is_ge)
+    ts(FST, P16, 0.0, AL.is_equal)
+    ts(GB16, GB, 16.0, AL.add)
+    ts(T1, FST, 8.0, AL.mult, P_, AL.add)
+    ts(T0, T1, -1.0, AL.add)
+    ts(T1, T0, 8.0, AL.add)
+    ts(IDX, P16, 1.0, AL.add)
+    ts(SV, P8, float(V), AL.mult)
+    ts(OFC, BOT, -64.0, AL.mult, -MAGIC, AL.add)
+    ts(P256, P16, 16.0, AL.mult)
+    ts(SW, TOP, 16.0, AL.mult, P_, AL.add)
+    ts(SW, SW, -8.0, AL.add)
+    io = lambda w: A("iot", 0, w)
+    ts(IB, io(128), P_, AL.is_equal)
+    ts(A("ibn"), io(128), P_, AL.is_equal, -1.0, AL.mult)
+    ts(A("iff"), io(128), P_, AL.is_equal)
+    for i, (c, m) in enumerate(((P_, TOP), (SW, TOP), (SW, BOT), (P_, BOT))):
+        ts(A("sq", 128 * i, 128 * i + 128), io(128), c, AL.is_equal, m, AL.mult)
+    for name, c in (("ztop", TOP), ("zbot", BOT), ("z0", FST), ("z64", 64.0), ("zn", -1.0)):
+        ts(A(name), io(160), GB16, AL.is_equal, c, AL.mult)
+    ts(A("selc", 0, 128), io(128), T0, AL.is_equal, TOP, AL.mult)
+    ts(A("selc", 128, 256), io(128), T1, AL.is_equal, TOP, AL.mult)
+    ts(A("h2"), io(64), PH, AL.is_equal)
+    ts(A("jm"), io(128), -128.0, AL.add)
+    cp(A("bc"), io(16))
+    iota(A("t1", 0, 48), [[0, 3], [16, 8], [0, 2]])
+    ts(A("b48"), A("t1", 0, 48), GB, AL.is_equal)
+    cp(A("b48p"), A("b48"))
+    ts(A("b48p", 1, 16, 2), A("b48", 1, 16, 2), -1.0, AL.mult)
+    ts(A("b48p", 32, 48), A("b48", 32, 48), -1.0, AL.mult)
+    ts(A("b48n"), A("b48p"), -1.0, AL.mult)
+    ms(A("ru"), 0.0)
+    ts(A("ru", 1, 16, 2), A("b48", 1, 16, 2), TOP, AL.mult)
+    ts(A("ru", 16, 32, 2), A("b48", 0, 16, 2), BOT, AL.mult)
+    ts(A("rf", 0, 16), A("b48", 0, 16), TOP, AL.mult)
+    ts(A("rf", 16, 32), A("b48", 0, 16), BOT, AL.mult)
+    ts(A("ro", 0, 16), A("b48", 0, 16), BOT, AL.mult)
+    ts(A("ro", 16, 32), A("b48", 0, 16), TOP, AL.mult)
+    iota(A("bias", 0, 128), [[0, 8], [-1, 2], [0, 8]])
+    iota(A("bias", 128, 384), [[-1, 2], [0, 128]])
+    iota(A("par"), [[0, 16], [1, 2], [0, 8]])
+    ts(A("par"), A("par"), P1, AL.is_equal)
+    iota(A("zero"), [[0, 256]])
+    iota(A("ones"), [[0, 128]], 1)
+    iota(A("t2", 0, 128), [[1, 16], [256, 8]])
+    ts(A("pil"), A("t2", 0, 128), P256, AL.add)
+    ms(A("t3", 0, 128), 1.0 / 3.0)
+    iota(A("t3", 128, 256), [[0, 128]])
+    op("V", lambda: vec.tensor_tensor_scan(A("t1", 128, 256)[0], A("t3", 0, 128)[0], A("t3", 128, 256)[0], float(3.0 ** 62), AL.mult, AL.add),
+       200, [A("t3")], [A("t1", 128, 256)])
+    ts(A("thr"), A("t1", 128, 256), 2.2, AL.mult)
+    tt(A("t3", 0, 128), A("t1", 128, 256), A("iff"), AL.mult)
+    op("V", lambda: vec.tensor_reduce(WC[0], A("t3", 0, 128)[0], AxisListType.X, AL.add), 200, [A("t3", 0, 128)], [WC])
+    ts(TC, WC, 2.2, AL.mult)
+    iota(A("cw"), [[0, 240]])
+    ts(A("cw", 112, 128), A("ones", 0, 16), WC, AL.mult)
+    asel(A("r8"), A("rr", 0, 1024), [[-16, 8], [0, 128]], 0, 1)
+    asel(A("rr"), A("rr"), [[-1, 128], [0, 16]], 0, 1)
+    iota(A("iot", 256, V), [[1, V - 256]], 256)
+    iota(A("mask"), [[0, 129], [1, 8]])
+    ts(A("mask"), A("mask"), P8, AL.is_equal)
+    for k in range(8):
+        ts(A("rom", 32 * k, 32 * k + 32), A("ro"), A("mask", k, k + 1), AL.mult)
+    ts(A("nb", 0, V0), A("nb", 0, V0), MAGIC, AL.add, OFC, AL.add)
+    ops[-1]["rd"] += [("nb%d" % s, 0, 1) for s in (0, 8, 9, 10, 11, 12, 13, 14, 15)]
+
+    xw, nbw, iow = A("xs"), A("nb"), A("iot")
+
+    def search(t, lo, w, e, banks, tiles, pieces):
+        d0, d1, kb, xb = banks
+        t1, t2, t3 = [(lambda a, b, s=1, x=x: A(x[0], x[1] + a, x[1] + b, s)) for x in tiles]
+        cs = lambda nm: A(nm, lo, lo + w)
+        ls = lambda nm: A(nm, lo // 16, (lo + w) // 16)
+        q = w // 16
+        for i in range(lo // 128, (lo + w) // 128):
+            xv = A("xf", M * t, M * t + M) if i else A("xs", V0 + M * t, V0 + M * t + M)
+            cp(A("p16", 8 * i, 8 * i + 8), A("stf" if i else "sti", 8 * t, 8 * t + 8))
+            cp(A("ph", 8 * i, 8 * i + 8), A("stf" if i else "sti", 8 * t, 8 * t + 8))
+            mm([(A(xb, 128 * i, 128 * i + 128), xv, IB, True, True)])
+            ac(A("xvt", 128 * i, 128 * i + 128), A(xb, 128 * i, 128 * i + 128), scale=-1.0)
+            tt(A("oh", 128 * i, 128 * i + 128), IN(A("xs", 0, V0), A("p16", 8 * i, 8 * i + 8)), xv, AL.subtract)
+        ac(cs("oh"), cs("oh"), AF.Abs)
+        mm([(A(kb, 0, w), Z("z64", 0), cs("oh"), True, True)])
+        ac(t1(0, w), A(kb, 0, w))
+        tr(t2(0, w), t1(0, w))
+        cp(ls("stay"), t2(0, w, 16))
+        for h in range(2):
+            cp(cs("c16"), IN(nbw, ls("p16")))
+            ac(t3(0, w), IN(nbw, ls("p16")))
+            tt(cs("pd"), IN(iow, ls("p16")), t3(0, w), AL.subtract)
+            for i in range(w // 64):
+                nm, o = pieces[i % len(pieces)]
+                j = lo + 64 * i
+                gat(e[i % len(e)], A(nm, o, o + 1024), IN(xw, A("c16", j, j + 64)))
+                for u, bank in enumerate((d0, d1)):
+                    ro = 16 * (j % 128) + 512 * u
+                    x = A(nm, o + 512 * u, o + 512 * u + 512)
+                    mm(acc(A(bank), [(IB, x), (A("xvt", j - j % 128, j - j % 128 + 128), A("rr", ro, ro + 512))]))
+                    ac(x, A(bank), AF.Abs)
+                mm(acc(A(kb, 64 * i, 64 * i + 64), [(Z("z64", s), A(nm, o + s, o + 1024, 16)) for s in range(16)]))
+            ac(t1(0, w), A(kb, 0, w), bias=IDX)
+            tr(t2(0, w), t1(0, w))
+            tt(t1(0, w // 2), t2(0, w, 2), t2(1, w, 2), AL.min)
+            a = 0
+            for m in (8 * q, 4 * q, 2 * q):
+                tt(t1(a + m, a + m + m // 2), t1(a, a + m, 2), t1(a + 1, a + m, 2), AL.min)
+                a += m
+            tt(ls("mm"), t1(a, a + q), ls("stay"), AL.min)
+            tt(cs("oh"), IN(ls("mm"), A("bc", 0, q)), t2(0, w), AL.is_equal)
+            tr(cs("oht"), cs("oh"))
+            tt(cs("sel"), cs("oht"), cs("pd"), AL.mult)
+            mm(acc(A(xb, 0, q), [(A("iff"), ls("ph"))] + [(Z("zn", r), A("sel", lo + r, lo + w, 16)) for r in range(16)]))
+            cp(ls("p16"), A(xb, 0, q))
+            if h == 0:
+                cp(ls("ph"), A(xb, 0, q))
+                ts(ls("stay"), ls("mm"), MAGIC64, AL.add, -MAGIC64, AL.add)
+
+    posf, posr, nbk = [0], [0], [0]
+    chain = {"V": [], "S": []}
+    for t in range(RO):
+        old, have = V0 + M * t, V0 + M * (t + 1)
+        first = len(ops)
+        iota(A("wt", 1024, V + 128), [[0, V + 128 - 1024]])
+        iota(A("val"), [[1, 128], [0, 8]], old)
+        VC, NVC = C(19 + t), C(22 + t)
+        ts(VC, P_, float(old), AL.add)
+        ts(NVC, VC, -1.0, AL.mult)
+        ts(A("dv"), IB, VC, AL.mult)
+        tl, pc = (("t1", 0), ("t2", 0), ("t3", 0)), (("sc", 0), ("sc", 1024))
+        if t == 0:
+            search(t, 0, 128, "V", (D0, D1, K, X), tl, pc)
+            search(t, 128, 128, "S", (Y0, Y1, Y2, Y2), (("ring", 3072), ("ring", 3328), ("ring", 3584)), (("sc2", 0),))
+        else:
+            search(t, 0, 256, PAR["sg"][t], (D0, D1, K, X), tl, pc)
+        iota(A("wt", 0, 1024), [[0, 1024]])
+        ac(A("ys"), IN(A("ya", 0, old), A("p16", 8, 16)))
+        dst = T.cores[(rank - 1 - t) % n]
+        rid, pid, _ = topo.addr(dst)
+        sent[0] += len(topo.engines(core, dst))
+        s = op("G", (lambda a=A("ya", old, have)[0], rid=rid, pid=pid, m=topo.mask(core, dst), t=t:
+                     g.remote_dma(a, A("ys")[0], T.sem["ay%d" % t], T.sem.sent, pid, rid, m)), 1500, [A("ys")], [], kind="x", sem=T.sem.sent, cnt=sent[0], lat=2500.0)
+        arrive("ay%d" % t, len(topo.engines(T.cores[(rank + 1 + t) % n], core)), A("ya", old, have), s)
+        bl = A("p16", 0, 8)
+        dma("Y", [(A("flat", s * V, s * V + old, p=row(s)), A("nb", 0, old, p=row(s))) for s in range(16)], 2800)
+        cp(A("nbb"), IN(nbw, bl))
+        mm(acc(A(X, 0, 64), [(A("selc", 128 * h, 128 * h + 128), A("nbb", h, 128, 2)) for h in range(2)]))
+        cp(A("cq"), A(X, 0, 64))
+        tt(A("gg"), IN(nbw, A("cq")), A("mask", 0, 1024), AL.mult)
+        ac(A("xcq"), IN(xw, A("cq")))
+        cp(A("brep"), IN(iow, bl))
+        ts(A("nbrep"), A("brep"), -1.0, AL.mult)
+        for u, bank in enumerate((D0, D1)):
+            c = []
+            for q in range(4):
+                rg = A("r8", 128 * (4 * u + q), 128 * (4 * u + q) + 128)
+                c += acc(A(bank, 128 * q, 128 * q + 128), [(rg, A("brep")), (A("nbrep"), rg)])
+            mm(c)
+            if PAR["eq"][t][u] == "V":
+                ts(A("eq", 512 * u, 512 * u + 512), A(bank), 0.0, AL.is_equal)
+            else:
+                ac(A("eq", 512 * u, 512 * u + 512), A(bank), AF.Abs)
+                ac(A("eq", 512 * u, 512 * u + 512), A("eq", 512 * u, 512 * u + 512), AF.Relu, scale=-1.0, bias=1.0)
+        mm(acc(A(X, 0, 64), [(Z("ztop", r), A("gg", r, 1024, 16)) for r in range(16)]) + acc(A(X, 64, 128), [(Z("zbot", r), A("gg", r, 1024, 16)) for r in range(16)]))
+        cp(A("fa"), A(X, 0, 128))
+        EQ = lambda q: A("eq", 128 * q, 128 * q + 128)
+        mm(acc(A(X, 128, 256), [(A("cw", 112 - 16 * q, 240 - 16 * q), EQ(q)) for q in range(8)]))
+        tt(A("t1", 0, 128), A(X, 128, 256), A("thr"), AL.is_ge)
+        tt(A("t1", 128, 256), A("jm"), A("brep"), AL.subtract)
+        tt(A("t2", 0, 128), A("t1", 0, 128), A("t1", 128, 256), AL.mult)
+        tt(A("oo"), A("t2", 0, 128), A("brep"), AL.add)
+        mm(acc(A(X, 256, 264), [(Z("z0", r), A("oo", r, 128, 16)) for r in range(16)]))
+        ts(A("rl"), A(X, 256, 264), 128.0, AL.add)
+        mm([(A(TT, 0, 256), A("nbb"), A("selc"), True, False)] + [(A(TT, k, 256, 8), A("gg", k, 1024, 8), A("ru"), False, k == 7) for k in range(8)]
+           + [(A(TT, 256 + k, 512, 8), A("gg", k, 1024, 8), A("rf"), True, True) for k in range(8)])
+        ac(A("t3"), A(TT, 0, 256), bias=NVC)
+        tt(A("fam"), A(TT, 256, 512), A("par"), AL.mult)
+        mm([(A(K, 0, 384), IB, A("bias"), True, False)])
+        for i, (l, sg) in enumerate(((0, "b48p"), (0, "b48n"), (1, "b48n"), (1, "b48p"))):
+            if i % 2 == 0:
+                gat(PAR["eg"][t], A("sc", 1024 * l, 1024 * l + 1024), IN(xw, A("fa", 64 * l, 64 * l + 64)))
+            ab, o = ("sc", 1024 * l) if i % 2 else ("ab", 0)
+            for u, bank in enumerate((D0, D1)):
+                sub = (A("xvt", 0, 128), A("rr", 1024 * u, 1024 * u + 1024, 2)) if i % 2 else (A("ibn"), A("xcq", 512 * u, 512 * u + 512))
+                mm(acc(A(bank), [(IB, A("sc", 1024 * l + 512 * u, 1024 * l + 512 * u + 512)), sub]))
+                ac(A(ab, o + 512 * u, o + 512 * u + 512), A(bank), AF.Abs)
+            mm([(A(K, k, 384, 8), A(ab, o + k, o + 1024, 8), A(sg), False, i == 3 and k == 7) for k in range(8)])
+        ts(A("ind"), A(K, 0, 384), 0.0, AL.is_ge)
+        ts(A("dw"), A("ind", 0, 128), WC, AL.mult)
+        tt(A("ot"), A("ind", 128, 384), A("fam"), AL.mult)
+        tt(A("t3"), A("ind", 128, 384), A("t3"), AL.mult)
+        mm([(A(X, 128 + 16 * q, 144 + 16 * q), EQ(q), A("dw", 16 * q, 16 * q + 16), True, True) for q in range(8)])
+        ac(A("wts"), A(X, 128, 256))
+        mm(acc(A(D0, 0, 64), [(A("ot", 128 * u, 128 * u + 128), A("h2")) for u in range(2)]))
+        cp(A("o16"), A(D0, 0, 64))
+        mm([(A(D1, 0, 128), A("wts"), IB, True, True)])
+        ac(A("wrow"), A(D1, 0, 128))
+        mm([(A(TT, 0, 256), IB, A("zero"), True, False)]
+           + [(A(TT, 128 * z + 16 * q + 8 * d, 128 * z + 16 * q + 8 * d + 8), EQ(q), A("dw", 16 * q + 8 * z, 16 * q + 8 * z + 8), False, False)
+              for z in range(2) for q in range(8) for d in range(2)])
+        tt(A("gg"), IN(nbw, A("o16")), A("mask", 1, 1025), AL.mult)
+        mm(acc(A(X, 0, 64), [(Z("zbot", r), A("gg", r, 1024, 16)) for r in range(16)]))
+        cp(A("b16"), A(X, 0, 64))
+        cp(IN(A("wt"), A("rl")), A("wrow"))
+        gat(PAR["wg"][t], A("gw"), IN(A("wt", 128, V + 128), A("b16")))
+        mm([(A(TT, k, 256, 8), A("gw", k, 1024, 8), A("rom", 32 * k, 32 * k + 32), False, k == 7) for k in range(8)])
+        ts(A("t1"), A(TT, 0, 256), TC, AL.is_lt)
+        tt(A("zz"), A("t1"), A("t3"), AL.mult)
+        mm(acc(A(X, 0, 128), [(A("ones"), A("dv")), (A("zz", 0, 128), IB), (A("zz", 128, 256), IB)]))
+        cp(A("thh"), A(X, 0, 128))
+        SQ = lambda i: A("sq", 128 * i, 128 * i + 128)
+        mm([c for z in range(2) for c in acc(A(D0, 64 * z, 64 * z + 64), [(SQ(2 * z + h), A("thh", h, 128, 2)) for h in range(2)])])
+        ts(A("sl"), A(D0, 0, 128), SV, AL.add)
+        cp(IN(A("flat", 0, 8 * V), A("sl", 0, 64)), A("val"))
+        ac(IN(A("flat", 8 * V, 16 * V), A("sl", 64, 128)), A("val"), AF.Silu)
+        dma("Y", [(A("nb", 0, old, p=row(s)), A("flat", s * V, s * V + old, p=row(s))) for s in range(16)], 2800)
+        mm(acc(A(D1, 0, 128), [(SQ(1), A("thh")), (SQ(2), A("thh"))]))
+        ac(A("nb", old, have), A(D1, 0, 128))
+        if t + 1 == RO:
+            dma("Y", [(T.nx[k::8, :], A("nb", p=row(k))) for k in range(8)], 3000)
+        cp(A("nbp"), IN(nbw, A("pil")))
+        for z in (1, 0):
+            dma("Y", [(A("off", 128 * s, 128 * s + 128), A("nbp", p=row(s))) for s in range(8 * z, 8 * z + 8)], 2500)
+        for o in ops[first:]:
+            o["lead"] = PAR["lead"][t]
+        nch = [0]
+        for sw in range(2):
+            nev = [0]
+            src, dst = ("ya", "yb") if sw == 0 else ("yb", "ya")
+            yw = A(src, 0, have)
+            cuts = PAR["cuts"][t]
+            for ci, (a, b) in enumerate(zip(cuts, cuts[1:])):
+                w = b - a
+                rn, rw, pos = ("flat", 16 * V, posf) if nch[0] < PAR["nflat"][t] else ("ring", RING, posr)
+                nch[0] += 1
+                parts = []
+                for i in range((w + 511) // 512):
+                    parts.append(((Y0, Y1, Y2)[nbk[0] % 3], 512 * i, min(w, 512 * i + 512)))
+                    nbk[0] += 1
+                fold = PAR["fold"][t] if ci < len(cuts) - 3 else PAR["foldl"][len(cuts) - 2 - ci]
+                terms = [(src, a)]
+                place = []
+                for k in range(8):
+                    if pos[0] + w > rw:
+                        pos[0] = 0
+                    o = pos[0]
+                    pos[0] += w
+                    place.append(o)
+                    pk = A(rn, o, o + w)
+                    chain["S"] = [ac(pk, IN(yw, A("off", 128 * (8 + k) + a // 16, 128 * (8 + k) + b // 16)), after=chain["S"], scale=-0.125)]
+                    chain["V"] = [tt(pk, IN(yw, A("off", 128 * k + a // 16, 128 * k + b // 16)), pk, AL.mult, after=chain["V"])]
+                    ops[chain["S"][0]]["lead"] = PAR["alead"][t]
+                    if k == 0 and -1 in fold:
+                        fold_dma(pk, A(src, a, b))
+                        terms = [(rn, o)]
+                    elif k - 1 in fold:
+                        fold_dma(A(rn, place[k - 1], place[k - 1] + w), pk)
+                        terms.append((rn, place[k - 1]))
+                    elif k not in fold:
+                        terms.append((rn, o))
+                    for i, (nm, c0) in enumerate(terms):
+                        mm([(A(bk, 0, q - p), A("iff"), A(nm, c0 + p, c0 + q), k == 0 and i == 0, k == 7 and i == len(terms) - 1) for bk, p, q in parts])
+                    terms = []
+                for bk, p, q in parts:
+                    if PAR["ev"][t][nev[0] % len(PAR["ev"][t])] == "S":
+                        ac(A(dst, a + p, a + q), A(bk, 0, q - p), bias=0.5, scale=0.5)
+                    else:
+                        ts(A(dst, a + p, a + q), A(bk, 0, q - p), 0.5, AL.mult, 0.5, AL.add)
+                    ops[-1]["lead"] = PAR["evl"]
+                    nev[0] += 1
+                if t == RO - 1 and sw == 1:
+                    dma("Y", [(T.y[:, a:b], A(dst, a, b))], 3000)
+    return ops, sent[0]
+
+
+def schedule(ops):
+    LAT = PAR["LAT"]
+    hist = {}
+    for i, o in enumerate(ops):
+        deps = set(o["after"])
+        soft = set(o["after"])
+        for regs, w in ((o["rd"], False), (o["wr"], True)):
+            for nm, a, b in regs:
+                for j, a2, b2, w2 in hist.get(nm, ()):
+                    if j != i and ((nm[:2] == "ps" and (ops[j]["eng"] != o["eng"] or o["eng"] == "P")) or ((w or w2) and a < b2 and a2 < b)):
+                        deps.add(j)
+                        soft.discard(j)
+        for regs, w in ((o["rd"], False), (o["wr"], True)):
+            for nm, a, b in regs:
+                h = hist.setdefault(nm, [])
+                if w and nm[:2] != "ps":
+                    h[:] = [e for e in h if not (a <= e[1] and e[2] <= b)]
+                if nm[:2] == "ps":
+                    h[:] = [e for e in h if e[0] != i][-12:]
+                h.append((i, a, b, w))
+        deps = set(j if ops[j].get("cons", i) == i else ops[j]["cons"] for j in deps) | set(o.get("hard", ()))
+        o["deps"], o["soft"] = sorted(deps), soft
+    for i in range(len(ops) - 1, -1, -1):
+        o = ops[i]
+        o["bl"] = o.get("bl", 0.0) + o["dur"] + o["lat"]
+        for j in o["deps"]:
+            ops[j]["bl"] = max(ops[j].get("bl", 0.0), o["bl"] + LAT)
+    succ = [[] for _ in ops]
+    left = [len(o["deps"]) for o in ops]
+    for i, o in enumerate(ops):
+        o["rdy"] = 0.0
+        for j in o["deps"]:
+            succ[j].append(i)
+    free = dict((e, 0.0) for e in "VSPGYR")
+    order = dict((e, []) for e in "VSPGYR")
+    ready = dict((e, []) for e in "VSPGYR")
+    for i, o in enumerate(ops):
+        if not left[i]:
+            ready[o["eng"]].append(i)
+    for _ in ops:
+        e = min((e for e in ready if ready[e]), key=lambda e: max(free[e], min(ops[i]["rdy"] for i in ready[e])))
+        now = max(free[e], min(ops[i]["rdy"] for i in ready[e]))
+        i = max((i for i in ready[e] if ops[i]["rdy"] <= now), key=lambda i: (ops[i]["bl"] + ops[i].get("lead", 0.0), -i))
+        ready[e].remove(i)
+        o = ops[i]
+        o["t0"] = now
+        free[e] = now + o["dur"]
+        o["end"] = free[e] + o["lat"]
+        order[e].append(i)
+        for j in succ[i]:
+            gap = 0.0 if ops[j]["eng"] == e and (e == "P" or i in ops[j]["soft"]) else LAT
+            ops[j]["rdy"] = max(ops[j]["rdy"], o["end"] + gap)
+            left[j] -= 1
+            if not left[j]:
+                ready[ops[j]["eng"]].append(j)
+    return order
+
+
+def rank_program(g, core, T, topo):
+    if T.rank_of(core) is None:
+        return
+    ops, sent = build(g, core, T, topo)
+    order = schedule(ops)
+    total = {}
+    for e in "VSPG":
+        c = 0
+        for i in order[e]:
+            if ops[i]["kind"] == "c":
+                c += 1
+                ops[i]["sem"], ops[i]["cnt"], ops[i]["key"] = T.sem["c" + e], c, e
+        total[e] = c
+    for i, o in enumerate(ops):
+        if o["kind"] != "c":
+            o["key"] = "sent" if o["kind"] == "x" else o.get("key", i)
+    seen = {}
+    for e, q in (("V", g.vector), ("S", g.scalar), ("P", g.tensor), ("Y", g.sync), ("G", g)):
+        seen = {}
+        for i in order[e]:
+            o = ops[i]
+            need = {}
+            for j in o["deps"]:
+                d = ops[j]
+                if j in o["soft"] or (e == "P" and d["eng"] == "P"):
+                    continue
+                if d["cnt"] > max(seen.get(d["key"], 0), need.get(d["key"], (0, None))[0]):
+                    need[d["key"]] = (d["cnt"], d["sem"])
+            for k, (c, s) in need.items():
+                q.wait_ge(s, c)
+                seen[k] = c
+            r = o["fn"]()
+            if o["kind"] == "c":
+                r.then_inc(o["sem"], 1)
+    for e in "VSPG":
+        if total[e] > seen.get(e, 0):
+            g.wait_ge(T.sem["c" + e], total[e])
+    for o in ops[::-1]:
+        if o["kind"] in "dr" and o["cnt"] > seen.get(o["key"], 0):
+            g.wait_ge(o["sem"], o["cnt"])
+            seen[o["key"]] = o["cnt"]
+    if sent > seen.get("sent", 0):
+        g.wait_ge(T.sem.sent, sent)

@@ -6,42 +6,47 @@ AF = ActivationFunctionType
 V0, M, RO, V = 1664, 128, 3, 2048
 H = "float16"
 F, B, I, U = "float32", "bfloat16", "int32", "uint16"
-RING = 4096
+OFF = 64.0
+RING = 3824
+WT = 2368
 NF = 64
 PAR = dict(
-    fold=((0, 2, 4, 6),) * 3, foldl=((0, 2), (0, 2, 4, 6)), eq=("VV", "SS", "SS"),
-    cuts=((0, 512, 1024, 1536, 1792), (0, 512, 1024, 1536, 1920), (0, 512, 1024, 1536, 1792, 2048)),
-    lead=(0.0, 0.0, 0.0),
-    nflat=(5, 5, 99),
-    alead=(0.0, 0.0, 0.0),
-    nsv=4,
-    ev=("S", "S", "SV"), evl=30000.0,
-    sg=("V", "V", "V"), eg=("V", "S", "S"), wg=("S", "S", "S"),
-    CY=1.0, GA=1.55, SCA=3.8, PE=0.52, LAT=90.0, DL=1.0)
-PAR.update({'lead': (0.0, 20000.0, 40000.0), 'evl': 5000.0, 'sg': ('V', 'SVVV', 'SVVV'), 'eg': ('V', 'V', 'V'), 'eq': ('VV', 'VV', 'VV'), 'ev': ('S', 'S', 'VS'), 'fold': ((-1, 1, 3, 5), (-1, 1, 3, 5), (-1, 1, 3, 5)), 'foldl': ((0, 2, 4, 6), (-1, 1, 3, 5)), 'cuts': ((0, 512, 1024, 1536, 1792), (0, 512, 1024, 1536, 1792, 1920), (0, 256, 768, 1280, 1792, 2048)), 'wg': ('V', 'S', 'S'), 'nflat': (6, 6, 99), 'alead': (0.0, 0.0, 0.0)})
+    cuts=((0, 512, 1024, 1536, 1792), (0, 512, 1024, 1536, 1792, 1920), (0, 512, 1024, 1536, 1792, 2048)),
+    dq=("YS", "YY", "YY"),
+    cutv=52,
+    fold=((-1, 1, 3, 5),) * 3,
+    foldl=(((), (-1, 1, 3)),) * 3,
+    nflat=(6, 6, 99),
+    lead=(0.0, 20000.0, 40000.0),
+    flead=(0.0, 0.0, 0.0),
+    ev=("S", "S", "VS"), evl=5000.0,
+    own=("VS", "VS", "VS"), far=("SV", "VV", "VV"),
+    gf=("S", "S", "S"),
+    look=150.0,
+    CY=0.9, GA=1.55, SCA=3.8, PE=0.5, LAT=90.0, DL=1.0)
+PAR.update({'cuts': ((0, 512, 1024, 1536, 1792), (0, 512, 1024, 1536, 1920), (0, 512, 1024, 1536, 1920, 2048)), 'dq': ('YY', 'YY', 'YY'), 'cutv': 88, 'fold': ((0, 2, 4), (1, 3, 5), (1, 3, 5)), 'foldl': (((), (-1, 1, 3)), ((-1, 1), (0, 2, 4)), ((0, 2, 4, 6),)), 'nflat': (6, 6, 99), 'lead': (-20000.0, 20000.0, 10000.0), 'flead': (-20000.0, 5000.0, 0.0), 'ev': ('S', 'SSV', 'SSV'), 'evl': 0.0, 'own': ('VS', 'VS', 'VS'), 'far': ('SV', 'VV', 'VV'), 'gf': ('S', 'V', 'S'), 'look': 200.0, 'CY': 0.9, 'GA': 1.3, 'SCA': 3.8, 'PE': 0.5, 'LAT': 90.0, 'DL': 1.0})
 SB = {
     "flat": (16 * V, F), "ring": (RING, F), "ya": (V, F), "yb": (V, F), "xs": (V, B), "nb": (V, F), "nbp": (V, U),
-    "off": (V, U), "iot": (V, I), "val": (1024, F), "rr": (V, B), "mask": (1032, B), "r8": (1024, B),
-    "wt": (V + 128, B), "sc": (2048, B), "gg": (1024, H), "xcq": (1024, B), "ab": (1024, B), "eq": (1024, B),
-    "sti": (24, I), "stf": (24, I), "xf": (384, B), "xvt": (256, B), "ys": (128, F),
-    "pi": (8, I), "col": (28, F), "ib": (128, B), "ibn": (128, B), "iff": (128, F), "ztop": (160, B), "zbot": (160, B),
-    "z0": (160, B), "z64": (160, B), "zn": (160, B), "selc": (256, B), "sq": (512, B), "b48": (48, B), "b48p": (48, B), "b48n": (48, B),
-    "bias": (384, B), "ru": (32, B), "rf": (32, B), "ro": (32, B), "rom": (256, B), "par": (256, B), "h2": (64, B), "zero": (256, B),
-    "ones": (128, B), "dv": (128, H), "jm": (128, F), "bc": (16, U), "pil": (128, U), "thr": (128, F), "cw": (240, B),
-    "t1": (256, F), "t2": (256, F), "t3": (256, F), "p16": (16, U), "ph": (16, F), "c16": (256, U), "pd": (256, H),
-    "mm": (16, F), "stay": (16, F), "oh": (256, B), "oht": (256, B), "sel": (256, H),
-    "nbb": (128, H), "cq": (64, U), "fa": (128, U), "brep": (128, H), "nbrep": (128, H), "oo": (128, H), "rl": (8, U),
-    "ind": (384, B), "dw": (128, B), "fam": (256, H), "ot": (256, H), "o16": (64, U), "b16": (64, U), "wts": (128, B),
-    "wrow": (128, B), "zz": (256, H), "sl": (128, U), "thh": (128, H),
+    "off": (V, U), "val": (1024, F), "ni": (832, I), "wt": (WT, B), "sc": (4096, B), "rep": (4096, B), "ab": (1024, B),
+    "gg": (1024, H), "xcq": (1024, B), "eq": (1024, B), "r8": (1024, B), "mask": (1032, B),
+    "xf": (384, B), "stall": (48, I), "p0": (48, U), "pr": (96, U), "ys": (128, F),
+    "pi": (8, I), "col": (28, F), "ib": (128, B), "ibn": (128, B), "i3": (128, B), "iff": (128, F), "zbot": (160, B),
+    "selc": (256, B), "sq": (512, B), "b48": (48, B), "bp": (48, B), "bn": (48, B), "bp2": (48, B), "bn2": (48, B),
+    "bias": (384, B), "ru": (32, B), "rf": (32, B), "rfd": (16, B), "ro": (32, B), "rom": (256, B), "par": (256, B), "h2": (64, B),
+    "zero": (128, B), "ones": (128, B), "nones": (256, B), "dv": (128, H), "bc": (16, U), "pil": (112, U), "cw": (16, B),
+    "b8": (8, B), "b64": (8, B), "kb": (288, B), "rst": (144, B), "dm": (144, F), "mt": (128, B), "negm": (128, B),
+    "d0": (256, B), "c16": (256, U), "cf": (256, F), "s1": (288, F), "nf": (288, B), "ee": (288, F), "xx": (256, H),
+    "nbb": (128, H), "cq": (64, U), "fa": (128, U), "brep": (128, H), "nbrep": (128, H), "rl": (8, U),
+    "dw": (256, B), "indp": (128, B), "fam": (256, H), "ot": (128, H), "o16": (64, U), "b16": (64, U), "wts": (128, B),
+    "wrow": (128, B), "sl": (128, U), "thh": (128, H),
 }
-ALIAS = {"ni": ("iot", 256, 832), "gw": ("xcq", 0, 1024), "sc2": ("wt", 0, 1024)}
+ALIAS = {"gw": ("xcq", 0, 1024), "iot": ("yb", 0, 256), "t1": ("yb", 256, 256), "t2": ("yb", 512, 256), "t3": ("yb", 768, 256),
+         "yy": ("xx", 0, 256), "nfx": ("thh", 0, 128), "rlx": ("ot", 0, 128), "mw": ("dw", 0, 256), "zz": ("fam", 0, 256)}
 SCRATCH = dict((k, ("sbuf", [128, n], d)) for k, (n, d) in SB.items())
+SCRATCH["wz"] = ("dram", [128, WT], B)
 for _b in range(8):
     SCRATCH["ps%d" % _b] = ("psum", [128, 512], F)
-SEMAPHORES = ["cV", "cS", "cP", "cG", "sent"] + ["d%d" % i for i in range(48)] + ["f%d" % i for i in range(NF)] + [k + str(t) for k in ("ax", "as", "ay") for t in range(RO)]
-
-MAGIC = 12582912.0
-MAGIC64 = 805306368.0
+SEMAPHORES = ["cV", "cS", "cP", "cG", "sent"] + ["d%d" % i for i in range(70)] + ["f%d" % i for i in range(NF)] + [k + str(t) for k in ("ax", "as", "ay") for t in range(RO)]
 
 
 def start_masks(T, topo, rank):
@@ -77,7 +82,7 @@ def build(g, core, T, topo):
             name, o, w = ALIAS[name]
             a, b = a + o, (w if b is None else b) + o
         t = T[name]
-        b = SB.get(name, (512, F))[0] if b is None else b
+        b = SCRATCH[name][1][1] if b is None else b
         cs = slice(a, b, s) if s > 1 else slice(a, b)
         return (t[slice(None) if p is None else p, cs], name, a, b, (b - a + s - 1) // s)
 
@@ -90,14 +95,14 @@ def build(g, core, T, topo):
         return len(ops) - 1
 
     def two(*xs):
-        return all(SB.get(x[1], (0, F))[1] in (B, H, U) for x in xs)
+        return all(SCRATCH[x[1]][2] in (B, H, U) for x in xs)
 
     def cost(out, a, per):
         if len(out) > 5:
             return 50 + 16 * out[5][4] * SCA * CY
         if len(a) > 5:
             return 55 + out[4] * GA * CY
-        return 30 + max(64, out[4] * per) * CY
+        return 45 + max(64, out[4] * per) * CY
 
     def ap(x):
         return x[0] if isinstance(x, tuple) else x
@@ -116,18 +121,12 @@ def build(g, core, T, topo):
             fn = lambda: vec.tensor_scalar(out[0], a[0], ap(s1), ap(s2), o1, o2)
         return op("V", fn, cost(out, a, .5 if two(out, a) else 1), [a, s1, s2], [out])
 
-    def ms(out, c):
-        return op("V", lambda: vec.memset(out[0], c), cost(out, out, .5 if two(out) else 1), [], [out])
-
-    def tr(out, a):
-        return op("V", lambda: vec.transpose(out[0], a[0]), cost(out, a, .5 if two(out) else 1), [a], [out])
+    def scan(out, a, b, first, o0, o1):
+        return op("V", lambda: vec.tensor_tensor_scan(out[0], a[0], b[0], first, o0, o1), cost(out, a, 1), [a, b], [out])
 
     def ac(out, a, f=AF.Identity, extra=0.0, after=(), **k):
         kw = dict((x, ap(y)) for x, y in k.items())
         return op("S", lambda: act.activation(out[0], a[0], f, **kw), cost(out, a, 1) + 15 + extra, [a] + list(k.values()), [out], after=after)
-
-    def gat(e, out, a):
-        return cp(out, a) if e == "V" else ac(out, a)
 
     def mm(calls):
         def fn():
@@ -140,6 +139,9 @@ def build(g, core, T, topo):
     def acc(out, pairs):
         return [(out, l, r, i == 0, i == len(pairs) - 1) for i, (l, r) in enumerate(pairs)]
 
+    def grp(calls, start=True, stop=True):
+        return mm([c + (start and i == 0, stop and i == len(calls) - 1) for i, c in enumerate(calls)])
+
     def iota(out, pat, base=0, cm=0):
         if SB[out[1]][1] == I:
             fn = lambda: g.iota(out[0], pat, base, cm)
@@ -147,8 +149,10 @@ def build(g, core, T, topo):
             fn = lambda: g.iota(out[0], pat, base, cm, allow_small_or_imprecise_dtypes=True)
         return op("G", fn, 150 + 2 * out[4] * CY, [], [out])
 
-    def asel(out, a, pat, base, cm):
-        return op("G", lambda: g.affine_select(out[0], a[0], pat, AL.is_equal, 0.0, base, cm), 190 + 2 * out[4] * CY, [a], [out])
+    def gcopy(out, a):
+        i = op("G", lambda: g.affine_select(out[0], a[0], [[0, a[4]]], AL.is_equal, 0.0, 0, 0), 190 + 2 * out[4] * CY, [a], [out])
+        ops[i]["comm"] = True
+        return i
 
     def dma(eng, pairs, lat, **k):
         sem = T.sem["d%d" % nsem[0]]
@@ -179,52 +183,55 @@ def build(g, core, T, topo):
     def row(s):
         return slice(s, 128, 16)
 
-    def Z(name, b):
-        return A(name, 16 - b, 144 - b)
-
-    Y0, Y1, Y2, D0, D1, K, TT, X = ["ps%d" % i for i in range(8)]
+    Y0, Y1, Y2, D0, D1, KO, KF, TT = ["ps%d" % i for i in range(8)]
     IB = A("ib")
+    XV = lambda t, sd: A("xf", M * t, M * t + M) if sd else A("xs", V0 + M * t, V0 + M * t + M)
+    ST = lambda nm, t, sd: A(nm, 16 * t + 8 * sd, 16 * t + 8 * sd + 8)
 
-    dma("Y", [(A("ni", 104 * k, 104 * k + 104), T.nx0[k::8, :]) for k in range(4)], 2200)
-    dma("S", [(A("ni", 104 * k, 104 * k + 104), T.nx0[k::8, :]) for k in range(4, 8)], 2200)
+    ops[dma("Y", [(A("ni", 0, 104), T.nx0[0::8, :])], 2200)]["lead"] = 50000.0
+    dma("S", [(A("ni", 416, 520), T.nx0[4::8, :])], 2200)
+    dma("Y", [(A("ni", 104 * k, 104 * k + 104), T.nx0[k::8, :]) for k in (5, 1, 2, 3, 6, 7)], 3600)
+    dma("Y", [(ST("stall", t, 0), T.st[:, 8 * t:8 * t + 8]) for t in range(RO)], 2300)
     dma("Y", [(A("xs"), T.x[:])], 3000)
-    dma("Y", [(A("sti"), T.st[:])], 2200)
-    vali = A("ring", 0, V0)
-    iota(vali, [[1, 104], [104, 16]], 64)
-    iota(A("pi", 0, 1), [[0, 1]], 0, 1)
-    iota(A("iot", 0, 256), [[1, 256]])
-    ms(A("rr"), 1.0)
-    ms(A("nb", V0, V), 0.0)
-    cp(A("nbp", 416, 832), A("ni", 416, 832))
-    cp(A("nbp", 0, 416), A("ni", 0, 416))
+    for h in range(2):
+        iota(A("ring", 832 * h, 832 * h + 832), [[1, 52], [104, 16]], int(OFF) + 52 * h)
+    ops[iota(A("pi", 0, 1), [[0, 1]], 0, 1)]["lead"] = 50000.0
+    ops[iota(A("iot"), [[1, 256]])]["lead"] = 50000.0
+    for a, b in ((4, 5), (0, 1), (1, 4), (5, 8)):
+        cp(A("nbp", 104 * a, 104 * b), A("ni", 104 * a, 104 * b))
+    cv = PAR["cutv"]
     for k in range(8):
-        w = IN(A("flat", (8 + k) * V, (8 + k) * V + V0), A("nbp", 104 * k, 104 * k + 104))
-        if k < PAR["nsv"]:
-            cp(w, vali)
-        else:
-            ac(w, vali, AF.Silu, extra=1500.0 if k == PAR["nsv"] else 0.0)
+        for a, b in (((0, 52), (52, 104)) if k % 4 == 0 else ((0, cv), (cv, 104)) if k == 3 and cv < 104 else ((0, 104),)):
+            w = IN(A("flat", (8 + k) * V, (8 + k) * V + V0), A("nbp", 104 * k + a, 104 * k + b))
+            if k < 3 or (k, a) == (3, 0):
+                cp(w, A("ring", 16 * a, 16 * b))
+            else:
+                ac(w, A("ring", 16 * a, 16 * b), AF.Silu, extra=1400.0 if (k, a) == (4, 0) else 0.0)
         dma("Y", [(A("nb", 0, V0, p=row(8 + k)), A("flat", (8 + k) * V, (8 + k) * V + V0, p=row(8 + k)))], 2300)
         ops[-1]["wr"] = [("nb%d" % (8 + k), 0, 1)]
-    cp(A("ring", 2048, 2048 + 832), A("ni"))
+    ts(A("ring", 2048, 2048 + 832), A("ni"), OFF, AL.add)
+    ops[-1]["lead"] = 30000.0
     dma("Y", [(A("nb", 0, V0, p=row(k)), A("ring", 2048 + 104 * k, 2152 + 104 * k)) for k in range(8)], 2500)
     ops[-1]["wr"] = [("nb0", 0, 1)]
-    dma("G", [(A("ya", 0, V0), T.y0[:])], 4000)
+    dma("Y", [(A("flat", k * V, k * V + V0, p=row(k)), A("ring", 2048 + 104 * k, 2152 + 104 * k)) for k in range(8)], 2500)
+    NBS = [("nb%d" % s, 0, 1) for s in (0, 8, 9, 10, 11, 12, 13, 14, 15)]
 
     mk = start_masks(T, topo, rank)
-    for name, src, dst, w0, w in (("ax", "xs", "xf", V0, M), ("as", "sti", "stf", 0, 8)):
+    for name, part in (("ax", XV), ("as", lambda t, sd: ST("stall", t, sd))):
         trs = []
         for t in range(RO):
             rid, pid, _ = topo.addr(T.cores[(rank + 1 + t) % n])
             trs.append(RemoteDMATransfer(dst_ids=[DstId(rid=rid, pnc=pid)], dma_engine_mask=sum(1 << e for e in mk[t]), remote_sem=T.sem[name + str(t)],
-                                         src=A(src, w0 + w * t, w0 + w * t + w)[0], dst=A(dst, w * t, w * t + w)[0]))
+                                         src=part(t, 0)[0], dst=part(t, 1)[0]))
         sent[0] += sum(len(m) for m in mk)
-        s = op("G", (lambda trs=trs: g.remote_dma_fused(trs, local_sem=T.sem.sent)), 2500, [A(src, w0, w0 + RO * w)], [], kind="x", lat=3000.0)
+        s = op("G", (lambda trs=trs: g.remote_dma_fused(trs, local_sem=T.sem.sent)), 2500, [part(t, 0) for t in range(RO)], [], kind="x", lat=3000.0)
         for t in range(RO):
-            arrive(name + str(t), len(start_masks(T, topo, (rank - 1 - t) % n)[t]), A(dst, w * t, w * t + w), s)
+            arrive(name + str(t), len(start_masks(T, topo, (rank - 1 - t) % n)[t]), part(t, 1), s)
+    dma("G", [(A("ya", 0, V0), T.y0[:])], 4000)
 
     def C(i):
         return A("col", i, i + 1)
-    P_, P16, P8, GB, P1, PH, T0, TOP, BOT, FST, GB16, T1, IDX, SV, OFC, P256, WC, TC, SW = [C(i) for i in range(19)]
+    P_, P16, P8, GB, P1, PH, T0, TOP, BOT, FST, GB16, T1, SV, P256, WC, TC, SW, JC, G18, SG = [C(i) for i in range(20)]
     for i, (c, o) in enumerate(((15, AL.bitwise_and), (7, AL.bitwise_and), (112, AL.bitwise_and), (1, AL.bitwise_and), (1, AL.arith_shift_right))):
         ts(A("pi", i + 1, i + 2), A("pi", 0, 1), c, o)
     cp(A("col", 0, 6), A("pi", 0, 6))
@@ -235,150 +242,164 @@ def build(g, core, T, topo):
     ts(T1, FST, 8.0, AL.mult, P_, AL.add)
     ts(T0, T1, -1.0, AL.add)
     ts(T1, T0, 8.0, AL.add)
-    ts(IDX, P16, 1.0, AL.add)
     ts(SV, P8, float(V), AL.mult)
-    ts(OFC, BOT, -64.0, AL.mult, -MAGIC, AL.add)
     ts(P256, P16, 16.0, AL.mult)
     ts(SW, TOP, 16.0, AL.mult, P_, AL.add)
     ts(SW, SW, -8.0, AL.add)
-    io = lambda w: A("iot", 0, w)
+    ts(JC, P_, 2.0, AL.mult, V + OFF, AL.add)
+    ts(G18, GB, 0.125, AL.mult, P_, AL.add)
+    ts(SG, TOP, 2.0, AL.mult, -1.0, AL.add)
+    io = lambda w, a=0: A("iot", a, a + w)
     ts(IB, io(128), P_, AL.is_equal)
-    ts(A("ibn"), io(128), P_, AL.is_equal, -1.0, AL.mult)
+    ts(A("ibn"), IB, -1.0, AL.mult)
+    ts(A("i3"), IB, 3.0, AL.mult)
     ts(A("iff"), io(128), P_, AL.is_equal)
+    iota(A("t1", 0, 8), [[16, 8]])
+    ts(A("b8"), A("t1", 0, 8), GB, AL.is_equal)
+    ts(A("b64"), A("b8"), 64.0, AL.mult)
+    iota(A("t1", 128, 256), [[0, 8], [1, 16]])
+    ts(A("mt"), A("t1", 128, 256), P16, AL.is_equal)
+    ts(A("negm"), A("mt"), -1.0, AL.add, 5e29, AL.mult)
+    cp(A("bc", 0, 8), io(8))
+    ts(A("bc", 8, 16), io(8), 18.0, AL.mult, 17.0, AL.add)
+    for h in range(2):
+        iota(A("kb", 144 * h, 144 * h + 144), [[0, 8], [1, 18]])
+        iota(A("kb", 144 * h + 17, 144 * h + 144, 18), [[0, 8]], 1 << 20)
+    iota(A("kb", 144, 288, 18), [[0, 8]], -17)
+    iota(A("rst"), [[0, 144]])
+    iota(A("rst", 0, 144, 18), [[0, 8]], 1 << 23)
+    ts(A("t2", 0, 144), io(144), -2.0, AL.add, G18, AL.is_equal)
+    ts(A("dm"), io(144), -1.0, AL.add, G18, AL.is_equal)
+    tt(A("dm"), A("t2", 0, 144), A("dm"), AL.subtract)
     for i, (c, m) in enumerate(((P_, TOP), (SW, TOP), (SW, BOT), (P_, BOT))):
         ts(A("sq", 128 * i, 128 * i + 128), io(128), c, AL.is_equal, m, AL.mult)
-    for name, c in (("ztop", TOP), ("zbot", BOT), ("z0", FST), ("z64", 64.0), ("zn", -1.0)):
-        ts(A(name), io(160), GB16, AL.is_equal, c, AL.mult)
+    ts(A("zbot"), io(160), GB16, AL.is_equal, BOT, AL.mult)
     ts(A("selc", 0, 128), io(128), T0, AL.is_equal, TOP, AL.mult)
     ts(A("selc", 128, 256), io(128), T1, AL.is_equal, TOP, AL.mult)
     ts(A("h2"), io(64), PH, AL.is_equal)
-    ts(A("jm"), io(128), -128.0, AL.add)
-    cp(A("bc"), io(16))
-    iota(A("t1", 0, 48), [[0, 3], [16, 8], [0, 2]])
-    ts(A("b48"), A("t1", 0, 48), GB, AL.is_equal)
-    cp(A("b48p"), A("b48"))
-    ts(A("b48p", 1, 16, 2), A("b48", 1, 16, 2), -1.0, AL.mult)
-    ts(A("b48p", 32, 48), A("b48", 32, 48), -1.0, AL.mult)
-    ts(A("b48n"), A("b48p"), -1.0, AL.mult)
-    ms(A("ru"), 0.0)
+    iota(A("t1", 16, 64), [[0, 3], [16, 8], [0, 2]])
+    ts(A("b48"), A("t1", 16, 64), GB, AL.is_equal)
+    cp(A("bp"), A("b48"))
+    ts(A("bp", 16, 32), A("b48", 16, 32), -1.0, AL.mult)
+    for nm, c in (("bn", -1.0), ("bp2", 2.0), ("bn2", -2.0)):
+        ts(A(nm), A("bp"), c, AL.mult)
+    iota(A("ru"), [[0, 32]])
     ts(A("ru", 1, 16, 2), A("b48", 1, 16, 2), TOP, AL.mult)
     ts(A("ru", 16, 32, 2), A("b48", 0, 16, 2), BOT, AL.mult)
     ts(A("rf", 0, 16), A("b48", 0, 16), TOP, AL.mult)
     ts(A("rf", 16, 32), A("b48", 0, 16), BOT, AL.mult)
+    ts(A("rfd"), A("b48", 0, 16), SG, AL.mult)
     ts(A("ro", 0, 16), A("b48", 0, 16), BOT, AL.mult)
     ts(A("ro", 16, 32), A("b48", 0, 16), TOP, AL.mult)
-    iota(A("bias", 0, 128), [[0, 8], [-1, 2], [0, 8]])
-    iota(A("bias", 128, 384), [[-1, 2], [0, 128]])
     iota(A("par"), [[0, 16], [1, 2], [0, 8]])
     ts(A("par"), A("par"), P1, AL.is_equal)
-    iota(A("zero"), [[0, 256]])
+    iota(A("bias", 0, 256), [[-1, 2], [0, 128]])
+    ts(A("bias", 256, 384), A("par", 0, 128), -1.0, AL.add, 16384.0, AL.mult)
+    iota(A("zero"), [[0, 128]])
     iota(A("ones"), [[0, 128]], 1)
-    iota(A("t2", 0, 128), [[1, 16], [256, 8]])
-    ts(A("pil"), A("t2", 0, 128), P256, AL.add)
-    ms(A("t3", 0, 128), 1.0 / 3.0)
-    iota(A("t3", 128, 256), [[0, 128]])
-    op("V", lambda: vec.tensor_tensor_scan(A("t1", 128, 256)[0], A("t3", 0, 128)[0], A("t3", 128, 256)[0], float(3.0 ** 62), AL.mult, AL.add),
-       200, [A("t3")], [A("t1", 128, 256)])
-    ts(A("thr"), A("t1", 128, 256), 2.2, AL.mult)
-    tt(A("t3", 0, 128), A("t1", 128, 256), A("iff"), AL.mult)
+    iota(A("nones"), [[0, 256]], -1)
+    iota(A("t2", 144, 208), [[1, 16], [256, 4]])
+    iota(A("t2", 208, 256), [[1, 16], [256, 3]])
+    ts(A("pil"), A("t2", 144, 256), P256, AL.add)
+    ts(A("t3", 0, 128), A("ones"), 1.0 / 3.0, AL.mult)
+    scan(A("t3", 128, 256), A("t3", 0, 128), A("zero"), float(3.0 ** 62), AL.mult, AL.add)
+    tt(A("t3", 0, 128), A("t3", 128, 256), A("iff"), AL.mult)
     op("V", lambda: vec.tensor_reduce(WC[0], A("t3", 0, 128)[0], AxisListType.X, AL.add), 200, [A("t3", 0, 128)], [WC])
     ts(TC, WC, 2.2, AL.mult)
-    iota(A("cw"), [[0, 240]])
-    ts(A("cw", 112, 128), A("ones", 0, 16), WC, AL.mult)
-    asel(A("r8"), A("rr", 0, 1024), [[-16, 8], [0, 128]], 0, 1)
-    asel(A("rr"), A("rr"), [[-1, 128], [0, 16]], 0, 1)
-    iota(A("iot", 256, V), [[1, V - 256]], 256)
+    ts(A("cw"), A("ones", 0, 16), WC, AL.mult)
+    iota(A("r8"), [[16, 8], [0, 128]])
+    ts(A("r8"), A("r8"), GB, AL.is_equal)
     iota(A("mask"), [[0, 129], [1, 8]])
     ts(A("mask"), A("mask"), P8, AL.is_equal)
     for k in range(8):
         ts(A("rom", 32 * k, 32 * k + 32), A("ro"), A("mask", k, k + 1), AL.mult)
-    ts(A("nb", 0, V0), A("nb", 0, V0), MAGIC, AL.add, OFC, AL.add)
-    ops[-1]["rd"] += [("nb%d" % s, 0, 1) for s in (0, 8, 9, 10, 11, 12, 13, 14, 15)]
+    cp(A("p0"), A("stall"))
+    iota(A("nb", V0, V), [[0, V - V0]], int(OFF))
+    iota(A("wt"), [[0, WT]])
+    dma("Y", [(A("wz"), A("wt"))], 2500)
 
-    xw, nbw, iow = A("xs"), A("nb"), A("iot")
+    xw = A("xs")
 
-    def search(t, lo, w, e, banks, tiles, pieces):
-        d0, d1, kb, xb = banks
-        t1, t2, t3 = [(lambda a, b, s=1, x=x: A(x[0], x[1] + a, x[1] + b, s)) for x in tiles]
-        cs = lambda nm: A(nm, lo, lo + w)
-        ls = lambda nm: A(nm, lo // 16, (lo + w) // 16)
-        q = w // 16
-        for i in range(lo // 128, (lo + w) // 128):
-            xv = A("xf", M * t, M * t + M) if i else A("xs", V0 + M * t, V0 + M * t + M)
-            cp(A("p16", 8 * i, 8 * i + 8), A("stf" if i else "sti", 8 * t, 8 * t + 8))
-            cp(A("ph", 8 * i, 8 * i + 8), A("stf" if i else "sti", 8 * t, 8 * t + 8))
-            mm([(A(xb, 128 * i, 128 * i + 128), xv, IB, True, True)])
-            ac(A("xvt", 128 * i, 128 * i + 128), A(xb, 128 * i, 128 * i + 128), scale=-1.0)
-            tt(A("oh", 128 * i, 128 * i + 128), IN(A("xs", 0, V0), A("p16", 8 * i, 8 * i + 8)), xv, AL.subtract)
-        ac(cs("oh"), cs("oh"), AF.Abs)
-        mm([(A(kb, 0, w), Z("z64", 0), cs("oh"), True, True)])
-        ac(t1(0, w), A(kb, 0, w))
-        tr(t2(0, w), t1(0, w))
-        cp(ls("stay"), t2(0, w, 16))
+    def nbg(i):
+        ops[i]["rd"] += NBS
+        return i
+
+    def search(t, sd, eng, d0, d1, kb):
+        nbw = A("nb", 0, V0 + M * t)
+        cs = lambda nm: A(nm, 128 * sd, 128 * sd + 128)
+        ks = lambda nm, a=0, s=1: A(nm, 144 * sd + a, 144 * sd + 144, s)
+        big = lambda nm, a, b, s=1: A(nm, 2048 * sd + a, 2048 * sd + b, s)
+        for s in range(16):
+            gcopy(big("rep", s, 2048, 16), XV(t, sd))
+        p = ST("p0", t, sd)
+        tt(cs("yy"), IN(ST("stall", t, sd), A("bc", 0, 8)), A("mt"), AL.mult)
+        tt(cs("d0"), IN(A("xs", 0, V0), p), XV(t, sd), AL.subtract)
+        ac(cs("d0"), cs("d0"), AF.Abs)
         for h in range(2):
-            cp(cs("c16"), IN(nbw, ls("p16")))
-            ac(t3(0, w), IN(nbw, ls("p16")))
-            tt(cs("pd"), IN(iow, ls("p16")), t3(0, w), AL.subtract)
-            for i in range(w // 64):
-                nm, o = pieces[i % len(pieces)]
-                j = lo + 64 * i
-                gat(e[i % len(e)], A(nm, o, o + 1024), IN(xw, A("c16", j, j + 64)))
-                for u, bank in enumerate((d0, d1)):
-                    ro = 16 * (j % 128) + 512 * u
-                    x = A(nm, o + 512 * u, o + 512 * u + 512)
-                    mm(acc(A(bank), [(IB, x), (A("xvt", j - j % 128, j - j % 128 + 128), A("rr", ro, ro + 512))]))
-                    ac(x, A(bank), AF.Abs)
-                mm(acc(A(kb, 64 * i, 64 * i + 64), [(Z("z64", s), A(nm, o + s, o + 1024, 16)) for s in range(16)]))
-            ac(t1(0, w), A(kb, 0, w), bias=IDX)
-            tr(t2(0, w), t1(0, w))
-            tt(t1(0, w // 2), t2(0, w, 2), t2(1, w, 2), AL.min)
-            a = 0
-            for m in (8 * q, 4 * q, 2 * q):
-                tt(t1(a + m, a + m + m // 2), t1(a, a + m, 2), t1(a + 1, a + m, 2), AL.min)
-                a += m
-            tt(ls("mm"), t1(a, a + q), ls("stay"), AL.min)
-            tt(cs("oh"), IN(ls("mm"), A("bc", 0, q)), t2(0, w), AL.is_equal)
-            tr(cs("oht"), cs("oh"))
-            tt(cs("sel"), cs("oht"), cs("pd"), AL.mult)
-            mm(acc(A(xb, 0, q), [(A("iff"), ls("ph"))] + [(Z("zn", r), A("sel", lo + r, lo + w, 16)) for r in range(16)]))
-            cp(ls("p16"), A(xb, 0, q))
-            if h == 0:
-                cp(ls("ph"), A(xb, 0, q))
-                ts(ls("stay"), ls("mm"), MAGIC64, AL.add, -MAGIC64, AL.add)
+            nbg(ts(cs("c16"), IN(nbw, p), -OFF, AL.add))
+            nbg(ac(cs("cf"), IN(nbw, p)))
+            one = A(kb, 145, 288, 18)
+            grp([(A(kb, 144, 288), cs("cf"), A("dm"))] + ([(one, cs("yy"), A("b8")), (one, A("mt"), A("b64"))] if h == 0 else [(one, A("iff"), ks("ee", 17, 18))]))
+            for i in range(2):
+                x, lst = big("sc", 1024 * i, 1024 * i + 1024), IN(xw, A("c16", 128 * sd + 64 * i, 128 * sd + 64 * i + 64))
+                if eng[i] == "V":
+                    tt(x, lst, big("rep", 1024 * i, 1024 * i + 1024), AL.subtract)
+                    ac(x, x, AF.Abs)
+                else:
+                    ac(x, lst)
+                    for u, bank in enumerate((d0, d1)):
+                        a = 1024 * i + 512 * u
+                        mm(acc(A(bank), [(IB, big("sc", a, a + 512)), (A("ibn"), big("rep", a, a + 512))]))
+                        ac(big("sc", a, a + 512), A(bank), AF.Abs)
+            stay = (A(kb, 0, 144, 18),) + ((cs("d0"), A("b64")) if h == 0 else (A("iff"), ks("s1", 17, 18)))
+            grp([(A(kb, 0, 144), IB, A("kb", 144 * h, 144 * h + 144)), stay] + [(A(kb, 1 + s, 144, 18), big("sc", s, 2048, 16), A("b64")) for s in range(16)])
+            scan(ks("s1"), A("rst"), A(kb, 0, 144), 0.0, AL.add, AL.min)
+            tt(ks("nf"), ks("s1"), A(kb, 0, 144), AL.not_equal)
+            scan(ks("ee"), A(kb, 144, 288), ks("nf"), 0.0, AL.add, AL.mult)
+            tt(cs("xx"), IN(ks("ee"), A("bc", 8, 16)), A("mt"), AL.mult)
+            mm([(A(kb, 288, 296), cs("xx"), A("b8"), True, True)])
+            p = A("pr", 32 * t + 16 * sd + 8 * h, 32 * t + 16 * sd + 8 * h + 8)
+            ts(p, A(kb, 288, 296), -OFF, AL.add)
+        return p
 
     posf, posr, nbk = [0], [0], [0]
     chain = {"V": [], "S": []}
     for t in range(RO):
         old, have = V0 + M * t, V0 + M * (t + 1)
+        nbw = A("nb", 0, old)
         first = len(ops)
-        iota(A("wt", 1024, V + 128), [[0, V + 128 - 1024]])
-        iota(A("val"), [[1, 128], [0, 8]], old)
-        VC, NVC = C(19 + t), C(22 + t)
-        ts(VC, P_, float(old), AL.add)
-        ts(NVC, VC, -1.0, AL.mult)
-        ts(A("dv"), IB, VC, AL.mult)
-        tl, pc = (("t1", 0), ("t2", 0), ("t3", 0)), (("sc", 0), ("sc", 1024))
-        if t == 0:
-            search(t, 0, 128, "V", (D0, D1, K, X), tl, pc)
-            search(t, 128, 128, "S", (Y0, Y1, Y2, Y2), (("ring", 3072), ("ring", 3328), ("ring", 3584)), (("sc2", 0),))
-        else:
-            search(t, 0, 256, PAR["sg"][t], (D0, D1, K, X), tl, pc)
-        iota(A("wt", 0, 1024), [[0, 1024]])
-        ac(A("ys"), IN(A("ya", 0, old), A("p16", 8, 16)))
+        pf = search(t, 1, PAR["far"][t], Y0, Y1, KF)
+        for o in ops[first:]:
+            o["lead"] = PAR["flead"][t]
+        ac(A("ys"), IN(A("ya", 0, old), pf))
         dst = T.cores[(rank - 1 - t) % n]
         rid, pid, _ = topo.addr(dst)
         sent[0] += len(topo.engines(core, dst))
         s = op("G", (lambda a=A("ya", old, have)[0], rid=rid, pid=pid, m=topo.mask(core, dst), t=t:
                      g.remote_dma(a, A("ys")[0], T.sem["ay%d" % t], T.sem.sent, pid, rid, m)), 1500, [A("ys")], [], kind="x", sem=T.sem.sent, cnt=sent[0], lat=2500.0)
         arrive("ay%d" % t, len(topo.engines(T.cores[(rank + 1 + t) % n], core)), A("ya", old, have), s)
-        bl = A("p16", 0, 8)
-        dma("Y", [(A("flat", s * V, s * V + old, p=row(s)), A("nb", 0, old, p=row(s))) for s in range(16)], 2800)
+        first = len(ops)
+        bl = search(t, 0, PAR["own"][t], D0, D1, KO)
+        iota(A("val"), [[1, 128], [0, 8]], old + int(OFF))
+        VC = C(20 + t)
+        ts(VC, P_, old - OFF, AL.add)
+        ts(A("dv"), IB, VC, AL.mult, 1.0, AL.add)
+        if t:
+            dma("Y", [(A("wt"), A("wz"))], 2500)
+            dma("Y", [(A("flat", s * V, s * V + old, p=row(s)), A("nb", 0, old, p=row(s))) for s in range(16)], 2800)
+        XX = A("xx", 0, 128)
         cp(A("nbb"), IN(nbw, bl))
-        mm(acc(A(X, 0, 64), [(A("selc", 128 * h, 128 * h + 128), A("nbb", h, 128, 2)) for h in range(2)]))
-        cp(A("cq"), A(X, 0, 64))
+        mm(acc(A(KO, 296, 360), [(A("selc", 128 * h, 128 * h + 128), A("nbb", h, 128, 2)) for h in range(2)]))
+        ts(A("cq"), A(KO, 296, 360), -OFF, AL.add)
         tt(A("gg"), IN(nbw, A("cq")), A("mask", 0, 1024), AL.mult)
         ac(A("xcq"), IN(xw, A("cq")))
-        cp(A("brep"), IN(iow, bl))
+        GK = lambda k: A("gg", k, 1024, 8)
+        mm([(A(KO, k, 256, 8), GK(k), A("rf"), True, True) for k in range(8)])
+        tt(A("fam"), A(KO, 0, 256), A("par"), AL.mult)
+        mm([(A(KO, 360 + 64 * u, 424 + 64 * u), A("fam", 128 * u, 128 * u + 128), A("h2"), True, True) for u in range(2)])
+        ts(A("fa"), A(KO, 360, 488), -OFF, AL.add)
+        mm([(A(TT, 384, 512), XX, IB, True, True)])
+        cp(A("brep"), A(TT, 384, 512))
         ts(A("nbrep"), A("brep"), -1.0, AL.mult)
         for u, bank in enumerate((D0, D1)):
             c = []
@@ -386,73 +407,79 @@ def build(g, core, T, topo):
                 rg = A("r8", 128 * (4 * u + q), 128 * (4 * u + q) + 128)
                 c += acc(A(bank, 128 * q, 128 * q + 128), [(rg, A("brep")), (A("nbrep"), rg)])
             mm(c)
-            if PAR["eq"][t][u] == "V":
-                ts(A("eq", 512 * u, 512 * u + 512), A(bank), 0.0, AL.is_equal)
-            else:
-                ac(A("eq", 512 * u, 512 * u + 512), A(bank), AF.Abs)
-                ac(A("eq", 512 * u, 512 * u + 512), A("eq", 512 * u, 512 * u + 512), AF.Relu, scale=-1.0, bias=1.0)
-        mm(acc(A(X, 0, 64), [(Z("ztop", r), A("gg", r, 1024, 16)) for r in range(16)]) + acc(A(X, 64, 128), [(Z("zbot", r), A("gg", r, 1024, 16)) for r in range(16)]))
-        cp(A("fa"), A(X, 0, 128))
+            ts(A("eq", 512 * u, 512 * u + 512), A(bank), 0.0, AL.is_equal)
         EQ = lambda q: A("eq", 128 * q, 128 * q + 128)
-        mm(acc(A(X, 128, 256), [(A("cw", 112 - 16 * q, 240 - 16 * q), EQ(q)) for q in range(8)]))
-        tt(A("t1", 0, 128), A(X, 128, 256), A("thr"), AL.is_ge)
-        tt(A("t1", 128, 256), A("jm"), A("brep"), AL.subtract)
-        tt(A("t2", 0, 128), A("t1", 0, 128), A("t1", 128, 256), AL.mult)
-        tt(A("oo"), A("t2", 0, 128), A("brep"), AL.add)
-        mm(acc(A(X, 256, 264), [(Z("z0", r), A("oo", r, 128, 16)) for r in range(16)]))
-        ts(A("rl"), A(X, 256, 264), 128.0, AL.add)
-        mm([(A(TT, 0, 256), A("nbb"), A("selc"), True, False)] + [(A(TT, k, 256, 8), A("gg", k, 1024, 8), A("ru"), False, k == 7) for k in range(8)]
-           + [(A(TT, 256 + k, 512, 8), A("gg", k, 1024, 8), A("rf"), True, True) for k in range(8)])
-        ac(A("t3"), A(TT, 0, 256), bias=NVC)
-        tt(A("fam"), A(TT, 256, 512), A("par"), AL.mult)
-        mm([(A(K, 0, 384), IB, A("bias"), True, False)])
-        for i, (l, sg) in enumerate(((0, "b48p"), (0, "b48n"), (1, "b48n"), (1, "b48p"))):
-            if i % 2 == 0:
-                gat(PAR["eg"][t], A("sc", 1024 * l, 1024 * l + 1024), IN(xw, A("fa", 64 * l, 64 * l + 64)))
-            ab, o = ("sc", 1024 * l) if i % 2 else ("ab", 0)
-            for u, bank in enumerate((D0, D1)):
-                sub = (A("xvt", 0, 128), A("rr", 1024 * u, 1024 * u + 1024, 2)) if i % 2 else (A("ibn"), A("xcq", 512 * u, 512 * u + 512))
-                mm(acc(A(bank), [(IB, A("sc", 1024 * l + 512 * u, 1024 * l + 512 * u + 512)), sub]))
-                ac(A(ab, o + 512 * u, o + 512 * u + 512), A(bank), AF.Abs)
-            mm([(A(K, k, 384, 8), A(ab, o + k, o + 1024, 8), A(sg), False, i == 3 and k == 7) for k in range(8)])
-        ts(A("ind"), A(K, 0, 384), 0.0, AL.is_ge)
-        ts(A("dw"), A("ind", 0, 128), WC, AL.mult)
-        tt(A("ot"), A("ind", 128, 384), A("fam"), AL.mult)
-        tt(A("t3"), A("ind", 128, 384), A("t3"), AL.mult)
-        mm([(A(X, 128 + 16 * q, 144 + 16 * q), EQ(q), A("dw", 16 * q, 16 * q + 16), True, True) for q in range(8)])
-        ac(A("wts"), A(X, 128, 256))
-        mm(acc(A(D0, 0, 64), [(A("ot", 128 * u, 128 * u + 128), A("h2")) for u in range(2)]))
-        cp(A("o16"), A(D0, 0, 64))
-        mm([(A(D1, 0, 128), A("wts"), IB, True, True)])
-        ac(A("wrow"), A(D1, 0, 128))
-        mm([(A(TT, 0, 256), IB, A("zero"), True, False)]
-           + [(A(TT, 128 * z + 16 * q + 8 * d, 128 * z + 16 * q + 8 * d + 8), EQ(q), A("dw", 16 * q + 8 * z, 16 * q + 8 * z + 8), False, False)
-              for z in range(2) for q in range(8) for d in range(2)])
+        grp([(A(D0, 0, 128), IB, A("negm"))] + [(A(D0, 16 * q, 16 * q + 16), EQ(q), A("cw")) for q in range(8)])
+        ts(A("nfx"), A(D0, 0, 128), TC, AL.is_ge, JC, AL.mult)
+        tt(A("rlx"), A("nfx"), XX, AL.max)
+        mm([(A(D1, 0, 8), A("rlx"), A("b8"), True, True)])
+        cp(A("rl"), A(D1, 0, 8))
+        grp([(A(TT, 0, 256), A("nbb"), A("selc")), (A(TT, 0, 256), A("dv"), A("nones"))] + [(A(TT, k, 256, 8), GK(k), A("ru")) for k in range(8)])
+        mm([(A(TT, 256 + k, 384, 8), GK(k), A("rfd"), True, True) for k in range(8)])
+        r8v = lambda a, b: A("rep", 2 * a, 2 * b, 2)
+        keys = lambda nm, o, sg: [(A(KO, k, 384, 8), A(nm, o + k, o + 1024, 8), A(sg)) for k in range(8)]
+        far = PAR["gf"][t] == "S"
+        fl, al = IN(xw, A("fa", 0, 64)), IN(xw, A("fa", 64, 128))
+        grp([(A(KO, 0, 384), IB, A("bias"))] + (keys("xcq", 0, "bp") + [(A(KO, k, 384, 8), XV(t, 0), A("bn")) for k in range(8)] if far else []), stop=False)
+        tt(A("sc", 0, 1024), al, A("xcq"), AL.max)
+        tt(A("sc", 1024, 2048), al, r8v(0, 1024), AL.max)
+        if far:
+            ac(A("ab"), fl)
+            for o, sub in (("xcq", lambda u: A("xcq", 512 * u, 512 * u + 512)), ("ab", lambda u: r8v(512 * u, 512 * u + 512))):
+                for u, bank in enumerate((D0, D1)):
+                    mm(acc(A(bank), [(IB, A("ab", 512 * u, 512 * u + 512)), (A("ibn"), sub(u))]))
+                    ac(A(o, 512 * u, 512 * u + 512), A(bank), AF.Abs)
+        else:
+            tt(A("ab"), fl, A("xcq"), AL.max)
+            tt(A("xcq"), fl, r8v(0, 1024), AL.max)
+        grp(keys("sc", 0, "bn2" if far else "bn"), start=False, stop=False)
+        grp(keys("sc", 1024, "bp2" if far else "bp"), start=False, stop=False)
+        grp(keys("xcq", 0, "bp" if far else "bn"), start=False, stop=False)
+        grp(keys("ab", 0, "bn" if far else "bp"), start=False)
+        ts(A("indp"), A(KO, 256, 384), 0.0, AL.is_ge)
+        ts(A("dw"), A(KO, 0, 256), 0.0, AL.is_ge, WC, AL.mult)
+        tt(A("ot"), A("indp"), A(TT, 256, 384), AL.mult)
+        mm(acc(A(D0, 0, 64), [(A("fam", 128, 256), A("h2")), (A("ot"), A("h2"))]))
+        ts(A("o16"), A(D0, 0, 64), -OFF, AL.add)
+        mm([(A(D1, 16 * q + 8 * z, 16 * q + 8 * z + 8), EQ(q), A("dw", 128 * z + 16 * q, 128 * z + 16 * q + 8), True, True) for q in range(8) for z in range(2)])
+        ac(A("wts"), A(D1, 0, 128))
+        mm([(A(D1, 128, 256), A("wts"), IB, True, True)])
+        ac(A("wrow"), A(D1, 128, 256))
+        grp([(A(KO, 0, 256), A("zero"), A("nones"))] + [(A(KO, 128 * z, 128 * z + 128), A("i3"), A("dw", 128 - 128 * z, 256 - 128 * z)) for z in range(2)]
+            + [(A(KO, 16 * q, 16 * q + 16), EQ(q % 8), A("dw", 16 * q, 16 * q + 16)) for q in range(16)], stop=False)
         tt(A("gg"), IN(nbw, A("o16")), A("mask", 1, 1025), AL.mult)
-        mm(acc(A(X, 0, 64), [(Z("zbot", r), A("gg", r, 1024, 16)) for r in range(16)]))
-        cp(A("b16"), A(X, 0, 64))
+        mm(acc(A(D0, 64, 128), [(A("zbot", 16 - r, 144 - r), A("gg", r, 1024, 16)) for r in range(16)]))
+        cp(A("b16"), A(D0, 64, 128))
         cp(IN(A("wt"), A("rl")), A("wrow"))
-        gat(PAR["wg"][t], A("gw"), IN(A("wt", 128, V + 128), A("b16")))
-        mm([(A(TT, k, 256, 8), A("gw", k, 1024, 8), A("rom", 32 * k, 32 * k + 32), False, k == 7) for k in range(8)])
-        ts(A("t1"), A(TT, 0, 256), TC, AL.is_lt)
-        tt(A("zz"), A("t1"), A("t3"), AL.mult)
-        mm(acc(A(X, 0, 128), [(A("ones"), A("dv")), (A("zz", 0, 128), IB), (A("zz", 128, 256), IB)]))
-        cp(A("thh"), A(X, 0, 128))
+        ac(A("gw"), IN(A("wt"), A("b16")))
+        grp([(A(KO, k, 256, 8), A("gw", k, 1024, 8), A("rom", 32 * k, 32 * k + 32)) for k in range(8)], start=False)
+        ts(A("mw"), A(KO, 0, 256), TC, AL.is_lt)
+        tt(A("zz"), A("mw"), A(TT, 0, 256), AL.mult)
+        mm(acc(A(D0, 128, 256), [(A("ones"), A("dv")), (A("zz", 0, 128), IB), (A("zz", 128, 256), IB)]))
+        ts(A("thh"), A(D0, 128, 256), -OFF, AL.add)
         SQ = lambda i: A("sq", 128 * i, 128 * i + 128)
-        mm([c for z in range(2) for c in acc(A(D0, 64 * z, 64 * z + 64), [(SQ(2 * z + h), A("thh", h, 128, 2)) for h in range(2)])])
-        ts(A("sl"), A(D0, 0, 128), SV, AL.add)
+        mm([c for z in range(2) for c in acc(A(D1, 64 * z, 64 * z + 64), [(SQ(2 * z + h), A("thh", h, 128, 2)) for h in range(2)])])
+        ts(A("sl"), A(D1, 0, 128), SV, AL.add)
         cp(IN(A("flat", 0, 8 * V), A("sl", 0, 64)), A("val"))
         ac(IN(A("flat", 8 * V, 16 * V), A("sl", 64, 128)), A("val"), AF.Silu)
-        dma("Y", [(A("nb", 0, old, p=row(s)), A("flat", s * V, s * V + old, p=row(s))) for s in range(16)], 2800)
-        mm(acc(A(D1, 0, 128), [(SQ(1), A("thh")), (SQ(2), A("thh"))]))
-        ac(A("nb", old, have), A(D1, 0, 128))
-        if t + 1 == RO:
-            dma("Y", [(T.nx[k::8, :], A("nb", p=row(k))) for k in range(8)], 3000)
-        cp(A("nbp"), IN(nbw, A("pil")))
-        for z in (1, 0):
-            dma("Y", [(A("off", 128 * s, 128 * s + 128), A("nbp", p=row(s))) for s in range(8 * z, 8 * z + 8)], 2500)
+        nbg(mm(acc(A(D0, 256, 384), [(SQ(1), A("thh")), (SQ(2), A("thh"))])))
+        ac(A("nb", old, have), A(D0, 256, 384), bias=OFF)
+        W = (64, 48 if have == 1792 else 64)
+        for r, (a, b) in enumerate(((0, 1024), (1024, old))):
+            for z in range(2):
+                dma(PAR["dq"][t][z], [(A("nb", a, b, p=row(s)), A("flat", s * V + a, s * V + b, p=row(s))) for s in range(8 * z, 8 * z + 8)], 2400)
+                ops[-1]["comm"] = True
+        for r in range(2):
+            a, w, l = 1024 * r, W[r], (0 if W[r] == 64 else 64)
+            ts(A("nbp", a, a + 16 * w), IN(A("nb", a, a + 16 * w), A("pil", l, l + w)), -OFF, AL.add)
+            for z in (1, 0):
+                dma(PAR["dq"][t][z], [(A("off", a + w * s, a + w * s + w), A("nbp", a, a + 16 * w, p=row(s))) for s in range(8 * z, 8 * z + 8)], 2300)
+        OL = lambda s, a, b: A("off", (a - a % 1024) + W[a // 1024] * s + a % 1024 // 16, (a - a % 1024) + W[a // 1024] * s + (b - a + a % 1024) // 16)
         for o in ops[first:]:
             o["lead"] = PAR["lead"][t]
+        if t + 1 == RO:
+            ac(A("nb"), A("nb"), bias=-OFF)
+            dma("Y", [(T.nx[k::8, :], A("nb", p=row(k))) for k in range(8)], 3000)
         nch = [0]
         for sw in range(2):
             nev = [0]
@@ -467,7 +494,8 @@ def build(g, core, T, topo):
                 for i in range((w + 511) // 512):
                     parts.append(((Y0, Y1, Y2)[nbk[0] % 3], 512 * i, min(w, 512 * i + 512)))
                     nbk[0] += 1
-                fold = PAR["fold"][t] if ci < len(cuts) - 3 else PAR["foldl"][len(cuts) - 2 - ci]
+                fl = PAR["foldl"][t]
+                fold = fl[len(cuts) - 2 - ci] if len(cuts) - 2 - ci < len(fl) else PAR["fold"][t]
                 terms = [(src, a)]
                 place = []
                 for k in range(8):
@@ -477,9 +505,8 @@ def build(g, core, T, topo):
                     pos[0] += w
                     place.append(o)
                     pk = A(rn, o, o + w)
-                    chain["S"] = [ac(pk, IN(yw, A("off", 128 * (8 + k) + a // 16, 128 * (8 + k) + b // 16)), after=chain["S"], scale=-0.125)]
-                    chain["V"] = [tt(pk, IN(yw, A("off", 128 * k + a // 16, 128 * k + b // 16)), pk, AL.mult, after=chain["V"])]
-                    ops[chain["S"][0]]["lead"] = PAR["alead"][t]
+                    chain["S"] = [ac(pk, IN(yw, OL(8 + k, a, b)), after=chain["S"], scale=-0.125)]
+                    chain["V"] = [tt(pk, IN(yw, OL(k, a, b)), pk, AL.mult, after=chain["V"])]
                     if k == 0 and -1 in fold:
                         fold_dma(pk, A(src, a, b))
                         terms = [(rn, o)]
@@ -512,13 +539,15 @@ def schedule(ops):
         for regs, w in ((o["rd"], False), (o["wr"], True)):
             for nm, a, b in regs:
                 for j, a2, b2, w2 in hist.get(nm, ()):
+                    if w and w2 and o.get("comm") and ops[j].get("comm"):
+                        continue
                     if j != i and ((nm[:2] == "ps" and (ops[j]["eng"] != o["eng"] or o["eng"] == "P")) or ((w or w2) and a < b2 and a2 < b)):
                         deps.add(j)
                         soft.discard(j)
         for regs, w in ((o["rd"], False), (o["wr"], True)):
             for nm, a, b in regs:
                 h = hist.setdefault(nm, [])
-                if w and nm[:2] != "ps":
+                if w and nm[:2] != "ps" and not o.get("comm"):
                     h[:] = [e for e in h if not (a <= e[1] and e[2] <= b)]
                 if nm[:2] == "ps":
                     h[:] = [e for e in h if e[0] != i][-12:]
@@ -545,11 +574,11 @@ def schedule(ops):
     for _ in ops:
         e = min((e for e in ready if ready[e]), key=lambda e: max(free[e], min(ops[i]["rdy"] for i in ready[e])))
         now = max(free[e], min(ops[i]["rdy"] for i in ready[e]))
-        i = max((i for i in ready[e] if ops[i]["rdy"] <= now), key=lambda i: (ops[i]["bl"] + ops[i].get("lead", 0.0), -i))
+        i = max((i for i in ready[e] if ops[i]["rdy"] <= now + PAR["look"]), key=lambda i: (ops[i]["bl"] + ops[i].get("lead", 0.0), -i))
         ready[e].remove(i)
         o = ops[i]
-        o["t0"] = now
-        free[e] = now + o["dur"]
+        o["t0"] = max(now, o["rdy"])
+        free[e] = o["t0"] + o["dur"]
         o["end"] = free[e] + o["lat"]
         order[e].append(i)
         for j in succ[i]:

@@ -1,3 +1,5 @@
+import math
+import numpy as np
 from concourse.bass import DstId, RemoteDMATransfer
 from concourse.mybir import AluOpType, AxisListType, ActivationFunctionType
 
@@ -9,7 +11,8 @@ F, B, I, U = "float32", "bfloat16", "int32", "uint16"
 OFF = 64.0
 RING = 3824
 WT = 2368
-NF = 64
+MAGIC = 12582912.0
+NF = 52
 PAR = dict(
     cuts=((0, 512, 1024, 1536, 1792), (0, 512, 1024, 1536, 1792, 1920), (0, 512, 1024, 1536, 1792, 2048)),
     dq=("YS", "YY", "YY"),
@@ -22,9 +25,17 @@ PAR = dict(
     ev=("S", "S", "VS"), evl=5000.0,
     own=("VS", "VS", "VS"), far=("SV", "VV", "VV"),
     gf=("S", "S", "S"),
-    look=150.0,
+    nxs=("V", "S", "S"), outl=0.0,
+    cs="S",
+    hold=(0, 1, 1),
+    passes=2, look=150.0,
     CY=0.9, GA=1.55, SCA=3.8, PE=0.5, LAT=90.0, DL=1.0)
 PAR.update({'cuts': ((0, 512, 1024, 1536, 1792), (0, 512, 1024, 1536, 1920), (0, 512, 1024, 1536, 1920, 2048)), 'dq': ('YY', 'YY', 'YY'), 'cutv': 88, 'fold': ((0, 2, 4), (1, 3, 5), (1, 3, 5)), 'foldl': (((), (-1, 1, 3)), ((-1, 1), (0, 2, 4)), ((0, 2, 4, 6),)), 'nflat': (6, 6, 99), 'lead': (-20000.0, 20000.0, 10000.0), 'flead': (-20000.0, 5000.0, 0.0), 'ev': ('S', 'SSV', 'SSV'), 'evl': 0.0, 'own': ('VS', 'VS', 'VS'), 'far': ('SV', 'VV', 'VV'), 'gf': ('S', 'V', 'S'), 'look': 200.0, 'CY': 0.9, 'GA': 1.3, 'SCA': 3.8, 'PE': 0.5, 'LAT': 90.0, 'DL': 1.0})
+PAR.update(swaps=0, heat=0.002, early=(0, 0, 0), ysl=(0.0, 0.0, 0.0), seed=0, shake=1500.0, share=0.1)
+COSTS = (dict(CY=0.83, GA=1.55, SCA=3.8, PE=0.42, DL=1.0, LAT=80.0), dict(CY=0.95, GA=1.15, SCA=2.5, PE=0.55, DL=1.0, LAT=150.0),
+         dict(CY=0.9, GA=1.3, SCA=3.0, PE=0.47, DL=1.3, LAT=100.0), dict(CY=1.1, GA=1.8, SCA=5.0, PE=0.55, DL=1.1, LAT=100.0))
+PAR.update({'cuts': ((0, 512, 1024, 1536, 1792), (0, 512, 1024, 1536, 1920), (0, 512, 1024, 1536, 1792, 2048)), 'dq': ('YY', 'YY', 'YS'), 'cutv': 88, 'fold': ((0, 2, 4, 6), (0, 2, 4, 6), (0, 2, 4, 6)), 'foldl': (((0, 2),), ((0, 2),), ((10, 12, 14, 16),)), 'nflat': (6, 6, 99), 'lead': (-20000.0, 20000.0, 20000.0), 'flead': (-20000.0, 0.0, 30000.0), 'ev': ('S', 'S', 'S'), 'evl': 0.0, 'own': ('RS', 'RS', 'SR'), 'far': ('ER', 'EE', 'ER'), 'gf': ('S', 'V', 'S'), 'nxs': ('V', 'V', 'V'), 'outl': 0.0, 'cs': 'S', 'hold': (0, 4, 24), 'passes': 2, 'look': 200.0, 'CY': 0.83, 'GA': 1.55, 'SCA': 3.8, 'PE': 0.5, 'LAT': 60.0, 'DL': 1.4, 'swaps': 3000, 'heat': 0.0005})
+ORDER = {}
 SB = {
     "flat": (16 * V, F), "ring": (RING, F), "ya": (V, F), "yb": (V, F), "xs": (V, B), "nb": (V, F), "nbp": (V, U),
     "off": (V, U), "val": (1024, F), "ni": (832, I), "wt": (WT, B), "sc": (4096, B), "rep": (4096, B), "ab": (1024, B),
@@ -32,9 +43,9 @@ SB = {
     "xf": (384, B), "stall": (48, I), "p0": (48, U), "pr": (96, U), "ys": (128, F),
     "pi": (8, I), "col": (28, F), "ib": (128, B), "ibn": (128, B), "i3": (128, B), "iff": (128, F), "zbot": (160, B),
     "selc": (256, B), "sq": (512, B), "b48": (48, B), "bp": (48, B), "bn": (48, B), "bp2": (48, B), "bn2": (48, B),
-    "bias": (384, B), "ru": (32, B), "rf": (32, B), "rfd": (16, B), "ro": (32, B), "rom": (256, B), "par": (256, B), "h2": (64, B),
+    "bias": (384, B), "ru": (32, B), "rf": (32, B), "rfd": (16, B), "rom": (256, B), "par": (256, B), "h2": (64, B),
     "zero": (128, B), "ones": (128, B), "nones": (256, B), "dv": (128, H), "bc": (16, U), "pil": (112, U), "cw": (16, B),
-    "b8": (8, B), "b64": (8, B), "kb": (288, B), "rst": (144, B), "dm": (144, F), "mt": (128, B), "negm": (128, B),
+    "b8": (8, B), "b64": (8, B), "b64n": (8, B), "b128": (8, B), "kb": (288, B), "rst": (144, B), "dm": (144, F), "mt": (128, B), "negm": (128, B),
     "d0": (256, B), "c16": (256, U), "cf": (256, F), "s1": (288, F), "nf": (288, B), "ee": (288, F), "xx": (256, H),
     "nbb": (128, H), "cq": (64, U), "fa": (128, U), "brep": (128, H), "nbrep": (128, H), "rl": (8, U),
     "dw": (256, B), "indp": (128, B), "fam": (256, H), "ot": (128, H), "o16": (64, U), "b16": (64, U), "wts": (128, B),
@@ -46,7 +57,7 @@ SCRATCH = dict((k, ("sbuf", [128, n], d)) for k, (n, d) in SB.items())
 SCRATCH["wz"] = ("dram", [128, WT], B)
 for _b in range(8):
     SCRATCH["ps%d" % _b] = ("psum", [128, 512], F)
-SEMAPHORES = ["cV", "cS", "cP", "cG", "sent"] + ["d%d" % i for i in range(70)] + ["f%d" % i for i in range(NF)] + [k + str(t) for k in ("ax", "as", "ay") for t in range(RO)]
+SEMAPHORES = ["cV", "cS", "cP", "cG", "sent"] + ["d%d" % i for i in range(82)] + ["f%d" % i for i in range(NF)] + [k + str(t) for k in ("ax", "as", "ay") for t in range(RO)]
 
 
 def start_masks(T, topo, rank):
@@ -69,13 +80,13 @@ def start_masks(T, topo, rank):
     return out
 
 
-def build(g, core, T, topo):
+def build(g, core, T, topo, costs):
     rank = T.rank_of(core)
     n = len(T.cores)
     ops = []
     nsem = [0]
     vec, act, pe = g.vector, g.scalar, g.tensor
-    CY, GA, SCA, PE, DL = PAR["CY"], PAR["GA"], PAR["SCA"], PAR["PE"], PAR["DL"]
+    CY, GA, SCA, PE, DL = [costs[k] for k in ("CY", "GA", "SCA", "PE", "DL")]
 
     def A(name, a=0, b=None, s=1, p=None):
         if name in ALIAS:
@@ -128,6 +139,9 @@ def build(g, core, T, topo):
         kw = dict((x, ap(y)) for x, y in k.items())
         return op("S", lambda: act.activation(out[0], a[0], f, **kw), cost(out, a, 1) + 15 + extra, [a] + list(k.values()), [out], after=after)
 
+    def lin(out, a, m, c=0.0):
+        return ac(out, a, scale=m, bias=c) if PAR["cs"] == "S" else ts(out, a, m, AL.mult, c, AL.add)
+
     def mm(calls):
         def fn():
             for c in calls:
@@ -154,7 +168,11 @@ def build(g, core, T, topo):
         ops[i]["comm"] = True
         return i
 
-    def dma(eng, pairs, lat, **k):
+    def pick(out, pat, base):
+        a = A("ones", 0, out[4])
+        return op("G", lambda: g.affine_select(out[0], a[0], pat, AL.is_equal, 0.0, base, 1), 190 + 2 * out[4] * CY, [a], [out])
+
+    def dma(eng, pairs, lat, xfer=200.0, **k):
         sem = T.sem["d%d" % nsem[0]]
         nsem[0] += 1
         q = {"G": g, "Y": g.sync, "S": act}[eng]
@@ -162,8 +180,10 @@ def build(g, core, T, topo):
         def fn():
             for o, i in pairs:
                 q.dma_start(ap(o), ap(i), **k).then_inc(sem, 16)
-        return op(eng, fn, (900 if eng == "G" else 70) * len(pairs) * DL, [i for o, i in pairs], [o for o, i in pairs if isinstance(o, tuple)],
-                  kind="d", lat=lat * DL, sem=sem, cnt=16 * len(pairs))
+        j = op(eng, fn, (900 if eng == "G" else 70) * len(pairs) * DL, [i for o, i in pairs], [o for o, i in pairs if isinstance(o, tuple)],
+               kind="d", lat=lat * DL, sem=sem, cnt=16 * len(pairs))
+        ops[j]["xfer"] = xfer * len(pairs) * DL
+        return j
 
     folds = []
 
@@ -172,7 +192,7 @@ def build(g, core, T, topo):
         sem = T.sem["f%d" % (i % NF)]
         op("G", lambda: g.dma_start(out[0], a[0], accum_op=AL.add).then_inc(sem, 16), 900 * DL, [a, out], [out], kind="d",
            lat=(1800 + 1.7 * out[4]) * DL, sem=sem, cnt=16 * (i // NF + 1))
-        ops[-1].update(key="f%d" % (i % NF), cons=len(ops), hard=[folds[i - NF] + 1] if i >= NF else [])
+        ops[-1].update(xfer=(240 + (0.85 if two(out) else 1.7) * out[4]) * DL * DL, key="f%d" % (i % NF), cons=len(ops), hard=[ops[folds[i - NF]]["cons"]] if i >= NF else [])
         folds.append(len(ops) - 1)
 
     sent = [0]
@@ -193,10 +213,9 @@ def build(g, core, T, topo):
     dma("Y", [(A("ni", 104 * k, 104 * k + 104), T.nx0[k::8, :]) for k in (5, 1, 2, 3, 6, 7)], 3600)
     dma("Y", [(ST("stall", t, 0), T.st[:, 8 * t:8 * t + 8]) for t in range(RO)], 2300)
     dma("Y", [(A("xs"), T.x[:])], 3000)
+    early = [iota(A("pi", 0, 1), [[0, 1]], 0, 1), iota(A("iot"), [[1, 256]])]
     for h in range(2):
-        iota(A("ring", 832 * h, 832 * h + 832), [[1, 52], [104, 16]], int(OFF) + 52 * h)
-    ops[iota(A("pi", 0, 1), [[0, 1]], 0, 1)]["lead"] = 50000.0
-    ops[iota(A("iot"), [[1, 256]])]["lead"] = 50000.0
+        ops[iota(A("ring", 832 * h, 832 * h + 832), [[1, 52], [104, 16]], int(OFF) + 52 * h)]["after"] = early
     for a, b in ((4, 5), (0, 1), (1, 4), (5, 8)):
         cp(A("nbp", 104 * a, 104 * b), A("ni", 104 * a, 104 * b))
     cv = PAR["cutv"]
@@ -238,28 +257,29 @@ def build(g, core, T, topo):
     ts(TOP, P16, 8.0, AL.is_lt)
     ts(BOT, P16, 8.0, AL.is_ge)
     ts(FST, P16, 0.0, AL.is_equal)
-    ts(GB16, GB, 16.0, AL.add)
-    ts(T1, FST, 8.0, AL.mult, P_, AL.add)
-    ts(T0, T1, -1.0, AL.add)
-    ts(T1, T0, 8.0, AL.add)
-    ts(SV, P8, float(V), AL.mult)
-    ts(P256, P16, 16.0, AL.mult)
-    ts(SW, TOP, 16.0, AL.mult, P_, AL.add)
-    ts(SW, SW, -8.0, AL.add)
-    ts(JC, P_, 2.0, AL.mult, V + OFF, AL.add)
-    ts(G18, GB, 0.125, AL.mult, P_, AL.add)
-    ts(SG, TOP, 2.0, AL.mult, -1.0, AL.add)
+    lin(GB16, GB, 1.0, 16.0)
+    lin(SW, FST, 8.0, P_)
+    lin(T0, SW, 1.0, -1.0)
+    lin(T1, SW, 1.0, 7.0)
+    lin(SV, P8, float(V))
+    lin(P256, P16, 16.0)
+    lin(JC, P_, 2.0, V + OFF)
+    lin(G18, GB, 0.125, P_)
+    lin(SG, TOP, 2.0, -1.0)
     io = lambda w, a=0: A("iot", a, a + w)
+    iota(A("ones"), [[0, 128]], 1)
+    iota(A("nones"), [[0, 256]], -1)
     ts(IB, io(128), P_, AL.is_equal)
-    ts(A("ibn"), IB, -1.0, AL.mult)
-    ts(A("i3"), IB, 3.0, AL.mult)
-    ts(A("iff"), io(128), P_, AL.is_equal)
+    lin(A("ibn"), IB, -1.0)
+    lin(A("i3"), IB, 3.0)
+    lin(A("iff"), IB, 1.0)
     iota(A("t1", 0, 8), [[16, 8]])
     ts(A("b8"), A("t1", 0, 8), GB, AL.is_equal)
-    ts(A("b64"), A("b8"), 64.0, AL.mult)
+    for nm, c in (("b64", 64.0), ("b64n", -64.0), ("b128", 128.0)):
+        lin(A(nm), A("b8"), c)
     iota(A("t1", 128, 256), [[0, 8], [1, 16]])
     ts(A("mt"), A("t1", 128, 256), P16, AL.is_equal)
-    ts(A("negm"), A("mt"), -1.0, AL.add, 5e29, AL.mult)
+    lin(A("negm"), A("mt"), 2.0 ** 98, -2.0 ** 98)
     cp(A("bc", 0, 8), io(8))
     ts(A("bc", 8, 16), io(8), 18.0, AL.mult, 17.0, AL.add)
     for h in range(2):
@@ -271,54 +291,51 @@ def build(g, core, T, topo):
     ts(A("t2", 0, 144), io(144), -2.0, AL.add, G18, AL.is_equal)
     ts(A("dm"), io(144), -1.0, AL.add, G18, AL.is_equal)
     tt(A("dm"), A("t2", 0, 144), A("dm"), AL.subtract)
-    for i, (c, m) in enumerate(((P_, TOP), (SW, TOP), (SW, BOT), (P_, BOT))):
-        ts(A("sq", 128 * i, 128 * i + 128), io(128), c, AL.is_equal, m, AL.mult)
+    for i, base in enumerate((0, 1000, -8, 992)):
+        pick(A("sq", 128 * i, 128 * i + 128), [[-16, 8], [-1000, 2], [-1, 8]], base)
     ts(A("zbot"), io(160), GB16, AL.is_equal, BOT, AL.mult)
     ts(A("selc", 0, 128), io(128), T0, AL.is_equal, TOP, AL.mult)
     ts(A("selc", 128, 256), io(128), T1, AL.is_equal, TOP, AL.mult)
     ts(A("h2"), io(64), PH, AL.is_equal)
     iota(A("t1", 16, 64), [[0, 3], [16, 8], [0, 2]])
     ts(A("b48"), A("t1", 16, 64), GB, AL.is_equal)
-    cp(A("bp"), A("b48"))
-    ts(A("bp", 16, 32), A("b48", 16, 32), -1.0, AL.mult)
+    lin(A("bp"), A("b48"), 1.0)
+    lin(A("bp", 16, 32), A("b48", 16, 32), -1.0)
     for nm, c in (("bn", -1.0), ("bp2", 2.0), ("bn2", -2.0)):
-        ts(A(nm), A("bp"), c, AL.mult)
+        lin(A(nm), A("bp"), c)
     iota(A("ru"), [[0, 32]])
-    ts(A("ru", 1, 16, 2), A("b48", 1, 16, 2), TOP, AL.mult)
-    ts(A("ru", 16, 32, 2), A("b48", 0, 16, 2), BOT, AL.mult)
-    ts(A("rf", 0, 16), A("b48", 0, 16), TOP, AL.mult)
-    ts(A("rf", 16, 32), A("b48", 0, 16), BOT, AL.mult)
-    ts(A("rfd"), A("b48", 0, 16), SG, AL.mult)
-    ts(A("ro", 0, 16), A("b48", 0, 16), BOT, AL.mult)
-    ts(A("ro", 16, 32), A("b48", 0, 16), TOP, AL.mult)
+    lin(A("ru", 1, 16, 2), A("b48", 1, 16, 2), TOP)
+    lin(A("ru", 16, 32, 2), A("b48", 0, 16, 2), BOT)
+    lin(A("rf", 0, 16), A("b48", 0, 16), TOP)
+    lin(A("rf", 16, 32), A("b48", 0, 16), BOT)
+    lin(A("rfd"), A("b48", 0, 16), SG)
     iota(A("par"), [[0, 16], [1, 2], [0, 8]])
     ts(A("par"), A("par"), P1, AL.is_equal)
     iota(A("bias", 0, 256), [[-1, 2], [0, 128]])
-    ts(A("bias", 256, 384), A("par", 0, 128), -1.0, AL.add, 16384.0, AL.mult)
+    lin(A("bias", 256, 384), A("par", 0, 128), 16384.0, -16384.0)
     iota(A("zero"), [[0, 128]])
-    iota(A("ones"), [[0, 128]], 1)
-    iota(A("nones"), [[0, 256]], -1)
     iota(A("t2", 144, 208), [[1, 16], [256, 4]])
     iota(A("t2", 208, 256), [[1, 16], [256, 3]])
     ts(A("pil"), A("t2", 144, 256), P256, AL.add)
-    ts(A("t3", 0, 128), A("ones"), 1.0 / 3.0, AL.mult)
+    lin(A("t3", 0, 128), A("ones"), 1.0 / 3.0)
     scan(A("t3", 128, 256), A("t3", 0, 128), A("zero"), float(3.0 ** 62), AL.mult, AL.add)
     tt(A("t3", 0, 128), A("t3", 128, 256), A("iff"), AL.mult)
     op("V", lambda: vec.tensor_reduce(WC[0], A("t3", 0, 128)[0], AxisListType.X, AL.add), 200, [A("t3", 0, 128)], [WC])
-    ts(TC, WC, 2.2, AL.mult)
-    ts(A("cw"), A("ones", 0, 16), WC, AL.mult)
+    lin(TC, WC, 2.2)
+    lin(A("cw"), A("ones", 0, 16), WC)
     iota(A("r8"), [[16, 8], [0, 128]])
     ts(A("r8"), A("r8"), GB, AL.is_equal)
     iota(A("mask"), [[0, 129], [1, 8]])
     ts(A("mask"), A("mask"), P8, AL.is_equal)
     for k in range(8):
-        ts(A("rom", 32 * k, 32 * k + 32), A("ro"), A("mask", k, k + 1), AL.mult)
+        pick(A("rom", 32 * k, 32 * k + 32), [[8, 2], [-16, 8], [0, 2]], -8 - k)
     cp(A("p0"), A("stall"))
     iota(A("nb", V0, V), [[0, V - V0]], int(OFF))
     iota(A("wt"), [[0, WT]])
     dma("Y", [(A("wz"), A("wt"))], 2500)
 
     xw = A("xs")
+    SQ = lambda i: A("sq", 128 * i, 128 * i + 128)
 
     def nbg(i):
         ops[i]["rd"] += NBS
@@ -329,30 +346,50 @@ def build(g, core, T, topo):
         cs = lambda nm: A(nm, 128 * sd, 128 * sd + 128)
         ks = lambda nm, a=0, s=1: A(nm, 144 * sd + a, 144 * sd + 144, s)
         big = lambda nm, a, b, s=1: A(nm, 2048 * sd + a, 2048 * sd + b, s)
+        if sd:
+            ac(XV(t, sd), XV(t, sd), scale=-1.0)
         for s in range(16):
             gcopy(big("rep", s, 2048, 16), XV(t, sd))
         p = ST("p0", t, sd)
         tt(cs("yy"), IN(ST("stall", t, sd), A("bc", 0, 8)), A("mt"), AL.mult)
-        tt(cs("d0"), IN(A("xs", 0, V0), p), XV(t, sd), AL.subtract)
+        tt(cs("d0"), IN(A("xs", 0, V0), p), XV(t, sd), AL.add if sd else AL.subtract)
         ac(cs("d0"), cs("d0"), AF.Abs)
         for h in range(2):
             nbg(ts(cs("c16"), IN(nbw, p), -OFF, AL.add))
             nbg(ac(cs("cf"), IN(nbw, p)))
             one = A(kb, 145, 288, 18)
             grp([(A(kb, 144, 288), cs("cf"), A("dm"))] + ([(one, cs("yy"), A("b8")), (one, A("mt"), A("b64"))] if h == 0 else [(one, A("iff"), ks("ee", 17, 18))]))
-            for i in range(2):
-                x, lst = big("sc", 1024 * i, 1024 * i + 1024), IN(xw, A("c16", 128 * sd + 64 * i, 128 * sd + 64 * i + 64))
-                if eng[i] == "V":
-                    tt(x, lst, big("rep", 1024 * i, 1024 * i + 1024), AL.subtract)
-                    ac(x, x, AF.Abs)
-                else:
-                    ac(x, lst)
-                    for u, bank in enumerate((d0, d1)):
-                        a = 1024 * i + 512 * u
-                        mm(acc(A(bank), [(IB, big("sc", a, a + 512)), (A("ibn"), big("rep", a, a + 512))]))
-                        ac(big("sc", a, a + 512), A(bank), AF.Abs)
             stay = (A(kb, 0, 144, 18),) + ((cs("d0"), A("b64")) if h == 0 else (A("iff"), ks("s1", 17, 18)))
-            grp([(A(kb, 0, 144), IB, A("kb", 144 * h, 144 * h + 144)), stay] + [(A(kb, 1 + s, 144, 18), big("sc", s, 2048, 16), A("b64")) for s in range(16)])
+            grp([(A(kb, 0, 144), IB, A("kb", 144 * h, 144 * h + 144)), stay], stop=False)
+            way = [eng[(2 * h + i) % len(eng)] for i in range(2)]
+            halves = [[0], [1]] if (way[0] in "RE") != (way[1] in "RE") else [[0, 1]]
+            for hv in halves:
+                a, b, wait = 1024 * hv[0], 1024 * hv[-1] + 1024, []
+                sums = lambda w, stop: grp([(A(kb, 1 + s, 144, 18, p=slice(a // 16, b // 16)), big("sc", a + s, b, 16), A(w)) for s in range(16)], start=False, stop=stop)
+                for i in hv:
+                    x, lst = big("sc", 1024 * i, 1024 * i + 1024), IN(xw, A("c16", 128 * sd + 64 * i, 128 * sd + 64 * i + 64))
+                    if way[i] in "VR":
+                        tt(x, lst, big("rep", 1024 * i, 1024 * i + 1024), AL.add if sd else AL.subtract)
+                    else:
+                        ac(x, lst)
+                    if way[i] in "DE":
+                        fold_dma(x, big("rep", 1024 * i, 1024 * i + 1024))
+                        wait.append(folds[-1])
+                    if way[i] in "VD":
+                        ac(x, x, AF.Abs)
+                    elif way[i] == "S":
+                        for u, bank in enumerate((d0, d1)):
+                            c = 1024 * i + 512 * u
+                            mm(acc(A(bank), [(IB, big("sc", c, c + 512)), (IB if sd else A("ibn"), big("rep", c, c + 512))]))
+                            ac(big("sc", c, c + 512), A(bank), AF.Abs)
+                if way[hv[0]] in "RE":
+                    for j in wait:
+                        ops[j]["cons"] = len(ops)
+                    sums("b64n", False)
+                    ts(big("sc", a, b), big("sc", a, b), 0.0, AL.max)
+                    sums("b128", True)
+                else:
+                    sums("b64", True)
             scan(ks("s1"), A("rst"), A(kb, 0, 144), 0.0, AL.add, AL.min)
             tt(ks("nf"), ks("s1"), A(kb, 0, 144), AL.not_equal)
             scan(ks("ee"), A(kb, 144, 288), ks("nf"), 0.0, AL.add, AL.mult)
@@ -364,6 +401,7 @@ def build(g, core, T, topo):
 
     posf, posr, nbk = [0], [0], [0]
     chain = {"V": [], "S": []}
+    made = {"V": [], "S": []}
     for t in range(RO):
         old, have = V0 + M * t, V0 + M * (t + 1)
         nbw = A("nb", 0, old)
@@ -371,7 +409,18 @@ def build(g, core, T, topo):
         pf = search(t, 1, PAR["far"][t], Y0, Y1, KF)
         for o in ops[first:]:
             o["lead"] = PAR["flead"][t]
-        ac(A("ys"), IN(A("ya", 0, old), pf))
+        if PAR["early"][t]:
+            yw = A("yb", 0, old)
+            cp(A("xx", 128, 256), IN(nbw, pf))
+            mm([c for z in range(2) for c in acc(A(KF, 296 + 64 * z, 360 + 64 * z), [(SQ(2 * z + h), A("xx", 128 + h, 256, 2)) for h in range(2)])])
+            ts(A("c16", 128, 256), A(KF, 296, 424), -OFF, AL.add)
+            ac(A("ys"), IN(yw, pf))
+            ac(A("val"), IN(yw, A("c16", 192, 256)), scale=-0.125)
+            tt(A("val"), IN(yw, A("c16", 128, 192)), A("val"), AL.mult)
+            mm(acc(A(KF, 0, 128), [(A("iff"), A("ys"))] + [(A("iff"), A("val", k, 1024, 8)) for k in range(8)]))
+            ac(A("ys"), A(KF, 0, 128), bias=0.5, scale=0.5)
+        else:
+            ac(A("ys"), IN(A("ya", 0, old), pf))
         dst = T.cores[(rank - 1 - t) % n]
         rid, pid, _ = topo.addr(dst)
         sent[0] += len(topo.engines(core, dst))
@@ -382,7 +431,7 @@ def build(g, core, T, topo):
         bl = search(t, 0, PAR["own"][t], D0, D1, KO)
         iota(A("val"), [[1, 128], [0, 8]], old + int(OFF))
         VC = C(20 + t)
-        ts(VC, P_, old - OFF, AL.add)
+        lin(VC, P_, 1.0, old - OFF)
         ts(A("dv"), IB, VC, AL.mult, 1.0, AL.add)
         if t:
             dma("Y", [(A("wt"), A("wz"))], 2500)
@@ -421,8 +470,7 @@ def build(g, core, T, topo):
         far = PAR["gf"][t] == "S"
         fl, al = IN(xw, A("fa", 0, 64)), IN(xw, A("fa", 64, 128))
         grp([(A(KO, 0, 384), IB, A("bias"))] + (keys("xcq", 0, "bp") + [(A(KO, k, 384, 8), XV(t, 0), A("bn")) for k in range(8)] if far else []), stop=False)
-        tt(A("sc", 0, 1024), al, A("xcq"), AL.max)
-        tt(A("sc", 1024, 2048), al, r8v(0, 1024), AL.max)
+        tt(A("sc", 1024, 2048), al, r8v(0, 1024), AL.max, after=[tt(A("sc", 0, 1024), al, A("xcq"), AL.max)])
         if far:
             ac(A("ab"), fl)
             for o, sub in (("xcq", lambda u: A("xcq", 512 * u, 512 * u + 512)), ("ab", lambda u: r8v(512 * u, 512 * u + 512))):
@@ -457,11 +505,14 @@ def build(g, core, T, topo):
         tt(A("zz"), A("mw"), A(TT, 0, 256), AL.mult)
         mm(acc(A(D0, 128, 256), [(A("ones"), A("dv")), (A("zz", 0, 128), IB), (A("zz", 128, 256), IB)]))
         ts(A("thh"), A(D0, 128, 256), -OFF, AL.add)
-        SQ = lambda i: A("sq", 128 * i, 128 * i + 128)
         mm([c for z in range(2) for c in acc(A(D1, 64 * z, 64 * z + 64), [(SQ(2 * z + h), A("thh", h, 128, 2)) for h in range(2)])])
         ts(A("sl"), A(D1, 0, 128), SV, AL.add)
-        cp(IN(A("flat", 0, 8 * V), A("sl", 0, 64)), A("val"))
-        ac(IN(A("flat", 8 * V, 16 * V), A("sl", 64, 128)), A("val"), AF.Silu)
+        hold = dict((e, made[e][-PAR["hold"][t]:][:1] if PAR["hold"][t] else []) for e in "VS")
+        if PAR["nxs"][t] == "V":
+            ops[cp(IN(A("flat", 0, 8 * V), A("sl", 0, 64)), A("val"))]["after"] = hold["V"]
+        else:
+            ac(IN(A("flat", 0, 8 * V), A("sl", 0, 64)), A("val"), AF.Silu, after=hold["S"])
+        ac(IN(A("flat", 8 * V, 16 * V), A("sl", 64, 128)), A("val"), AF.Silu, after=hold["S"])
         nbg(mm(acc(A(D0, 256, 384), [(SQ(1), A("thh")), (SQ(2), A("thh"))])))
         ac(A("nb", old, have), A(D0, 256, 384), bias=OFF)
         W = (64, 48 if have == 1792 else 64)
@@ -472,13 +523,17 @@ def build(g, core, T, topo):
         for r in range(2):
             a, w, l = 1024 * r, W[r], (0 if W[r] == 64 else 64)
             ts(A("nbp", a, a + 16 * w), IN(A("nb", a, a + 16 * w), A("pil", l, l + w)), -OFF, AL.add)
-            for z in (1, 0):
-                dma(PAR["dq"][t][z], [(A("off", a + w * s, a + w * s + w), A("nbp", a, a + 16 * w, p=row(s))) for s in range(8 * z, 8 * z + 8)], 2300)
+            for z, ks in enumerate(((0,), (1, 2), (3, 4), (5, 6, 7)) if r == 0 else ((0, 1, 2, 3), (4, 5, 6, 7))):
+                dma(PAR["dq"][t][z % 2], [(A("off", a + w * s, a + w * s + w), A("nbp", a, a + 16 * w, p=row(s))) for k in ks for s in (8 + k, k)], 1900 + 250 * len(ks))
         OL = lambda s, a, b: A("off", (a - a % 1024) + W[a // 1024] * s + a % 1024 // 16, (a - a % 1024) + W[a // 1024] * s + (b - a + a % 1024) // 16)
         for o in ops[first:]:
             o["lead"] = PAR["lead"][t]
         if t + 1 == RO:
-            ac(A("nb"), A("nb"), bias=-OFF)
+            if "S" in PAR["nxs"]:
+                ts(A("nb"), A("nb"), MAGIC - OFF, AL.add, -MAGIC, AL.add)
+            else:
+                ac(A("nb"), A("nb"), bias=-OFF)
+            ops[-1]["lead"] = PAR["outl"]
             dma("Y", [(T.nx[k::8, :], A("nb", p=row(k))) for k in range(8)], 3000)
         nch = [0]
         for sw in range(2):
@@ -507,13 +562,19 @@ def build(g, core, T, topo):
                     pk = A(rn, o, o + w)
                     chain["S"] = [ac(pk, IN(yw, OL(8 + k, a, b)), after=chain["S"], scale=-0.125)]
                     chain["V"] = [tt(pk, IN(yw, OL(k, a, b)), pk, AL.mult, after=chain["V"])]
+                    made["S"] += chain["S"]
+                    made["V"] += chain["V"]
                     if k == 0 and -1 in fold:
                         fold_dma(pk, A(src, a, b))
                         terms = [(rn, o)]
                     elif k - 1 in fold:
                         fold_dma(A(rn, place[k - 1], place[k - 1] + w), pk)
                         terms.append((rn, place[k - 1]))
-                    elif k not in fold:
+                    elif k + 9 in fold:
+                        chain["V"] = [tt(pk, pk, A(rn, place[k - 1], place[k - 1] + w), AL.add, after=chain["V"])]
+                        if k + 10 not in fold:
+                            terms.append((rn, o))
+                    elif k not in fold and k + 10 not in fold:
                         terms.append((rn, o))
                     for i, (nm, c0) in enumerate(terms):
                         mm([(A(bk, 0, q - p), A("iff"), A(nm, c0 + p, c0 + q), k == 0 and i == 0, k == 7 and i == len(terms) - 1) for bk, p, q in parts])
@@ -530,7 +591,7 @@ def build(g, core, T, topo):
     return ops, sent[0]
 
 
-def schedule(ops):
+def schedule(ops, other):
     LAT = PAR["LAT"]
     hist = {}
     for i, o in enumerate(ops):
@@ -587,14 +648,140 @@ def schedule(ops):
             left[j] -= 1
             if not left[j]:
                 ready[ops[j]["eng"]].append(j)
-    return order
+    gap = lambda i, j: ops[i]["lat"] + (0.0 if ops[j]["eng"] == ops[i]["eng"] and (ops[i]["eng"] == "P" or i in ops[j]["soft"]) else LAT)
+    pre = [[(j, gap(j, i)) for j in o["deps"]] for i, o in enumerate(ops)]
+    post = [[(j, gap(i, j)) for j in succ[i]] for i in range(len(ops))]
+
+    def place(seq, before, tail):
+        busy = dict((e, ([], [])) for e in "VSPGYR")
+        end = [0.0] * len(ops)
+        for i in seq:
+            d = ops[i]["dur"]
+            t = max([end[j] + w for j, w in before[i]] + [ops[i]["lat"] if tail else 0.0])
+            st, en = busy[ops[i]["eng"]]
+            k = len(st)
+            while k and en[k - 1] > t:
+                k -= 1
+            while k < len(st) and st[k] < t + d:
+                t = max(t, en[k])
+                k += 1
+            st.insert(k, t)
+            en.insert(k, t + d)
+            end[i] = t + d
+        return end
+
+    def rank(key, before, behind):
+        wait = [len(b) for b in before]
+        top = list(key)
+        out = sorted((i for i in range(len(ops)) if not wait[i]), key=lambda i: key[i])
+        for i in out:
+            for j, _ in behind[i]:
+                top[j] = max(top[j], top[i])
+                wait[j] -= 1
+                if not wait[j]:
+                    out.append(j)
+        pos = dict((i, n) for n, i in enumerate(out))
+        return sorted(out, key=lambda i: (top[i], pos[i]))
+
+    def length(seq):
+        tot = 0.0
+        for dur, lat, xfer, wake in other:
+            free = dict((e, 0.0) for e in "VSPGYRD")
+            end = [0.0] * len(ops)
+            for i in seq:
+                e = ops[i]["eng"]
+                t = free[e]
+                for j, hard in link[i]:
+                    if end[j] + wake * hard > t:
+                        t = end[j] + wake * hard
+                free[e] = t = t + dur[i]
+                end[i] = t + lat[i]
+            tot += math.log(max(end))
+        return tot
+
+    link = [[(j, 1.0 if w > ops[j]["lat"] else 0.0) for j, w in b] for b in pre]
+    rnd = np.random.RandomState(PAR["seed"])
+    end = [o["t0"] + o["dur"] for o in ops]
+    best = None
+    for n in range(PAR["passes"]):
+        shake = PAR["shake"] * rnd.rand(len(ops)) * (rnd.rand(len(ops)) < PAR["share"]) if n > 1 else np.zeros(len(ops))
+        back = place(rank([float(s) - x for s, x in zip(shake, end)], post, pre), post, True)
+        end = place(rank([-x for x in back], pre, post), pre, False)
+        seq = sorted(range(len(ops)), key=lambda i: (end[i], i))
+        now = length(seq)
+        if best is None or now < best[0]:
+            best = (now, end, seq)
+        end = best[1]
+    seq = best[2]
+    eng = [o["eng"] for o in ops]
+
+    def run(seq, c, why=None):
+        dur, lat, _, wake = c
+        free = dict((e, 0.0) for e in "VSPGYR")
+        last = dict((e, -1) for e in "VSPGYR")
+        end = [0.0] * len(ops)
+        for i in seq:
+            e = eng[i]
+            t, w = free[e], last[e]
+            for j, hard in link[i]:
+                if end[j] + wake * hard >= t:
+                    t, w = end[j] + wake * hard, -2 - j
+            free[e] = t = t + dur[i]
+            end[i] = t + lat[i]
+            last[e] = i
+            if why is not None:
+                why[i] = w
+        return end
+
+    now = top = best[0]
+    keep = seq
+    for n in range(PAR["swaps"]):
+        if n % 8 == 0 or fresh:
+            why = {}
+            end = run(seq, other[rnd.randint(len(other))], why)
+            i, arcs = max(range(len(ops)), key=lambda i: end[i]), []
+            while why[i] != -1:
+                if why[i] >= 0:
+                    arcs.append((why[i], i))
+                i = why[i] if why[i] >= 0 else -2 - why[i]
+            pos = dict((i, k) for k, i in enumerate(seq))
+        fresh = False
+        a, b = arcs[rnd.randint(len(arcs))]
+        line = [i for i in seq[max(0, pos[a] - 40):pos[a] + 1] if eng[i] == eng[a]]
+        a = line[max(0, len(line) - 1 - int(rnd.choice((0, 0, 0, 1, 2, 4))))]
+        part = seq[pos[a]:pos[b] + 1]
+        up, first = {b}, {eng[b]: False}
+        for i in part[-2::-1]:
+            if first.get(eng[i]) or any(j in up for j in succ[i]):
+                up.add(i)
+                first[eng[i]] = True
+        if a in up:
+            continue
+        new = seq[:pos[a]] + [i for i in part if i in up] + [i for i in part if i not in up] + seq[pos[b] + 1:]
+        x = sum(math.log(max(run(new, c))) for c in other)
+        if x <= now + PAR["heat"] * (1.0 - n / PAR["swaps"]) * rnd.rand():
+            seq, now, fresh = new, x, True
+            if x < top:
+                top, keep = x, new
+    seq = keep
+    return dict((e, [i for i in seq if ops[i]["eng"] == e]) for e in order)
 
 
 def rank_program(g, core, T, topo):
     if T.rank_of(core) is None:
         return
-    ops, sent = build(g, core, T, topo)
-    order = schedule(ops)
+    ops, sent = build(g, core, T, topo, PAR)
+    other = []
+    for c in COSTS:
+        alt = build(g, core, T, topo, c)[0]
+        other.append(([o["dur"] for o in alt], [o["lat"] for o in alt], None, c["LAT"]))
+    key = repr(sorted(PAR.items()))
+    if key not in ORDER:
+        ORDER.clear()
+        ORDER[key] = (schedule(ops, other), [(o["deps"], o["soft"]) for o in ops])
+    order = ORDER[key][0]
+    for o, (d, s) in zip(ops, ORDER[key][1]):
+        o["deps"], o["soft"] = d, s
     total = {}
     for e in "VSPG":
         c = 0

@@ -9,50 +9,63 @@ V0, M, RO, V = 1664, 128, 3, 2048
 H = "float16"
 F, B, I, U = "float32", "bfloat16", "int32", "uint16"
 OFF = 64.0
-RING = 3824
+RING = 5120
 WT = 2368
 MAGIC = 12582912.0
 NF = 52
 PAR = dict(
-    cuts=((0, 512, 1024, 1536, 1792), (0, 512, 1024, 1536, 1792, 1920), (0, 512, 1024, 1536, 1792, 2048)),
-    dq=("YS", "YY", "YY"),
-    cutv=52,
-    fold=((-1, 1, 3, 5),) * 3,
-    foldl=(((), (-1, 1, 3)),) * 3,
-    nflat=(6, 6, 99),
-    lead=(0.0, 20000.0, 40000.0),
-    flead=(0.0, 0.0, 0.0),
-    ev=("S", "S", "VS"), evl=5000.0,
-    own=("VS", "VS", "VS"), far=("SV", "VV", "VV"),
-    gf=("S", "S", "S"),
-    nxs=("V", "S", "S"), outl=0.0,
+    plan=None,
+    nflat=(6, 6, 99), s0=8,
+    dq=("YY", "YY", "YS"),
+    cutv=88,
+    lead=(-20000.0, 20000.0, 20000.0),
+    flead=(-20000.0, 0.0, 30000.0),
+    direct=(0, 0, 0), head=(0,) * 6, holdw=(0, 0, 0), late=(1, 1, 1, 1, 1, 1),
+    evl=0.0,
+    both=(0, 1, 1),
+    own=("RS", "RE", "RE"), far=("ER", "EE", "ER"),
+    gf=("S", "V", "S"),
+    gg=("VV", "VV", "VV"),
     cs="S",
-    hold=(0, 1, 1),
-    passes=2, look=150.0,
-    CY=0.9, GA=1.55, SCA=3.8, PE=0.5, LAT=90.0, DL=1.0)
-PAR.update({'cuts': ((0, 512, 1024, 1536, 1792), (0, 512, 1024, 1536, 1920), (0, 512, 1024, 1536, 1920, 2048)), 'dq': ('YY', 'YY', 'YY'), 'cutv': 88, 'fold': ((0, 2, 4), (1, 3, 5), (1, 3, 5)), 'foldl': (((), (-1, 1, 3)), ((-1, 1), (0, 2, 4)), ((0, 2, 4, 6),)), 'nflat': (6, 6, 99), 'lead': (-20000.0, 20000.0, 10000.0), 'flead': (-20000.0, 5000.0, 0.0), 'ev': ('S', 'SSV', 'SSV'), 'evl': 0.0, 'own': ('VS', 'VS', 'VS'), 'far': ('SV', 'VV', 'VV'), 'gf': ('S', 'V', 'S'), 'look': 200.0, 'CY': 0.9, 'GA': 1.3, 'SCA': 3.8, 'PE': 0.5, 'LAT': 90.0, 'DL': 1.0})
-PAR.update(swaps=0, heat=0.002, early=(0, 0, 0), ysl=(0.0, 0.0, 0.0), seed=0, shake=1500.0, share=0.1)
-COSTS = (dict(CY=0.83, GA=1.55, SCA=3.8, PE=0.42, DL=1.0, LAT=80.0), dict(CY=0.95, GA=1.15, SCA=2.5, PE=0.55, DL=1.0, LAT=150.0),
-         dict(CY=0.9, GA=1.3, SCA=3.0, PE=0.47, DL=1.3, LAT=100.0), dict(CY=1.1, GA=1.8, SCA=5.0, PE=0.55, DL=1.1, LAT=100.0))
-PAR.update({'cuts': ((0, 512, 1024, 1536, 1792), (0, 512, 1024, 1536, 1920), (0, 512, 1024, 1536, 1792, 2048)), 'dq': ('YY', 'YY', 'YS'), 'cutv': 88, 'fold': ((0, 2, 4, 6), (0, 2, 4, 6), (0, 2, 4, 6)), 'foldl': (((0, 2),), ((0, 2),), ((10, 12, 14, 16),)), 'nflat': (6, 6, 99), 'lead': (-20000.0, 20000.0, 20000.0), 'flead': (-20000.0, 0.0, 30000.0), 'ev': ('S', 'S', 'S'), 'evl': 0.0, 'own': ('RS', 'RS', 'SR'), 'far': ('ER', 'EE', 'ER'), 'gf': ('S', 'V', 'S'), 'nxs': ('V', 'V', 'V'), 'outl': 0.0, 'cs': 'S', 'hold': (0, 4, 24), 'passes': 2, 'look': 200.0, 'CY': 0.83, 'GA': 1.55, 'SCA': 3.8, 'PE': 0.5, 'LAT': 60.0, 'DL': 1.4, 'swaps': 3000, 'heat': 0.0005})
+    hold=(0, 4, 24),
+    early=(0, 0, 0),
+    passes=2, look=200.0,
+    swaps=3000, heat=0.0005, seed=0, mean=0.2, local=0.5, starts=24, kept=3, first=2000, meet=(0, 0, 0), block=0.03, span=20000.0, slow=(0.0, 200.0, 400.0), nxs=(0, 0, 0), wrap=("VV", "VV", "VV"), haste=(0.0, 0.0, 0.0), shake=1500.0, share=0.1,
+    CY=0.83, GA=1.55, SCA=3.8, PE=0.5, LAT=60.0, DL=1.4)
+PAIRS, LAST = "Pp0p2p4p6S", "Pp0ppppppS"
+PAR["plan"] = (tuple(((512, PAIRS), (512, PAIRS), (512, PAIRS), (w, LAST)) for w in (256, 256, 384, 384))
+               + (((512, PAIRS), (512, PAIRS), (512, PAIRS), (256, PAIRS), (256, "PpApCpEpGS")),) * 2)
+E4 = "Pp0p2p4peV"
+PAR.update(inflat=((0, 0), (0, 0), (0, 99999)), hold=(0, 0, 33), lead=(0.0, 20000.0, 20000.0), flead=(-5000.0, 0.0, 0.0), early=(0, 1, 1), swaps=12000, gg=("VHH", "SSS", "SSS"), sm=("bd", "cbdnx", "cbdnx"),
+           direct=(1, 0, 0), head=(256, 0, 0, 0, 0, 0), passes=1, heat=0.0003,
+           plan=(((1024, PAIRS), (512, PAIRS), (256, LAST)), ((1024, PAIRS), (512, E4), (256, E4)), ((512, PAIRS), (512, PAIRS), (512, PAIRS), (384, LAST)),
+                 ((512, PAIRS), (512, PAIRS), (512, E4), (384, E4))) + (((512, E4),) * 4,) * 2)
+PAR.update(plan=(((1024, PAIRS), (768, E4)), ((1024, PAIRS), (512, E4), (256, E4)), ((1024, E4), (896, E4)), ((1024, E4), (512, E4), (384, E4))) + (((512, E4),) * 4,) * 2,
+           gf="SSS", own=("RS", "RE", "RE"), far=("SR", "EE", "EE"), dq=("YY",) * 3, cutv=88, sm=("bd", "bdnx", "bdnx"), inflat=((2048, 16384), (0, 17408), (0, 99999)),
+           hold=(0, 0, 0), LAT=100.0, DL=1.25, lead=(0.0, 3000.0, 3000.0), starts=30, kept=4, first=2000, swaps=25000, heat=0.0004)
+PAR.update(plan=(((1024, PAIRS), (768, E4)), ((1024, PAIRS), (768, E4))) + PAR["plan"][2:], inflat=((4096, 18432), (3072, 19456), (2048, 99999)),
+           gg=("VHH", "SHH", "SHH"), starts=24, kept=6, first=4000, swaps=25000, heat=0.0008, DL=1.1, block=0.0, seed=1, span=30000.0, lead=(0.0, 6000.0, 6000.0))
+COSTS = (dict(CY=0.83, GA=1.45, SCA=3.5, PE=0.42, DL=1.2, LAT=80.0, OV=65.0), dict(CY=0.95, GA=1.15, SCA=2.5, PE=0.5, DL=1.0, LAT=120.0, OV=60.0),
+         dict(CY=1.04, GA=1.5, SCA=3.5, PE=0.52, DL=1.5, LAT=80.0, OV=75.0), dict(CY=1.15, GA=1.85, SCA=5.0, PE=0.58, DL=1.0, LAT=100.0, OV=60.0))
 ORDER = {}
 SB = {
     "flat": (16 * V, F), "ring": (RING, F), "ya": (V, F), "yb": (V, F), "xs": (V, B), "nb": (V, F), "nbp": (V, U),
-    "off": (V, U), "val": (1024, F), "ni": (832, I), "wt": (WT, B), "sc": (4096, B), "rep": (4096, B), "ab": (1024, B),
-    "gg": (1024, H), "xcq": (1024, B), "eq": (1024, B), "r8": (1024, B), "mask": (1032, B),
+    "off": (V, U), "val": (1024, F), "ni": (832, I), "big": (8192, B), "mix": (4096, H), "r8": (1024, B),
     "xf": (384, B), "stall": (48, I), "p0": (48, U), "pr": (96, U), "ys": (128, F),
-    "pi": (8, I), "col": (28, F), "ib": (128, B), "ibn": (128, B), "i3": (128, B), "iff": (128, F), "zbot": (160, B),
-    "selc": (256, B), "sq": (512, B), "b48": (48, B), "bp": (48, B), "bn": (48, B), "bp2": (48, B), "bn2": (48, B),
-    "bias": (384, B), "ru": (32, B), "rf": (32, B), "rfd": (16, B), "rom": (256, B), "par": (256, B), "h2": (64, B),
-    "zero": (128, B), "ones": (128, B), "nones": (256, B), "dv": (128, H), "bc": (16, U), "pil": (112, U), "cw": (16, B),
-    "b8": (8, B), "b64": (8, B), "b64n": (8, B), "b128": (8, B), "kb": (288, B), "rst": (144, B), "dm": (144, F), "mt": (128, B), "negm": (128, B),
-    "d0": (256, B), "c16": (256, U), "cf": (256, F), "s1": (288, F), "nf": (288, B), "ee": (288, F), "xx": (256, H),
+    "pi": (8, I), "col": (28, F), "ib": (128, B), "ibn": (128, B), "i3": (128, B), "iff": (128, F), "ifh": (128, F), "zb": (1152, B), "lam": (128, B),
+    "selc": (256, B), "sq": (640, B), "m17": (16, B), "b48": (48, B), "bp": (48, B), "bn": (48, B), "bp2": (48, B), "bn2": (48, B),
+    "bias": (384, B), "rf": (256, B), "rfs": (256, B), "rom": (256, B), "par": (256, B), "h2": (64, B),
+    "zero": (128, B), "ones": (128, B), "nones": (512, B), "dv": (128, H), "bc": (32, U), "pil": (112, U), "cw": (16, B),
+    "b8": (8, B), "b64": (8, B), "b64n": (8, B), "b128": (8, B), "kb": (288, B), "rst": (288, B), "dm": (144, B), "mt": (256, B), "negm": (128, B),
+    "d0": (256, B), "c16": (256, U), "nf": (288, B), "xx": (256, H),
     "nbb": (128, H), "cq": (64, U), "fa": (128, U), "brep": (128, H), "nbrep": (128, H), "rl": (8, U),
     "dw": (256, B), "indp": (128, B), "fam": (256, H), "ot": (128, H), "o16": (64, U), "b16": (64, U), "wts": (128, B),
     "wrow": (128, B), "sl": (128, U), "thh": (128, H),
 }
-ALIAS = {"gw": ("xcq", 0, 1024), "iot": ("yb", 0, 256), "t1": ("yb", 256, 256), "t2": ("yb", 512, 256), "t3": ("yb", 768, 256),
-         "yy": ("xx", 0, 256), "nfx": ("thh", 0, 128), "rlx": ("ot", 0, 128), "mw": ("dw", 0, 256), "zz": ("fam", 0, 256)}
+ALIAS = {"gw": ("big", 0, 1024), "ab": ("mix", 0, 1024), "xcq": ("mix", 1024, 1024), "gg": ("mix", 2048, 1024), "eq": ("mix", 3072, 1024), "iot": ("yb", 0, 256), "t1": ("yb", 256, 256), "t2": ("yb", 512, 256), "t3": ("yb", 768, 256),
+         "yy": ("xx", 0, 256), "nfx": ("thh", 0, 128), "rlx": ("ot", 0, 128), "mw": ("dw", 0, 256), "zz": ("fam", 0, 256),
+         "t4": ("yb", 1024, 256), "cf": ("fam", 0, 256), "s1": ("val", 256, 288), "ee": ("val", 544, 288),
+         "sc": ("big", 0, 2048), "rep": ("big", 2048, 2048), "wt": ("big", 4096, WT)}
 SCRATCH = dict((k, ("sbuf", [128, n], d)) for k, (n, d) in SB.items())
 SCRATCH["wz"] = ("dram", [128, WT], B)
 for _b in range(8):
@@ -87,6 +100,7 @@ def build(g, core, T, topo, costs):
     nsem = [0]
     vec, act, pe = g.vector, g.scalar, g.tensor
     CY, GA, SCA, PE, DL = [costs[k] for k in ("CY", "GA", "SCA", "PE", "DL")]
+    OV = costs.get("OV", 55.0)
 
     def A(name, a=0, b=None, s=1, p=None):
         if name in ALIAS:
@@ -110,10 +124,10 @@ def build(g, core, T, topo, costs):
 
     def cost(out, a, per):
         if len(out) > 5:
-            return 50 + 16 * out[5][4] * SCA * CY
+            return OV + 16 * out[5][4] * SCA * CY
         if len(a) > 5:
-            return 55 + out[4] * GA * CY
-        return 45 + max(64, out[4] * per) * CY
+            return OV + out[4] * GA * CY
+        return OV + max(64, out[4] * per) * CY
 
     def ap(x):
         return x[0] if isinstance(x, tuple) else x
@@ -172,7 +186,7 @@ def build(g, core, T, topo, costs):
         a = A("ones", 0, out[4])
         return op("G", lambda: g.affine_select(out[0], a[0], pat, AL.is_equal, 0.0, base, 1), 190 + 2 * out[4] * CY, [a], [out])
 
-    def dma(eng, pairs, lat, xfer=200.0, **k):
+    def dma(eng, pairs, lat, xfer=100.0, **k):
         sem = T.sem["d%d" % nsem[0]]
         nsem[0] += 1
         q = {"G": g, "Y": g.sync, "S": act}[eng]
@@ -190,20 +204,22 @@ def build(g, core, T, topo, costs):
     def fold_dma(out, a):
         i = len(folds)
         sem = T.sem["f%d" % (i % NF)]
+        x = (100 + (0.85 if two(out) else 1.7) * out[4]) * DL
         op("G", lambda: g.dma_start(out[0], a[0], accum_op=AL.add).then_inc(sem, 16), 900 * DL, [a, out], [out], kind="d",
-           lat=(1800 + 1.7 * out[4]) * DL, sem=sem, cnt=16 * (i // NF + 1))
-        ops[-1].update(xfer=(240 + (0.85 if two(out) else 1.7) * out[4]) * DL * DL, key="f%d" % (i % NF), cons=len(ops), hard=[ops[folds[i - NF]]["cons"]] if i >= NF else [])
+           lat=1700 * DL + x, sem=sem, cnt=16 * (i // NF + 1))
+        ops[-1].update(xfer=x, key="f%d" % (i % NF), fold=folds[i - NF] if i >= NF else -1)
         folds.append(len(ops) - 1)
 
     sent = [0]
 
     def arrive(name, cnt, reg, after):
-        return op("R", None, 0.0, [], [reg], kind="r", lat=2000.0 * DL, sem=T.sem[name], cnt=cnt, after=[after])
+        return op("R", None, 0.0, [], [reg], kind="r", lat=1000.0 * DL, sem=T.sem[name], cnt=cnt, after=[after])
 
     def row(s):
         return slice(s, 128, 16)
 
-    Y0, Y1, Y2, D0, D1, KO, KF, TT = ["ps%d" % i for i in range(8)]
+    Y0, Y1, Y2, Y3, D0, D1, KO, KF = ["ps%d" % i for i in range(8)]
+    TT = KF
     IB = A("ib")
     XV = lambda t, sd: A("xf", M * t, M * t + M) if sd else A("xs", V0 + M * t, V0 + M * t + M)
     ST = lambda nm, t, sd: A(nm, 16 * t + 8 * sd, 16 * t + 8 * sd + 8)
@@ -213,23 +229,32 @@ def build(g, core, T, topo, costs):
     dma("Y", [(A("ni", 104 * k, 104 * k + 104), T.nx0[k::8, :]) for k in (5, 1, 2, 3, 6, 7)], 3600)
     dma("Y", [(ST("stall", t, 0), T.st[:, 8 * t:8 * t + 8]) for t in range(RO)], 2300)
     dma("Y", [(A("xs"), T.x[:])], 3000)
-    early = [iota(A("pi", 0, 1), [[0, 1]], 0, 1), iota(A("iot"), [[1, 256]])]
+    early = [iota(A("col", 0, 1), [[0, 1]], 0, 1), iota(A("pi", 0, 1), [[0, 1]], 0, 1), iota(A("iot"), [[1, 256]])]
+    silu = ac(A("col", 17, 18), A("col", 0, 1), AF.Silu, extra=1400.0, scale=2.0, bias=V + OFF)
+    ops[-1]["lead"] = 90000.0
     for h in range(2):
         ops[iota(A("ring", 832 * h, 832 * h + 832), [[1, 52], [104, 16]], int(OFF) + 52 * h)]["after"] = early
-    for a, b in ((4, 5), (0, 1), (1, 4), (5, 8)):
-        cp(A("nbp", 104 * a, 104 * b), A("ni", 104 * a, 104 * b))
+    for a, b in ((4, 5), (0, 1)):
+        ops[cp(A("nbp", 104 * a, 104 * b), A("ni", 104 * a, 104 * b))]["lead"] = 60000.0
     cv = PAR["cutv"]
     for k in range(8):
         for a, b in (((0, 52), (52, 104)) if k % 4 == 0 else ((0, cv), (cv, 104)) if k == 3 and cv < 104 else ((0, 104),)):
+            if (k, a) == (0, 52):
+                piece = len(ops) - 1
+                for c, d in ((5, 8), (1, 4)):
+                    ops[cp(A("nbp", 104 * c, 104 * d), A("ni", 104 * c, 104 * d))]["after"] = [piece]
             w = IN(A("flat", (8 + k) * V, (8 + k) * V + V0), A("nbp", 104 * k + a, 104 * k + b))
             if k < 3 or (k, a) == (3, 0):
-                cp(w, A("ring", 16 * a, 16 * b))
+                ops[cp(w, A("ring", 16 * a, 16 * b))]["lead"] = 40000.0 if k == 0 else 0.0
             else:
-                ac(w, A("ring", 16 * a, 16 * b), AF.Silu, extra=1400.0 if (k, a) == (4, 0) else 0.0)
-        dma("Y", [(A("nb", 0, V0, p=row(8 + k)), A("flat", (8 + k) * V, (8 + k) * V + V0, p=row(8 + k)))], 2300)
+                j = ac(w, A("ring", 16 * a, 16 * b), AF.Silu, after=[silu])
+                silu = j if k == 4 else silu
+        dma("Y", [(A("nb", 0, V0, p=row(8 + k)), A("flat", (8 + k) * V, (8 + k) * V + V0, p=row(k)))], 2500, 400.0)
         ops[-1]["wr"] = [("nb%d" % (8 + k), 0, 1)]
-    ts(A("ring", 2048, 2048 + 832), A("ni"), OFF, AL.add)
-    ops[-1]["lead"] = 30000.0
+        if k == 0:
+            after = len(ops) - 2
+    cp(A("ring", 2048, 2048 + 832), A("ni"))
+    ops[-1].update(lead=30000.0, after=[after])
     dma("Y", [(A("nb", 0, V0, p=row(k)), A("ring", 2048 + 104 * k, 2152 + 104 * k)) for k in range(8)], 2500)
     ops[-1]["wr"] = [("nb0", 0, 1)]
     dma("Y", [(A("flat", k * V, k * V + V0, p=row(k)), A("ring", 2048 + 104 * k, 2152 + 104 * k)) for k in range(8)], 2500)
@@ -251,49 +276,59 @@ def build(g, core, T, topo, costs):
     def C(i):
         return A("col", i, i + 1)
     P_, P16, P8, GB, P1, PH, T0, TOP, BOT, FST, GB16, T1, SV, P256, WC, TC, SW, JC, G18, SG = [C(i) for i in range(20)]
-    for i, (c, o) in enumerate(((15, AL.bitwise_and), (7, AL.bitwise_and), (112, AL.bitwise_and), (1, AL.bitwise_and), (1, AL.arith_shift_right))):
+    for i, (c, o) in enumerate(((15, AL.bitwise_and), (3, AL.bitwise_and), (112, AL.bitwise_and), (1, AL.bitwise_and), (1, AL.arith_shift_right))):
         ts(A("pi", i + 1, i + 2), A("pi", 0, 1), c, o)
-    cp(A("col", 0, 6), A("pi", 0, 6))
+    cp(A("col", 1, 6), A("pi", 1, 6))
     ts(TOP, P16, 8.0, AL.is_lt)
     ts(BOT, P16, 8.0, AL.is_ge)
     ts(FST, P16, 0.0, AL.is_equal)
-    lin(GB16, GB, 1.0, 16.0)
+    TOFF, NOFF, BOFF = C(23), C(24), C(25)
+    lin(TOFF, TOP, OFF)
+    lin(NOFF, BOT, -OFF)
+    lin(BOFF, BOT, OFF)
     lin(SW, FST, 8.0, P_)
     lin(T0, SW, 1.0, -1.0)
     lin(T1, SW, 1.0, 7.0)
     lin(SV, P8, float(V))
     lin(P256, P16, 16.0)
-    lin(JC, P_, 2.0, V + OFF)
+    lin(GB16, P_, 1.0, V0 + M)
     lin(G18, GB, 0.125, P_)
     lin(SG, TOP, 2.0, -1.0)
     io = lambda w, a=0: A("iot", a, a + w)
     iota(A("ones"), [[0, 128]], 1)
-    iota(A("nones"), [[0, 256]], -1)
+    iota(A("nones"), [[0, 512]], -1)
+    lin(A("lam"), A("ones"), -0.5)
     ts(IB, io(128), P_, AL.is_equal)
     lin(A("ibn"), IB, -1.0)
     lin(A("i3"), IB, 3.0)
     lin(A("iff"), IB, 1.0)
+    lin(A("ifh"), IB, 0.5)
     iota(A("t1", 0, 8), [[16, 8]])
     ts(A("b8"), A("t1", 0, 8), GB, AL.is_equal)
     for nm, c in (("b64", 64.0), ("b64n", -64.0), ("b128", 128.0)):
         lin(A(nm), A("b8"), c)
-    iota(A("t1", 128, 256), [[0, 8], [1, 16]])
-    ts(A("mt"), A("t1", 128, 256), P16, AL.is_equal)
-    lin(A("negm"), A("mt"), 2.0 ** 98, -2.0 ** 98)
-    cp(A("bc", 0, 8), io(8))
-    ts(A("bc", 8, 16), io(8), 18.0, AL.mult, 17.0, AL.add)
-    for h in range(2):
-        iota(A("kb", 144 * h, 144 * h + 144), [[0, 8], [1, 18]])
-        iota(A("kb", 144 * h + 17, 144 * h + 144, 18), [[0, 8]], 1 << 20)
-    iota(A("kb", 144, 288, 18), [[0, 8]], -17)
-    iota(A("rst"), [[0, 144]])
-    iota(A("rst", 0, 144, 18), [[0, 8]], 1 << 23)
+    iota(A("t4"), [[0, 16], [1, 16]])
+    ts(A("mt"), A("t4"), P16, AL.is_equal)
+    MT = A("mt", 0, 128)
+    lin(A("negm"), MT, 2.0 ** 98, -2.0 ** 98)
+    cp(A("bc", 0, 16), io(16))
+    ts(A("bc", 16, 32), io(16), 18.0, AL.mult, 17.0, AL.add)
+    iota(A("kb"), [[0, 16], [1, 18]])
+    iota(A("kb", 17, 288, 18), [[0, 16]], 1 << 20)
+    iota(A("m17"), [[0, 16]], -17)
+    iota(A("rst"), [[0, 288]])
+    iota(A("rst", 0, 288, 18), [[0, 16]], 1 << 23)
     ts(A("t2", 0, 144), io(144), -2.0, AL.add, G18, AL.is_equal)
     ts(A("dm"), io(144), -1.0, AL.add, G18, AL.is_equal)
     tt(A("dm"), A("t2", 0, 144), A("dm"), AL.subtract)
-    for i, base in enumerate((0, 1000, -8, 992)):
-        pick(A("sq", 128 * i, 128 * i + 128), [[-16, 8], [-1000, 2], [-1, 8]], base)
-    ts(A("zbot"), io(160), GB16, AL.is_equal, BOT, AL.mult)
+    iota(A("sq"), [[0, 640]])
+    for q in range(4):
+        pick(A("sq", 160 * q + 16 + 4 * q, 160 * q + 144 + 4 * q), [[-16, 8], [-1000, 4], [-1, 4]], -4 * q)
+    iota(A("zb"), [[0, 1152]])
+    pick(A("zb", 0, 1152, 16), [[-1, 8], [-16, 9]], 8)
+    for e in range(2):
+        pick(A("rf", e, 256, 2), [[-1, 8], [-8, 2], [-16, 8]], 0)
+    lin(A("rfs"), A("rf"), SG)
     ts(A("selc", 0, 128), io(128), T0, AL.is_equal, TOP, AL.mult)
     ts(A("selc", 128, 256), io(128), T1, AL.is_equal, TOP, AL.mult)
     ts(A("h2"), io(64), PH, AL.is_equal)
@@ -303,12 +338,6 @@ def build(g, core, T, topo, costs):
     lin(A("bp", 16, 32), A("b48", 16, 32), -1.0)
     for nm, c in (("bn", -1.0), ("bp2", 2.0), ("bn2", -2.0)):
         lin(A(nm), A("bp"), c)
-    iota(A("ru"), [[0, 32]])
-    lin(A("ru", 1, 16, 2), A("b48", 1, 16, 2), TOP)
-    lin(A("ru", 16, 32, 2), A("b48", 0, 16, 2), BOT)
-    lin(A("rf", 0, 16), A("b48", 0, 16), TOP)
-    lin(A("rf", 16, 32), A("b48", 0, 16), BOT)
-    lin(A("rfd"), A("b48", 0, 16), SG)
     iota(A("par"), [[0, 16], [1, 2], [0, 8]])
     ts(A("par"), A("par"), P1, AL.is_equal)
     iota(A("bias", 0, 256), [[-1, 2], [0, 128]])
@@ -325,131 +354,144 @@ def build(g, core, T, topo, costs):
     lin(A("cw"), A("ones", 0, 16), WC)
     iota(A("r8"), [[16, 8], [0, 128]])
     ts(A("r8"), A("r8"), GB, AL.is_equal)
-    iota(A("mask"), [[0, 129], [1, 8]])
-    ts(A("mask"), A("mask"), P8, AL.is_equal)
     for k in range(8):
         pick(A("rom", 32 * k, 32 * k + 32), [[8, 2], [-16, 8], [0, 2]], -8 - k)
     cp(A("p0"), A("stall"))
     iota(A("nb", V0, V), [[0, V - V0]], int(OFF))
-    iota(A("wt"), [[0, WT]])
+    op("V", lambda: vec.memset(A("wt")[0], 0.0), 45 + WT * 0.5 * CY, [], [A("wt")])
+    ops[-1]["lead"] = 90000.0
     dma("Y", [(A("wz"), A("wt"))], 2500)
 
     xw = A("xs")
-    SQ = lambda i: A("sq", 128 * i, 128 * i + 128)
+    SQ = lambda q, h: A("sq", 160 * q + 16 + 4 * q - 4 * h, 160 * q + 144 + 4 * q - 4 * h)
 
     def nbg(i):
         ops[i]["rd"] += NBS
         return i
 
-    def search(t, sd, eng, d0, d1, kb):
+    def search(t, sds, d0, d1, kb, ki):
         nbw = A("nb", 0, V0 + M * t)
-        cs = lambda nm: A(nm, 128 * sd, 128 * sd + 128)
-        ks = lambda nm, a=0, s=1: A(nm, 144 * sd + a, 144 * sd + 144, s)
-        big = lambda nm, a, b, s=1: A(nm, 2048 * sd + a, 2048 * sd + b, s)
-        if sd:
-            ac(XV(t, sd), XV(t, sd), scale=-1.0)
-        for s in range(16):
-            gcopy(big("rep", s, 2048, 16), XV(t, sd))
-        p = ST("p0", t, sd)
-        tt(cs("yy"), IN(ST("stall", t, sd), A("bc", 0, 8)), A("mt"), AL.mult)
-        tt(cs("d0"), IN(A("xs", 0, V0), p), XV(t, sd), AL.add if sd else AL.subtract)
+        lo, m = sds[0], len(sds)
+        io = 144 if m == 1 else 0
+        cs = lambda nm, sd=None: A(nm, 128 * lo, 128 * (lo + m)) if sd is None else A(nm, 128 * sd, 128 * sd + 128)
+        ks = lambda nm, a=0, s=1, sd=None: A(nm, 144 * lo + a, 144 * (lo + m), s) if sd is None else A(nm, 144 * sd + a, 144 * sd + 144, s)
+        big = lambda nm, sd, a, b, s=1: A("big", 4096 * sd + 2048 * (nm == "rep") + a, 4096 * sd + 2048 * (nm == "rep") + b, s)
+        for sd in sds:
+            for s in range(16):
+                gcopy(big("rep", sd, s, 2048, 16), XV(t, sd))
+            tt(cs("d0", sd), IN(A("xs", 0, V0), ST("p0", t, sd)), XV(t, sd), AL.subtract)
         ac(cs("d0"), cs("d0"), AF.Abs)
+        p = A("p0", 16 * t + 8 * lo, 16 * t + 8 * (lo + m))
+        tt(cs("yy"), IN(A("stall", 16 * t + 8 * lo, 16 * t + 8 * (lo + m)), A("bc", 0, 8 * m)), A("mt", 0, 128 * m), AL.mult)
         for h in range(2):
-            nbg(ts(cs("c16"), IN(nbw, p), -OFF, AL.add))
-            nbg(ac(cs("cf"), IN(nbw, p)))
-            one = A(kb, 145, 288, 18)
-            grp([(A(kb, 144, 288), cs("cf"), A("dm"))] + ([(one, cs("yy"), A("b8")), (one, A("mt"), A("b64"))] if h == 0 else [(one, A("iff"), ks("ee", 17, 18))]))
-            stay = (A(kb, 0, 144, 18),) + ((cs("d0"), A("b64")) if h == 0 else (A("iff"), ks("s1", 17, 18)))
-            grp([(A(kb, 0, 144), IB, A("kb", 144 * h, 144 * h + 144)), stay], stop=False)
-            way = [eng[(2 * h + i) % len(eng)] for i in range(2)]
-            halves = [[0], [1]] if (way[0] in "RE") != (way[1] in "RE") else [[0, 1]]
-            for hv in halves:
-                a, b, wait = 1024 * hv[0], 1024 * hv[-1] + 1024, []
-                sums = lambda w, stop: grp([(A(kb, 1 + s, 144, 18, p=slice(a // 16, b // 16)), big("sc", a + s, b, 16), A(w)) for s in range(16)], start=False, stop=stop)
-                for i in hv:
-                    x, lst = big("sc", 1024 * i, 1024 * i + 1024), IN(xw, A("c16", 128 * sd + 64 * i, 128 * sd + 64 * i + 64))
-                    if way[i] in "VR":
-                        tt(x, lst, big("rep", 1024 * i, 1024 * i + 1024), AL.add if sd else AL.subtract)
-                    else:
-                        ac(x, lst)
-                    if way[i] in "DE":
-                        fold_dma(x, big("rep", 1024 * i, 1024 * i + 1024))
-                        wait.append(folds[-1])
-                    if way[i] in "VD":
-                        ac(x, x, AF.Abs)
-                    elif way[i] == "S":
-                        for u, bank in enumerate((d0, d1)):
-                            c = 1024 * i + 512 * u
-                            mm(acc(A(bank), [(IB, big("sc", c, c + 512)), (IB if sd else A("ibn"), big("rep", c, c + 512))]))
-                            ac(big("sc", c, c + 512), A(bank), AF.Abs)
-                if way[hv[0]] in "RE":
-                    for j in wait:
-                        ops[j]["cons"] = len(ops)
-                    sums("b64n", False)
-                    ts(big("sc", a, b), big("sc", a, b), 0.0, AL.max)
-                    sums("b128", True)
-                else:
-                    sums("b64", True)
-            scan(ks("s1"), A("rst"), A(kb, 0, 144), 0.0, AL.add, AL.min)
-            tt(ks("nf"), ks("s1"), A(kb, 0, 144), AL.not_equal)
-            scan(ks("ee"), A(kb, 144, 288), ks("nf"), 0.0, AL.add, AL.mult)
-            tt(cs("xx"), IN(ks("ee"), A("bc", 8, 16)), A("mt"), AL.mult)
-            mm([(A(kb, 288, 296), cs("xx"), A("b8"), True, True)])
-            p = A("pr", 32 * t + 16 * sd + 8 * h, 32 * t + 16 * sd + 8 * h + 8)
-            ts(p, A(kb, 288, 296), -OFF, AL.add)
-        return p
+            if "c" in PAR["sm"][t]:
+                nbg(ac(cs("cf"), IN(nbw, p), bias=TOFF))
+                ts(cs("c16"), cs("cf"), -OFF, AL.add)
+            elif "C" in PAR["sm"][t]:
+                nbg(ts(cs("cf"), IN(nbw, p), TOFF, AL.add))
+                ts(cs("c16"), cs("cf"), -OFF, AL.add)
+            else:
+                nbg(ts(cs("c16"), IN(nbw, p), NOFF, AL.add))
+                nbg(ac(cs("cf"), IN(nbw, p), bias=TOFF))
+            for i, sd in enumerate(sds):
+                one = A(ki, io + 144 * i + 1, io + 144 * i + 144, 18)
+                grp([(A(ki, io + 144 * i, io + 144 * i + 144), cs("cf", sd), A("dm"))]
+                    + ([(one, cs("yy", sd), A("b8")), (one, MT, A("b64"))] if h == 0 else [(one, A("iff"), ks("ee", 17, 18, sd))]))
+            stay = [(A(kb, 144 * i, 144 * i + 144, 18), cs("d0", sd), A("b64")) for i, sd in enumerate(sds)] if h == 0 else [(A(kb, 0, 144 * m, 18), A("iff"), ks("s1", 17, 18)), (A(kb, 0, 144 * m, 18), IB, A("m17", 0, 8 * m))]
+            grp([(A(kb, 0, 144 * m), IB, A("kb", 0, 144 * m))] + stay, stop=False)
+            last = []
+            for n, sd in enumerate(sds):
+                eng = PAR["far" if sd else "own"][t]
+                way = [eng[(2 * h + i) % len(eng)] for i in range(2)]
+                for hv in [[0], [1]] if (way[0] in "RE") != (way[1] in "RE") else [[0, 1]]:
+                    a, b = 1024 * hv[0], 1024 * hv[-1] + 1024
+                    sums = lambda w, stop, a=a, b=b, n=n, sd=sd: grp([(A(kb, 144 * n + 1 + s, 144 * n + 144, 18, p=slice(a // 16, b // 16)),
+                                                                       A("mix", 2048 * sd + a + s, 2048 * sd + b, 16) if w == "b128" and not lo else big("sc", sd, a + s, b, 16), A(w))
+                                                                      for s in range(16)], start=False, stop=stop)
+                    for i in hv:
+                        x, lst = big("sc", sd, 1024 * i, 1024 * i + 1024), IN(xw, A("c16", 128 * sd + 64 * i, 128 * sd + 64 * i + 64))
+                        if way[i] in "VR":
+                            tt(x, lst, big("rep", sd, 1024 * i, 1024 * i + 1024), AL.subtract)
+                        else:
+                            ac(x, lst, scale=-1.0)
+                        if way[i] in "DE":
+                            fold_dma(x, big("rep", sd, 1024 * i, 1024 * i + 1024))
+                        if way[i] in "VD":
+                            ac(x, x, AF.Abs)
+                        elif way[i] == "S":
+                            for u, bank in enumerate((d0, d1)):
+                                c = 1024 * i + 512 * u
+                                mm(acc(A(bank), [(IB, big("sc", sd, c, c + 512)), (IB, big("rep", sd, c, c + 512))]))
+                                ac(big("sc", sd, c, c + 512), A(bank), AF.Abs)
+                    if way[hv[0]] in "RE":
+                        sums("b64n", False)
+                        for u, v in ((a, b),) if way[hv[0]] == way[hv[-1]] else ((a, a + 1024), (a + 1024, b)):
+                            ts(big("sc", sd, u, v) if lo else A("mix", 2048 * sd + u, 2048 * sd + v), big("sc", sd, u, v), 0.0, AL.max)
+                    last.append((sums, "b128" if way[hv[0]] in "RE" else "b64", n == m - 1))
+            for sums, w, stop in last:
+                sums(w, stop)
+            scan(ks("s1"), A("rst", 0, 144 * m), A(kb, 0, 144 * m), 0.0, AL.add, AL.min)
+            tt(ks("nf"), ks("s1"), A(kb, 0, 144 * m), AL.not_equal)
+            scan(ks("ee"), A(ki, io, io + 144 * m), ks("nf"), 0.0, AL.add, AL.mult)
+            tt(cs("xx"), IN(ks("ee"), A("bc", 16, 16 + 8 * m)), A("mt", 0, 128 * m), AL.mult)
+            mm([(A(kb, 288 + 8 * i, 296 + 8 * i), cs("xx", sd), A("b8"), True, True) for i, sd in enumerate(sds)])
+            p = A("pr", 32 * t + 16 * h + 8 * lo, 32 * t + 16 * h + 8 * (lo + m))
+            ts(p, A(kb, 288, 288 + 8 * m), -OFF, AL.add)
 
-    posf, posr, nbk = [0], [0], [0]
+    def shift(e, out, a, m, c):
+        return ac(out, a, scale=m, bias=c) if e else ts(out, a, m, AL.mult, c, AL.add)
+
+    def nbrs(out, win, lst, e, off):
+        for x, a, b in (("V", 0, 512), ("S", 512, 1024)) if e == "H" else ((e, 0, 1024),):
+            shift(x == "S", A(out, a, b), IN(win, A(lst, a // 16, b // 16)), 1.0, off)
+
+    posf, posr = [PAR["s0"] * V], [0]
     chain = {"V": [], "S": []}
-    made = {"V": [], "S": []}
+    made, mid = {"V": [], "S": []}, [0]
     for t in range(RO):
         old, have = V0 + M * t, V0 + M * (t + 1)
         nbw = A("nb", 0, old)
         first = len(ops)
-        pf = search(t, 1, PAR["far"][t], Y0, Y1, KF)
-        for o in ops[first:]:
-            o["lead"] = PAR["flead"][t]
-        if PAR["early"][t]:
-            yw = A("yb", 0, old)
-            cp(A("xx", 128, 256), IN(nbw, pf))
-            mm([c for z in range(2) for c in acc(A(KF, 296 + 64 * z, 360 + 64 * z), [(SQ(2 * z + h), A("xx", 128 + h, 256, 2)) for h in range(2)])])
-            ts(A("c16", 128, 256), A(KF, 296, 424), -OFF, AL.add)
-            ac(A("ys"), IN(yw, pf))
-            ac(A("val"), IN(yw, A("c16", 192, 256)), scale=-0.125)
-            tt(A("val"), IN(yw, A("c16", 128, 192)), A("val"), AL.mult)
-            mm(acc(A(KF, 0, 128), [(A("iff"), A("ys"))] + [(A("iff"), A("val", k, 1024, 8)) for k in range(8)]))
-            ac(A("ys"), A(KF, 0, 128), bias=0.5, scale=0.5)
+        bl, pf = [A("pr", 32 * t + 16 + 8 * sd, 32 * t + 24 + 8 * sd) for sd in range(2)]
+        if PAR["both"][t]:
+            search(t, (0, 1), D0, D1, KO, KF)
         else:
-            ac(A("ys"), IN(A("ya", 0, old), pf))
-        dst = T.cores[(rank - 1 - t) % n]
-        rid, pid, _ = topo.addr(dst)
-        sent[0] += len(topo.engines(core, dst))
-        s = op("G", (lambda a=A("ya", old, have)[0], rid=rid, pid=pid, m=topo.mask(core, dst), t=t:
-                     g.remote_dma(a, A("ys")[0], T.sem["ay%d" % t], T.sem.sent, pid, rid, m)), 1500, [A("ys")], [], kind="x", sem=T.sem.sent, cnt=sent[0], lat=2500.0)
-        arrive("ay%d" % t, len(topo.engines(T.cores[(rank + 1 + t) % n], core)), A("ya", old, have), s)
-        first = len(ops)
-        bl = search(t, 0, PAR["own"][t], D0, D1, KO)
-        iota(A("val"), [[1, 128], [0, 8]], old + int(OFF))
+            search(t, (1,), Y0, Y1, KF if t else Y3, KF if t else Y3)
+            for o in ops[first:]:
+                o["lead"] = PAR["flead"][t]
+            first = len(ops)
+        if PAR["early"][t]:
+            shift("x" in PAR["sm"][t], A("xx", 128, 256), IN(nbw, pf), 1.0, TOFF)
+            mm([c for z in range(2) for c in acc(A(KF, 296 + 64 * z, 360 + 64 * z), [(SQ(2 * z + u, 2 * h + u), A("xx", 128 + h, 256, 2)) for h in range(2) for u in range(2)])])
+            ts(A("c16", 128, 256), A(KF, 296, 424), -OFF, AL.add)
+        if not PAR["both"][t]:
+            search(t, (0,), D0, D1, KO, KO)
+        iota(A("val", 0, 512), [[1, 128], [0, 4]], old + int(OFF))
         VC = C(20 + t)
         lin(VC, P_, 1.0, old - OFF)
-        ts(A("dv"), IB, VC, AL.mult, 1.0, AL.add)
+        shift("d" in PAR["sm"][t], A("dv"), IB, VC, 1.0)
+        wt = A("wt") if t else A("big", 6144, 8064)
+        dma("Y", [(wt, A("wz", 0, wt[4]))], 2500)
         if t:
-            dma("Y", [(A("wt"), A("wz"))], 2500)
-            dma("Y", [(A("flat", s * V, s * V + old, p=row(s)), A("nb", 0, old, p=row(s))) for s in range(16)], 2800)
+            s0 = PAR["s0"] if PAR["inflat"][t - 1][1] else 16
+            dma("Y", [(A("flat", s * V + old - M, s * V + old, p=row(s)), A("nb", old - M, old, p=row(s))) for s in range(s0)], 2200, 50.0)
+            if s0 < 16:
+                dma("Y", [(A("flat", s * V, s * V + old, p=row(s)), A("nb", 0, old, p=row(s))) for s in range(s0, 16)], 1900 + 2.2 * old, 0.155 * old)
         XX = A("xx", 0, 128)
-        cp(A("nbb"), IN(nbw, bl))
-        mm(acc(A(KO, 296, 360), [(A("selc", 128 * h, 128 * h + 128), A("nbb", h, 128, 2)) for h in range(2)]))
-        ts(A("cq"), A(KO, 296, 360), -OFF, AL.add)
-        tt(A("gg"), IN(nbw, A("cq")), A("mask", 0, 1024), AL.mult)
+        shift("n" in PAR["sm"][t], A("nbb"), IN(nbw, bl), 1.0, TOFF)
+        mm(acc(A(KO, 304, 368), [(A("selc", 128 * h, 128 * h + 128), A("nbb", h, 128, 2)) for h in range(2)]))
+        ts(A("cq"), A(KO, 304, 368), -OFF, AL.add)
+        nbrs("gg", nbw, "cq", PAR["gg"][t][0], TOFF)
         ac(A("xcq"), IN(xw, A("cq")))
         GK = lambda k: A("gg", k, 1024, 8)
-        mm([(A(KO, k, 256, 8), GK(k), A("rf"), True, True) for k in range(8)])
+        RF = lambda nm, k, a, b, s=1: A(nm, 32 * k + a, 32 * k + b, s)
+        mm([(A(KO, k, 256, 8), GK(k), RF("rf", k, 0, 32), True, True) for k in range(8)])
         tt(A("fam"), A(KO, 0, 256), A("par"), AL.mult)
         mm([(A(KO, 360 + 64 * u, 424 + 64 * u), A("fam", 128 * u, 128 * u + 128), A("h2"), True, True) for u in range(2)])
         ts(A("fa"), A(KO, 360, 488), -OFF, AL.add)
-        mm([(A(TT, 384, 512), XX, IB, True, True)])
-        cp(A("brep"), A(TT, 384, 512))
-        ts(A("nbrep"), A("brep"), -1.0, AL.mult)
+        mm([(A(D1, 384, 512), XX, IB, True, True)])
+        shift("b" in PAR["sm"][t], A("brep"), A(D1, 384, 512), 1.0, 0.0)
+        shift("b" in PAR["sm"][t], A("nbrep"), A("brep"), -1.0, 0.0)
         for u, bank in enumerate((D0, D1)):
             c = []
             for q in range(4):
@@ -459,31 +501,39 @@ def build(g, core, T, topo, costs):
             ts(A("eq", 512 * u, 512 * u + 512), A(bank), 0.0, AL.is_equal)
         EQ = lambda q: A("eq", 128 * q, 128 * q + 128)
         grp([(A(D0, 0, 128), IB, A("negm"))] + [(A(D0, 16 * q, 16 * q + 16), EQ(q), A("cw")) for q in range(8)])
-        ts(A("nfx"), A(D0, 0, 128), TC, AL.is_ge, JC, AL.mult)
+        ts(A("nfx"), A(D0, 0, 128), TC, AL.is_ge, JC if t else GB16, AL.mult)
         tt(A("rlx"), A("nfx"), XX, AL.max)
         mm([(A(D1, 0, 8), A("rlx"), A("b8"), True, True)])
         cp(A("rl"), A(D1, 0, 8))
-        grp([(A(TT, 0, 256), A("nbb"), A("selc")), (A(TT, 0, 256), A("dv"), A("nones"))] + [(A(TT, k, 256, 8), GK(k), A("ru")) for k in range(8)])
-        mm([(A(TT, 256 + k, 384, 8), GK(k), A("rfd"), True, True) for k in range(8)])
+        grp([(A(TT, 0, 256), A("nbb"), A("selc")), (A(TT, 0, 256), A("dv"), A("nones", 0, 256))]
+            + [(A(TT, 120 * u + 8 + k, 128 * u + 128, 16), GK(k), RF("rf", k, 16 * u, 16 * u + 16, 2)) for k in range(8) for u in range(2)])
+        mm([c for k in range(8) for c in acc(A(TT, 256 + k, 384, 8), [(GK(k), RF("rfs", k, 16 * u, 16 * u + 16)) for u in range(2)])])
         r8v = lambda a, b: A("rep", 2 * a, 2 * b, 2)
         keys = lambda nm, o, sg: [(A(KO, k, 384, 8), A(nm, o + k, o + 1024, 8), A(sg)) for k in range(8)]
-        far = PAR["gf"][t] == "S"
+        far, both = PAR["gf"][t] == "S", PAR["gf"][t] == "B"
         fl, al = IN(xw, A("fa", 0, 64)), IN(xw, A("fa", 64, 128))
         grp([(A(KO, 0, 384), IB, A("bias"))] + (keys("xcq", 0, "bp") + [(A(KO, k, 384, 8), XV(t, 0), A("bn")) for k in range(8)] if far else []), stop=False)
-        tt(A("sc", 1024, 2048), al, r8v(0, 1024), AL.max, after=[tt(A("sc", 0, 1024), al, A("xcq"), AL.max)])
-        if far:
-            ac(A("ab"), fl)
-            for o, sub in (("xcq", lambda u: A("xcq", 512 * u, 512 * u + 512)), ("ab", lambda u: r8v(512 * u, 512 * u + 512))):
+        meet = dict((e, [made[e][mid[0] - PAR["meet"][t]]] if PAR["meet"][t] else []) for e in "VS")
+        gains = len(ops)
+        def sizes(got, at, lst, to, after):
+            ac(A(got, at, at + 1024), lst, after=after)
+            for (o, c), sub in zip(to, (lambda u: A("xcq", 512 * u, 512 * u + 512), lambda u: r8v(512 * u, 512 * u + 512))):
                 for u, bank in enumerate((D0, D1)):
-                    mm(acc(A(bank), [(IB, A("ab", 512 * u, 512 * u + 512)), (A("ibn"), sub(u))]))
-                    ac(A(o, 512 * u, 512 * u + 512), A(bank), AF.Abs)
+                    mm(acc(A(bank), [(IB, A(got, at + 512 * u, at + 512 * u + 512)), (A("ibn"), sub(u))]))
+                    ac(A(o, c + 512 * u, c + 512 * u + 512), A(bank), AF.Abs)
+        if both:
+            sizes("sc", 1024, al, (("sc", 0), ("sc", 1024)), meet["S"])
+        else:
+            tt(A("sc", 1024, 2048), al, r8v(0, 1024), AL.max, after=[tt(A("sc", 0, 1024), al, A("xcq"), AL.max, after=meet["V"])])
+        if far or both:
+            sizes("ab", 0, fl, (("xcq", 0), ("ab", 0)), meet["S"])
         else:
             tt(A("ab"), fl, A("xcq"), AL.max)
             tt(A("xcq"), fl, r8v(0, 1024), AL.max)
         grp(keys("sc", 0, "bn2" if far else "bn"), start=False, stop=False)
         grp(keys("sc", 1024, "bp2" if far else "bp"), start=False, stop=False)
-        grp(keys("xcq", 0, "bp" if far else "bn"), start=False, stop=False)
-        grp(keys("ab", 0, "bn" if far else "bp"), start=False)
+        grp(keys("xcq", 0, "bp" if far or both else "bn"), start=False, stop=False)
+        grp(keys("ab", 0, "bn" if far or both else "bp"), start=False)
         ts(A("indp"), A(KO, 256, 384), 0.0, AL.is_ge)
         ts(A("dw"), A(KO, 0, 256), 0.0, AL.is_ge, WC, AL.mult)
         tt(A("ot"), A("indp"), A(TT, 256, 384), AL.mult)
@@ -493,101 +543,156 @@ def build(g, core, T, topo, costs):
         ac(A("wts"), A(D1, 0, 128))
         mm([(A(D1, 128, 256), A("wts"), IB, True, True)])
         ac(A("wrow"), A(D1, 128, 256))
-        grp([(A(KO, 0, 256), A("zero"), A("nones"))] + [(A(KO, 128 * z, 128 * z + 128), A("i3"), A("dw", 128 - 128 * z, 256 - 128 * z)) for z in range(2)]
+        grp([(A(KO, 0, 256), A("zero"), A("nones", 0, 256))] + [(A(KO, 128 * z, 128 * z + 128), A("i3"), A("dw", 128 - 128 * z, 256 - 128 * z)) for z in range(2)]
             + [(A(KO, 16 * q, 16 * q + 16), EQ(q % 8), A("dw", 16 * q, 16 * q + 16)) for q in range(16)], stop=False)
-        tt(A("gg"), IN(nbw, A("o16")), A("mask", 1, 1025), AL.mult)
-        mm(acc(A(D0, 64, 128), [(A("zbot", 16 - r, 144 - r), A("gg", r, 1024, 16)) for r in range(16)]))
+        nbrs("gg", nbw, "o16", PAR["gg"][t][1], 0.0)
+        mm(acc(A(D0, 64, 128), [(A("zb", 144 * ((r + 1) % 8) + 16 - r, 144 * ((r + 1) % 8) + 144 - r), A("gg", r, 1024, 16)) for r in range(16)]))
         cp(A("b16"), A(D0, 64, 128))
-        cp(IN(A("wt"), A("rl")), A("wrow"))
-        ac(A("gw"), IN(A("wt"), A("b16")))
+        cp(IN(wt, A("rl")), A("wrow"))
+        nbrs("gw", wt, "b16", PAR["gg"][t][2], 0.0)
         grp([(A(KO, k, 256, 8), A("gw", k, 1024, 8), A("rom", 32 * k, 32 * k + 32)) for k in range(8)], start=False)
         ts(A("mw"), A(KO, 0, 256), TC, AL.is_lt)
         tt(A("zz"), A("mw"), A(TT, 0, 256), AL.mult)
         mm(acc(A(D0, 128, 256), [(A("ones"), A("dv")), (A("zz", 0, 128), IB), (A("zz", 128, 256), IB)]))
-        ts(A("thh"), A(D0, 128, 256), -OFF, AL.add)
-        mm([c for z in range(2) for c in acc(A(D1, 64 * z, 64 * z + 64), [(SQ(2 * z + h), A("thh", h, 128, 2)) for h in range(2)])])
+        shift("t" in PAR["sm"][t], A("thh"), A(D0, 128, 256), 1.0, -OFF)
+        mm([c for q in range(4) for c in acc(A(D1, 32 * q, 32 * q + 32), [(SQ(q, h), A("thh", h, 128, 4)) for h in range(4)])])
         ts(A("sl"), A(D1, 0, 128), SV, AL.add)
         hold = dict((e, made[e][-PAR["hold"][t]:][:1] if PAR["hold"][t] else []) for e in "VS")
-        if PAR["nxs"][t] == "V":
-            ops[cp(IN(A("flat", 0, 8 * V), A("sl", 0, 64)), A("val"))]["after"] = hold["V"]
-        else:
-            ac(IN(A("flat", 0, 8 * V), A("sl", 0, 64)), A("val"), AF.Silu, after=hold["S"])
-        ac(IN(A("flat", 8 * V, 16 * V), A("sl", 64, 128)), A("val"), AF.Silu, after=hold["S"])
-        nbg(mm(acc(A(D0, 256, 384), [(SQ(1), A("thh")), (SQ(2), A("thh"))])))
-        ac(A("nb", old, have), A(D0, 256, 384), bias=OFF)
+        for q in range(2):
+            ops[ts(IN(A("flat", 4 * q * V, 4 * q * V + 4 * V), A("sl", 32 * q, 32 * q + 32)), A("val", 0, 512), 1.0, AL.mult, -OFF, AL.add)]["after"] = hold["V"]
+            ac(IN(A("flat", (8 + 4 * q) * V, (12 + 4 * q) * V), A("sl", 64 + 32 * q, 96 + 32 * q)), A("val", 0, 512), AF.Silu, after=hold["S"])
+        nbg(mm(acc(A(D0, 256, 384), [(SQ(q, (q + 2) % 4), A("thh")) for q in range(4)])))
+        ac(A("nb", old, have), A(D0, 256, 384), bias=BOFF)
         W = (64, 48 if have == 1792 else 64)
-        for r, (a, b) in enumerate(((0, 1024), (1024, old))):
+        direct = PAR["direct"][t]
+        if direct:
+            at = lambda s: 512 * (s % 8 < 4) + 256 * (s // 8) + 64 * (s % 4)
+            for z, ks in enumerate(((0,), (1, 2, 3), (4, 5, 6, 7))):
+                dma(PAR["dq"][t][z % 2], [(A("val", at(s), at(s) + 64), A("flat", s * V, s * V + 1024, p=row(s))) for k in ks for s in (8 + k, k)], 1900 + 400 * len(ks), 160.0)
+                for u in (8, 0):
+                    ts(A("off", 64 * (u + ks[0]), 64 * (u + ks[-1] + 1)), A("val", at(u + ks[0]), at(u + ks[-1]) + 64), -OFF if u else 0.0, AL.add)
+        for a, b in ((0, 1024), (1024, old))[::-1 if direct else 1]:
             for z in range(2):
-                dma(PAR["dq"][t][z], [(A("nb", a, b, p=row(s)), A("flat", s * V + a, s * V + b, p=row(s))) for s in range(8 * z, 8 * z + 8)], 2400)
+                dma(PAR["dq"][t][z], [(A("nb", a, b, p=row(s)), A("flat", s * V + a, s * V + b, p=row(s))) for s in range(8 * z, 8 * z + 8)], 1900 + 2.2 * (b - a), 0.155 * (b - a))
                 ops[-1]["comm"] = True
-        for r in range(2):
+        for r in range(direct, 2):
             a, w, l = 1024 * r, W[r], (0 if W[r] == 64 else 64)
-            ts(A("nbp", a, a + 16 * w), IN(A("nb", a, a + 16 * w), A("pil", l, l + w)), -OFF, AL.add)
+            if PAR["wrap"][t][r] == "S":
+                ac(A("mix", 2048 + a, 2048 + a + 16 * w), IN(A("nb", a, a + 16 * w), A("pil", l, l + w)), bias=NOFF)
+                cp(A("nbp", a, a + 16 * w), A("mix", 2048 + a, 2048 + a + 16 * w))
+            else:
+                ts(A("nbp", a, a + 16 * w), IN(A("nb", a, a + 16 * w), A("pil", l, l + w)), NOFF, AL.add)
+            ops[-1]["after"] = made["V"][-PAR["holdw"][t]:][:1] if r and PAR["holdw"][t] else []
             for z, ks in enumerate(((0,), (1, 2), (3, 4), (5, 6, 7)) if r == 0 else ((0, 1, 2, 3), (4, 5, 6, 7))):
                 dma(PAR["dq"][t][z % 2], [(A("off", a + w * s, a + w * s + w), A("nbp", a, a + 16 * w, p=row(s))) for k in ks for s in (8 + k, k)], 1900 + 250 * len(ks))
         OL = lambda s, a, b: A("off", (a - a % 1024) + W[a // 1024] * s + a % 1024 // 16, (a - a % 1024) + W[a // 1024] * s + (b - a + a % 1024) // 16)
         for o in ops[first:]:
             o["lead"] = PAR["lead"][t]
+            o["round"] = t
+        for o in ops[first:gains]:
+            o["lead"] += PAR["haste"][t]
         if t + 1 == RO:
-            if "S" in PAR["nxs"]:
-                ts(A("nb"), A("nb"), MAGIC - OFF, AL.add, -MAGIC, AL.add)
-            else:
-                ac(A("nb"), A("nb"), bias=-OFF)
-            ops[-1]["lead"] = PAR["outl"]
             dma("Y", [(T.nx[k::8, :], A("nb", p=row(k))) for k in range(8)], 3000)
-        nch = [0]
+        if PAR["early"][t]:
+            yw = A("yb", 0, old)
+            ac(A("ys"), IN(yw, pf), scale=0.5)
+            ac(A("val"), IN(yw, A("c16", 192, 256)), scale=-0.0625)
+            tt(A("val"), IN(yw, A("c16", 128, 192)), A("val"), AL.mult)
+            mm(acc(A(D0, 0, 128), [(A("iff"), A("ys"))] + [(A("iff"), A("val", k, 1024, 8)) for k in range(8)]))
+            ac(A("ys"), A(D0, 0, 128), bias=0.5)
+        else:
+            ac(A("ys"), IN(A("ya", 0, old), pf))
+        to = T.cores[(rank - 1 - t) % n]
+        rid, pid, _ = topo.addr(to)
+        sent[0] += len(topo.engines(core, to))
+        s = op("G", (lambda a=A("ya", old, have)[0], rid=rid, pid=pid, m=topo.mask(core, to), t=t:
+                     g.remote_dma(a, A("ys")[0], T.sem["ay%d" % t], T.sem.sent, pid, rid, m)), 1500, [A("ys")], [], kind="x", sem=T.sem.sent, cnt=sent[0], lat=2500.0)
+        arrive("ay%d" % t, len(topo.engines(T.cores[(rank + 1 + t) % n], core)), A("ya", old, have), s)
+        nch = 0
         for sw in range(2):
-            nev = [0]
+            mid[0] = len(made["V"])
             src, dst = ("ya", "yb") if sw == 0 else ("yb", "ya")
             yw = A(src, 0, have)
-            cuts = PAR["cuts"][t]
-            for ci, (a, b) in enumerate(zip(cuts, cuts[1:])):
+            chunks, a = [], 0
+            for w, plan in PAR["plan"][2 * t + sw]:
+                chunks.append((a, a + w, plan))
+                a += w
+            over = lambda q: [c for c in chunks if c[0] < 512 * q + 512 and c[1] > 512 * q]
+            banks = {}
+
+            def term(q, lo, hi, lhs, rhs, turn=False):
+                b, bank = banks[q], (Y0, Y1, Y2, Y3)[q]
+                calls = [(A(bank, lo - 512 * q, hi - 512 * q), rhs)]
+                if turn:
+                    calls = [(A(bank, 64 * i, 64 * i + 64), A(rhs[1], rhs[2] + 8 * q + i, rhs[3], 16)) for i in range(8)]
+
+                def fn(b=b, first=not b["ops"]):
+                    b["left"] -= 1
+                    for c in calls:
+                        r = pe.matmul(c[0][0], lhs[0], c[1][0], first, b["left"] == 0 and c is calls[-1])
+                    return r
+                b["left"] += 1
+                j = op("P", fn, 40 + max(64, hi - lo) * (4 if SB[rhs[1]][1] == F else 1) * PE, [lhs, rhs], [A(bank, lo - 512 * q, hi - 512 * q)])
+                if b["ops"]:
+                    ops[j]["grp"] = b["ops"][0]
+                b["ops"].append(j)
+
+            nl = PAR["late"][2 * t + sw]
+            late = [ci for ci, c in enumerate(chunks) if c[2][8] in "el"]
+            places = [[] for c in chunks]
+            for ci, ks in [(ci, range(8 - nl if ci in late else 8)) for ci in range(len(chunks))] + [(ci, (k,)) for k in range(8 - nl, 8) for ci in late]:
+                a, b, plan = chunks[ci]
                 w = b - a
-                rn, rw, pos = ("flat", 16 * V, posf) if nch[0] < PAR["nflat"][t] else ("ring", RING, posr)
-                nch[0] += 1
-                parts = []
-                for i in range((w + 511) // 512):
-                    parts.append(((Y0, Y1, Y2)[nbk[0] % 3], 512 * i, min(w, 512 * i + 512)))
-                    nbk[0] += 1
-                fl = PAR["foldl"][t]
-                fold = fl[len(cuts) - 2 - ci] if len(cuts) - 2 - ci < len(fl) else PAR["fold"][t]
-                terms = [(src, a)]
-                place = []
-                for k in range(8):
+                parts = [(q, max(a, 512 * q), min(b, 512 * q + 512)) for q in range(a // 512, (b + 511) // 512)]
+                for q, lo, hi in parts if ks[0] == 0 else []:
+                    if q not in banks:
+                        top = min(have, 512 * q + 512)
+                        banks[q] = dict(ops=[], left=0, mu=0.0, ev=[])
+                        if any(c[2][9] == "V" for c in over(q)):
+                            banks[q]["mu"] = 0.5
+                            term(q, 512 * q, top, A("lam", p=slice(0, 1)), A("nones", 0, top - 512 * q, p=slice(0, 1)))
+                        term(q, 512 * q, top, A("ifh"), A(src, 512 * q, top))
+                place = places[ci]
+                for k in ks:
+                    rn, r0, rw, pos = ("flat", PAR["s0"] * V, 16 * V, posf) if PAR["inflat"][t][0] <= nch < PAR["inflat"][t][1] else ("ring", 0, RING, posr)
+                    nch += w
                     if pos[0] + w > rw:
-                        pos[0] = 0
-                    o = pos[0]
+                        pos[0] = r0
+                    place.append((rn, pos[0]))
                     pos[0] += w
-                    place.append(o)
-                    pk = A(rn, o, o + w)
-                    chain["S"] = [ac(pk, IN(yw, OL(8 + k, a, b)), after=chain["S"], scale=-0.125)]
-                    chain["V"] = [tt(pk, IN(yw, OL(k, a, b)), pk, AL.mult, after=chain["V"])]
+                    pr = lambda i, lo=a, hi=b: A(place[i][0], place[i][1] + lo - a, place[i][1] + hi - a)
+                    hd = PAR["head"][2 * t + sw] if ci == 0 and k == 0 else 0
+                    for lo, hi in ((a, a + hd), (a + hd, b)) if hd else ((a, b),):
+                        chain["S"] = [ac(pr(k, lo, hi), IN(yw, OL(8 + k, lo, hi)), after=chain["S"], scale=-0.0625)]
+                        chain["V"] = [tt(pr(k, lo, hi), IN(yw, OL(k, lo, hi)), pr(k, lo, hi), AL.mult, after=chain["V"])]
+                    ops[chain["S"][0]]["cut"] = ci == 0 and k == 0
                     made["S"] += chain["S"]
                     made["V"] += chain["V"]
-                    if k == 0 and -1 in fold:
-                        fold_dma(pk, A(src, a, b))
-                        terms = [(rn, o)]
-                    elif k - 1 in fold:
-                        fold_dma(A(rn, place[k - 1], place[k - 1] + w), pk)
-                        terms.append((rn, place[k - 1]))
-                    elif k + 9 in fold:
-                        chain["V"] = [tt(pk, pk, A(rn, place[k - 1], place[k - 1] + w), AL.add, after=chain["V"])]
-                        if k + 10 not in fold:
-                            terms.append((rn, o))
-                    elif k not in fold and k + 10 not in fold:
-                        terms.append((rn, o))
-                    for i, (nm, c0) in enumerate(terms):
-                        mm([(A(bk, 0, q - p), A("iff"), A(nm, c0 + p, c0 + q), k == 0 and i == 0, k == 7 and i == len(terms) - 1) for bk, p, q in parts])
-                    terms = []
-                for bk, p, q in parts:
-                    if PAR["ev"][t][nev[0] % len(PAR["ev"][t])] == "S":
-                        ac(A(dst, a + p, a + q), A(bk, 0, q - p), bias=0.5, scale=0.5)
-                    else:
-                        ts(A(dst, a + p, a + q), A(bk, 0, q - p), 0.5, AL.mult, 0.5, AL.add)
-                    ops[-1]["lead"] = PAR["evl"]
-                    nev[0] += 1
-                if t == RO - 1 and sw == 1:
-                    dma("Y", [(T.y[:, a:b], A(dst, a, b))], 3000)
+                    c = plan[k + 1]
+                    if c.isdigit():
+                        fold_dma(pr(int(c)), pr(k))
+                    elif c in "ABCDEFG":
+                        chain["V"] = [tt(pr(k), pr(k), pr(ord(c) - 65), AL.add, after=chain["V"])]
+                    for i in range(k + 1):
+                        mine = plan[i + 1] not in "e01234567" and chr(65 + i) not in plan[1:9]
+                        if mine and max(i, plan.rfind(str(i), 1, 9) - 1) == k:
+                            for q, lo, hi in parts:
+                                term(q, lo, hi, A("iff"), pr(i) if direct and ci == 0 else pr(i, lo, hi), direct and ci == 0)
+                for q, lo, hi in parts if ks[-1] == 7 else []:
+                    banks[q]["ev"].append((lo, hi, plan[9], pr(7, lo, hi) if plan[8] == "e" else A(src, lo, hi)))
+                    if len(banks[q]["ev"]) == len(over(q)):
+                        ev = sorted(banks[q]["ev"], key=lambda e: e[0])
+                        if all(e[2] == ev[0][2] != "V" for e in ev):
+                            ev = [(ev[0][0], ev[-1][1], ev[0][2], None)]
+                        for lo, hi, e, more in ev:
+                            bk = A((Y0, Y1, Y2, Y3)[q], lo - 512 * q, hi - 512 * q)
+                            if e != "V":
+                                shift(e == "S", A(dst, lo, hi), bk, 1.0, 0.5 - banks[q]["mu"])
+                            else:
+                                tt(A(dst, lo, hi), bk, more, AL.add)
+                            ops[-1].update(lead=PAR["evl"], hard=list(banks[q]["ops"]))
+                            if t == RO - 1 and sw == 1:
+                                dma("Y", [(T.y[:, lo:hi], A(dst, lo, hi))], 2000 + 1.0 * (hi - lo))
     return ops, sent[0]
 
 
@@ -602,9 +707,13 @@ def schedule(ops, other):
                 for j, a2, b2, w2 in hist.get(nm, ()):
                     if w and w2 and o.get("comm") and ops[j].get("comm"):
                         continue
+                    if nm[:2] == "ps" and o.get("grp", -1) == ops[j].get("grp", -2):
+                        continue
                     if j != i and ((nm[:2] == "ps" and (ops[j]["eng"] != o["eng"] or o["eng"] == "P")) or ((w or w2) and a < b2 and a2 < b)):
                         deps.add(j)
                         soft.discard(j)
+                        if "fold" in ops[j] and w2 and "cons" not in ops[j]:
+                            ops[j]["cons"] = i
         for regs, w in ((o["rd"], False), (o["wr"], True)):
             for nm, a, b in regs:
                 h = hist.setdefault(nm, [])
@@ -613,52 +722,68 @@ def schedule(ops, other):
                 if nm[:2] == "ps":
                     h[:] = [e for e in h if e[0] != i][-12:]
                 h.append((i, a, b, w))
-        deps = set(j if ops[j].get("cons", i) == i else ops[j]["cons"] for j in deps) | set(o.get("hard", ()))
+        deps |= set(o.get("hard", ())) | set([o["grp"]] if "grp" in o else []) | set([o["fold"]] if o.get("fold", -1) >= 0 else [])
+        for j in list(deps):
+            while "fold" in ops[j] and ops[j]["cons"] != i:
+                deps.discard(j)
+                j = ops[j]["cons"]
+                deps.add(j)
+        known = done = 0
+        for j in deps:
+            if j not in soft and not o["eng"] == ops[j]["eng"] == "P":
+                known |= ops[j]["done"] ^ 1 << j
+            elif o["kind"] == ops[j]["kind"] == "c":
+                known |= ops[j]["known"]
+                done |= ops[j]["done"]
+        deps = [j for j in deps if not known >> j & 1]
+        o["known"] = known | sum(1 << j for j in deps if j not in soft and not o["eng"] == ops[j]["eng"] == "P")
+        o["done"] = o["known"] | done | 1 << i
         o["deps"], o["soft"] = sorted(deps), soft
-    for i in range(len(ops) - 1, -1, -1):
-        o = ops[i]
-        o["bl"] = o.get("bl", 0.0) + o["dur"] + o["lat"]
-        for j in o["deps"]:
-            ops[j]["bl"] = max(ops[j].get("bl", 0.0), o["bl"] + LAT)
     succ = [[] for _ in ops]
-    left = [len(o["deps"]) for o in ops]
     for i, o in enumerate(ops):
-        o["rdy"] = 0.0
         for j in o["deps"]:
             succ[j].append(i)
-    free = dict((e, 0.0) for e in "VSPGYR")
-    order = dict((e, []) for e in "VSPGYR")
-    ready = dict((e, []) for e in "VSPGYR")
-    for i, o in enumerate(ops):
-        if not left[i]:
-            ready[o["eng"]].append(i)
-    for _ in ops:
-        e = min((e for e in ready if ready[e]), key=lambda e: max(free[e], min(ops[i]["rdy"] for i in ready[e])))
-        now = max(free[e], min(ops[i]["rdy"] for i in ready[e]))
-        i = max((i for i in ready[e] if ops[i]["rdy"] <= now + PAR["look"]), key=lambda i: (ops[i]["bl"] + ops[i].get("lead", 0.0), -i))
-        ready[e].remove(i)
-        o = ops[i]
-        o["t0"] = max(now, o["rdy"])
-        free[e] = o["t0"] + o["dur"]
-        o["end"] = free[e] + o["lat"]
-        order[e].append(i)
-        for j in succ[i]:
-            gap = 0.0 if ops[j]["eng"] == e and (e == "P" or i in ops[j]["soft"]) else LAT
-            ops[j]["rdy"] = max(ops[j]["rdy"], o["end"] + gap)
-            left[j] -= 1
-            if not left[j]:
-                ready[ops[j]["eng"]].append(j)
-    gap = lambda i, j: ops[i]["lat"] + (0.0 if ops[j]["eng"] == ops[i]["eng"] and (ops[i]["eng"] == "P" or i in ops[j]["soft"]) else LAT)
-    pre = [[(j, gap(j, i)) for j in o["deps"]] for i, o in enumerate(ops)]
-    post = [[(j, gap(i, j)) for j in succ[i]] for i in range(len(ops))]
+    eng = [o["eng"] for o in ops]
+    link = [[(j, 0.0 if eng[j] == eng[i] and (eng[i] == "P" or j in o["soft"]) else 1.0) for j in o["deps"]] for i, o in enumerate(ops)]
 
-    def place(seq, before, tail):
+    def begin(dur, lat, wake, lead, slow, look):
+        pre = [[(j, lat[j] + wake * h) for j, h in b] for b in link]
+        post = [[] for _ in ops]
+        for i, b in enumerate(pre):
+            for j, w in b:
+                post[j].append((i, w))
+        bl = [0.0] * len(ops)
+        for i in range(len(ops) - 1, -1, -1):
+            bl[i] = max([bl[j] + wake for j in succ[i]] + [0.0]) + dur[i] + lat[i] + (slow if ops[i].get("round") and eng[i] in "VS" else 0.0)
+        key = [bl[i] + o.get("lead", 0.0) + lead[o.get("round", 0)] for i, o in enumerate(ops)]
+        left = [len(b) for b in link]
+        rdy, end = [0.0] * len(ops), [0.0] * len(ops)
+        free = dict((e, 0.0) for e in "VSPGYR")
+        ready = dict((e, [i for i in range(len(ops)) if not left[i] and eng[i] == e]) for e in "VSPGYR")
+        for _ in ops:
+            now, e = min((max(free[e], min(rdy[i] for i in ready[e])), e) for e in ready if ready[e])
+            i = max((i for i in ready[e] if rdy[i] <= now + look), key=lambda i: (key[i], -i))
+            ready[e].remove(i)
+            end[i] = free[e] = max(now, rdy[i]) + dur[i]
+            for j, w in post[i]:
+                rdy[j] = max(rdy[j], end[i] + w)
+                left[j] -= 1
+                if not left[j]:
+                    ready[eng[j]].append(j)
+        back = place(rank([-x for x in end], post, pre), post, dur, lat)
+        end = place(rank([-x for x in back], pre, post), pre, dur, None)
+        seq = sorted(range(len(ops)), key=lambda i: (end[i], i))
+        end = run(seq, other[0])
+        at = [end[i] - other[0][1][i] - other[0][0][i] if eng[i] != "Y" else max([end[j] for j, _ in link[i]] + [0.0]) for i in range(len(ops))]
+        return rank(at, pre, post)
+
+    def place(seq, before, dur, tail):
         busy = dict((e, ([], [])) for e in "VSPGYR")
         end = [0.0] * len(ops)
         for i in seq:
-            d = ops[i]["dur"]
-            t = max([end[j] + w for j, w in before[i]] + [ops[i]["lat"] if tail else 0.0])
-            st, en = busy[ops[i]["eng"]]
+            d = dur[i]
+            t = max([end[j] + w for j, w in before[i]] + [tail[i] if tail else 0.0])
+            st, en = busy[eng[i]]
             k = len(st)
             while k and en[k - 1] > t:
                 k -= 1
@@ -684,42 +809,14 @@ def schedule(ops, other):
         return sorted(out, key=lambda i: (top[i], pos[i]))
 
     def length(seq):
-        tot = 0.0
-        for dur, lat, xfer, wake in other:
-            free = dict((e, 0.0) for e in "VSPGYRD")
-            end = [0.0] * len(ops)
-            for i in seq:
-                e = ops[i]["eng"]
-                t = free[e]
-                for j, hard in link[i]:
-                    if end[j] + wake * hard > t:
-                        t = end[j] + wake * hard
-                free[e] = t = t + dur[i]
-                end[i] = t + lat[i]
-            tot += math.log(max(end))
-        return tot
-
-    link = [[(j, 1.0 if w > ops[j]["lat"] else 0.0) for j, w in b] for b in pre]
-    rnd = np.random.RandomState(PAR["seed"])
-    end = [o["t0"] + o["dur"] for o in ops]
-    best = None
-    for n in range(PAR["passes"]):
-        shake = PAR["shake"] * rnd.rand(len(ops)) * (rnd.rand(len(ops)) < PAR["share"]) if n > 1 else np.zeros(len(ops))
-        back = place(rank([float(s) - x for s, x in zip(shake, end)], post, pre), post, True)
-        end = place(rank([-x for x in back], pre, post), pre, False)
-        seq = sorted(range(len(ops)), key=lambda i: (end[i], i))
-        now = length(seq)
-        if best is None or now < best[0]:
-            best = (now, end, seq)
-        end = best[1]
-    seq = best[2]
-    eng = [o["eng"] for o in ops]
+        return sum(math.log(max(run(seq, c))) for c in other)
 
     def run(seq, c, why=None):
-        dur, lat, _, wake = c
+        dur, lat, xfer, wake = c
         free = dict((e, 0.0) for e in "VSPGYR")
         last = dict((e, -1) for e in "VSPGYR")
         end = [0.0] * len(ops)
+        moved = 0.0
         for i in seq:
             e = eng[i]
             t, w = free[e], last[e]
@@ -727,44 +824,156 @@ def schedule(ops, other):
                 if end[j] + wake * hard >= t:
                     t, w = end[j] + wake * hard, -2 - j
             free[e] = t = t + dur[i]
-            end[i] = t + lat[i]
+            t += lat[i]
+            if xfer[i]:
+                moved = t = max(t, min(moved, t + 4000.0) + xfer[i])
+            end[i] = t
             last[e] = i
             if why is not None:
                 why[i] = w
         return end
 
-    now = top = best[0]
-    keep = seq
-    for n in range(PAR["swaps"]):
-        if n % 8 == 0 or fresh:
-            why = {}
-            end = run(seq, other[rnd.randint(len(other))], why)
-            i, arcs = max(range(len(ops)), key=lambda i: end[i]), []
+    rnd = np.random.RandomState(PAR["seed"])
+    starts = []
+    for n in range(PAR["starts"]):
+        mix = rnd.dirichlet([1.0] * len(other))
+        dur, lat = [[float(x) for x in sum(m * np.array(c[k]) for m, c in zip(mix, other))] for k in range(2)]
+        lat = [x * PAR["DL"] for x in lat]
+        seq = begin(dur, lat, LAT, [0.0] + [float(x) for x in PAR["span"] * (rnd.rand(2) - 0.5)], float(rnd.choice(PAR["slow"])), float(rnd.choice((100.0, 200.0))))
+        starts.append((length(seq), n, seq))
+    starts = [s[2] for s in sorted(starts)]
+    num = ["VSPGYR".index(e) for e in eng]
+    tied = [[[(j, c[3] * hard) for j, hard in b] for b in link] for c in other]
+    STEP = 32
+
+    def rerun(seq, k, start, old, stop=99999):
+        dur, lat, xfer, _ = other[k]
+        m = start // STEP
+        end, marks, ln = old[0][:], old[1][:m + 1], tied[k]
+        free = list(marks[m])
+        for a in range(m * STEP, len(seq), STEP):
+            for i in seq[a:a + STEP]:
+                e = num[i]
+                t = free[e]
+                for j, w in ln[i]:
+                    if end[j] + w > t:
+                        t = end[j] + w
+                free[e] = t = t + dur[i]
+                t += lat[i]
+                if xfer[i]:
+                    free[6] = t = max(t, min(free[6], t + 4000.0) + xfer[i])
+                if t > free[7]:
+                    free[7] = t
+                free[8] += t
+                end[i] = t
+            marks.append(tuple(free))
+            if a >= stop and a + STEP < len(seq):
+                was = old[1][len(marks) - 1]
+                d, ago = free[0] - was[0], min(free[0], was[0]) - 7000.0
+                if (all(abs(free[e] - was[e] - d) < 1.0 or max(free[e], was[e]) < ago for e in (1, 2, 3, 4, 6))
+                        and all(abs(end[i] - old[0][i] - d) < 1.0 or max(end[i], old[0][i]) < ago for i in seq[max(0, a - 2 * STEP):a + STEP])):
+                    last = old[1][-1]
+                    return None, [last[:7] + (last[7] + d, last[8] - was[8] + free[8] + d * (len(seq) - a - STEP))]
+        return end, marks
+
+    def cross(seqs):
+        cuts = [i for i, o in enumerate(ops) if o.get("cut")]
+        back = [[(j, 0.0) for j in s] for s in succ]
+        best, top = seqs[0], length(seqs[0])
+        for c in cuts[::-1] + cuts:
+            for s in seqs:
+                for a, b in ((best, s), (s, best)):
+                    pa, pb = dict((i, k) for k, i in enumerate(a)), dict((i, k) for k, i in enumerate(b))
+                    new = rank([pa[i] if pa[i] < pa[c] else len(ops) + pb[i] for i in range(len(ops))], link, back)
+                    x = length(new)
+                    if x < top:
+                        best, top = new, x
+        return best
+
+    starts = [cross(starts[k::PAR["kept"]]) for k in range(PAR["kept"])]
+
+    back = [[(j, 0.0) for j in s] for s in succ]
+    whole_ops = [i for i, o in enumerate(ops) if "round" in o]
+    worth = lambda x: math.log(x[1][-1][7]) + PAR["mean"] * math.log(x[1][-1][8])
+    stages = [PAR["first"]] * len(starts) + [PAR["swaps"]]
+    found, left = [], 0
+    for n in range(sum(stages) + 1):
+        if not left:
+            if n:
+                found.append((top, len(found), keep))
+            if len(found) == len(stages):
+                break
+            seq = keep = starts[len(found)] if len(found) < len(starts) else cross([f[2] for f in sorted(found)])
+            left = span = stages[len(found)]
+            state = [rerun(seq, k, 0, ([0.0] * len(ops), [(0.0,) * 9])) for k in range(len(other))]
+            now, top, fresh = sum(worth(x) for x in state), sum(math.log(x[1][-1][7]) for x in state), True
+        left -= 1
+        if n % 24 == 0 or fresh:
+            why, c = {}, other[rnd.randint(len(other))]
+            end = run(seq, c, why)
+            pos = dict((i, k) for k, i in enumerate(seq))
+            idle = [i for i in seq if why[i] < -1 and eng[i] in "VS"]
+            i, whole = max(range(len(ops)), key=lambda i: end[i]), []
             while why[i] != -1:
+                if why[i] >= 0:
+                    whole.append((why[i], i))
+                i = why[i] if why[i] >= 0 else -2 - why[i]
+        fresh, arcs = False, whole
+        if rnd.rand() < PAR["block"]:
+            a = whole_ops[rnd.randint(len(whole_ops))]
+            b, d = a + int(rnd.choice((4, 10, 25, 60))), float(rnd.choice((-1, 1)) * rnd.choice((4, 10, 20, 40)))
+            new = rank([pos[i] + (d + 0.5 if a <= i < b and "round" in ops[i] else 0.0) for i in range(len(ops))], link, back)
+            trial = [rerun(new, k, 0, state[k]) for k in range(len(other))]
+            if sum(worth(y) for y in trial) <= now + PAR["heat"] * left / span * rnd.rand():
+                seq, now, fresh, state = new, sum(worth(y) for y in trial), True, trial
+            continue
+        if rnd.rand() < PAR["local"]:
+            i, arcs = idle[rnd.randint(len(idle))], []
+            stop = end[i] - 12000.0
+            while why[i] != -1 and end[i] > stop:
                 if why[i] >= 0:
                     arcs.append((why[i], i))
                 i = why[i] if why[i] >= 0 else -2 - why[i]
-            pos = dict((i, k) for k, i in enumerate(seq))
-        fresh = False
+        if not arcs:
+            continue
         a, b = arcs[rnd.randint(len(arcs))]
-        line = [i for i in seq[max(0, pos[a] - 40):pos[a] + 1] if eng[i] == eng[a]]
-        a = line[max(0, len(line) - 1 - int(rnd.choice((0, 0, 0, 1, 2, 4))))]
+        way = rnd.randint(3)
+        if way < 2:
+            line = [i for i in seq[max(0, pos[a] - 40):pos[a] + 1] if eng[i] == eng[a]]
+            a = line[max(0, len(line) - 1 - int(rnd.choice((0, 0, 0, 1, 2, 4))))]
+        else:
+            line = [i for i in seq[pos[b]:pos[b] + 40] if eng[i] == eng[b]]
+            b = line[min(len(line) - 1, int(rnd.choice((0, 0, 0, 1, 2, 4))))]
         part = seq[pos[a]:pos[b] + 1]
-        up, first = {b}, {eng[b]: False}
-        for i in part[-2::-1]:
-            if first.get(eng[i]) or any(j in up for j in succ[i]):
-                up.add(i)
-                first[eng[i]] = True
-        if a in up:
+        if way < 2:
+            up, first = {b}, {eng[b]: False}
+            for i in part[-2::-1]:
+                if (way == 0 and first.get(eng[i])) or any(j in up for j in succ[i]):
+                    up.add(i)
+                    first[eng[i]] = True
+        else:
+            down = {a}
+            for i in part[1:]:
+                if any(j in down for j, _ in link[i]):
+                    down.add(i)
+            up = set(part) - down
+        if a in up or b not in up:
             continue
         new = seq[:pos[a]] + [i for i in part if i in up] + [i for i in part if i not in up] + seq[pos[b] + 1:]
-        x = sum(math.log(max(run(new, c))) for c in other)
-        if x <= now + PAR["heat"] * (1.0 - n / PAR["swaps"]) * rnd.rand():
-            seq, now, fresh = new, x, True
+        trial, x = [], now
+        for k in range(len(other)):
+            trial.append(rerun(new, k, pos[a], state[k], pos[b]))
+            x += worth(trial[k]) - worth(state[k])
+            if x > now + 4 * PAR["heat"]:
+                break
+        if x <= now + PAR["heat"] * left / span * rnd.rand():
+            state = [y if y[0] else rerun(new, k, pos[a], state[k]) for k, y in enumerate(trial)]
+            seq, now, fresh = new, sum(worth(y) for y in state), True
+            x = sum(math.log(y[1][-1][7]) for y in state)
             if x < top:
                 top, keep = x, new
     seq = keep
-    return dict((e, [i for i in seq if ops[i]["eng"] == e]) for e in order)
+    return dict((e, [i for i in seq if ops[i]["eng"] == e]) for e in "VSPGYR")
 
 
 def rank_program(g, core, T, topo):
@@ -774,7 +983,7 @@ def rank_program(g, core, T, topo):
     other = []
     for c in COSTS:
         alt = build(g, core, T, topo, c)[0]
-        other.append(([o["dur"] for o in alt], [o["lat"] for o in alt], None, c["LAT"]))
+        other.append(([o["dur"] for o in alt], [o["lat"] for o in alt], [o.get("xfer", 0.0) for o in alt], c["LAT"]))
     key = repr(sorted(PAR.items()))
     if key not in ORDER:
         ORDER.clear()

@@ -9,63 +9,48 @@ V0, M, RO, V = 1664, 128, 3, 2048
 H = "float16"
 F, B, I, U = "float32", "bfloat16", "int32", "uint16"
 OFF = 64.0
-RING = 5120
+RING = 10752
 WT = 2368
-MAGIC = 12582912.0
 NF = 52
+PAIRS, PV, E4, EL = "Pp0p2p4p6S", "Pp0p2p4p6v", "Pp0p2p4peV", "Pp0p2pppeV"
 PAR = dict(
-    plan=None,
-    nflat=(6, 6, 99), s0=8,
-    dq=("YY", "YY", "YS"),
+    plan=(((1024, PV), (768, E4)), ((1024, PAIRS), (768, EL)), ((1024, PV), (896, E4)), ((1024, PAIRS), (896, EL)),
+          ((512, E4),) * 4, ((512, E4),) * 4),
+    head=(256,) * 6,
+    end=128,
     cutv=88,
-    lead=(-20000.0, 20000.0, 20000.0),
-    flead=(-20000.0, 0.0, 30000.0),
-    direct=(0, 0, 0), head=(0,) * 6, holdw=(0, 0, 0), late=(1, 1, 1, 1, 1, 1),
-    evl=0.0,
-    both=(0, 1, 1),
-    own=("RS", "RE", "RE"), far=("ER", "EE", "ER"),
-    gf=("S", "V", "S"),
-    gg=("VV", "VV", "VV"),
-    cs="S",
-    hold=(0, 4, 24),
-    early=(0, 0, 0),
-    passes=2, look=200.0,
-    swaps=3000, heat=0.0005, seed=0, mean=0.2, local=0.5, starts=24, kept=3, first=2000, meet=(0, 0, 0), block=0.03, span=20000.0, slow=(0.0, 200.0, 400.0), nxs=(0, 0, 0), wrap=("VV", "VV", "VV"), haste=(0.0, 0.0, 0.0), shake=1500.0, share=0.1,
-    CY=0.83, GA=1.55, SCA=3.8, PE=0.5, LAT=60.0, DL=1.4)
-PAIRS, LAST = "Pp0p2p4p6S", "Pp0ppppppS"
-PAR["plan"] = (tuple(((512, PAIRS), (512, PAIRS), (512, PAIRS), (w, LAST)) for w in (256, 256, 384, 384))
-               + (((512, PAIRS), (512, PAIRS), (512, PAIRS), (256, PAIRS), (256, "PpApCpEpGS")),) * 2)
-E4 = "Pp0p2p4peV"
-PAR.update(inflat=((0, 0), (0, 0), (0, 99999)), hold=(0, 0, 33), lead=(0.0, 20000.0, 20000.0), flead=(-5000.0, 0.0, 0.0), early=(0, 1, 1), swaps=12000, gg=("VHH", "SSS", "SSS"), sm=("bd", "cbdnx", "cbdnx"),
-           direct=(1, 0, 0), head=(256, 0, 0, 0, 0, 0), passes=1, heat=0.0003,
-           plan=(((1024, PAIRS), (512, PAIRS), (256, LAST)), ((1024, PAIRS), (512, E4), (256, E4)), ((512, PAIRS), (512, PAIRS), (512, PAIRS), (384, LAST)),
-                 ((512, PAIRS), (512, PAIRS), (512, E4), (384, E4))) + (((512, E4),) * 4,) * 2)
-PAR.update(plan=(((1024, PAIRS), (768, E4)), ((1024, PAIRS), (512, E4), (256, E4)), ((1024, E4), (896, E4)), ((1024, E4), (512, E4), (384, E4))) + (((512, E4),) * 4,) * 2,
-           gf="SSS", own=("RS", "RE", "RE"), far=("SR", "EE", "EE"), dq=("YY",) * 3, cutv=88, sm=("bd", "bdnx", "bdnx"), inflat=((2048, 16384), (0, 17408), (0, 99999)),
-           hold=(0, 0, 0), LAT=100.0, DL=1.25, lead=(0.0, 3000.0, 3000.0), starts=30, kept=4, first=2000, swaps=25000, heat=0.0004)
-PAR.update(plan=(((1024, PAIRS), (768, E4)), ((1024, PAIRS), (768, E4))) + PAR["plan"][2:], inflat=((4096, 18432), (3072, 19456), (2048, 99999)),
-           gg=("VHH", "SHH", "SHH"), starts=24, kept=6, first=4000, swaps=25000, heat=0.0008, DL=1.1, block=0.0, seed=1, span=30000.0, lead=(0.0, 6000.0, 6000.0))
-COSTS = (dict(CY=0.83, GA=1.45, SCA=3.5, PE=0.42, DL=1.2, LAT=80.0, OV=65.0), dict(CY=0.95, GA=1.15, SCA=2.5, PE=0.5, DL=1.0, LAT=120.0, OV=60.0),
-         dict(CY=1.04, GA=1.5, SCA=3.5, PE=0.52, DL=1.5, LAT=80.0, OV=75.0), dict(CY=1.15, GA=1.85, SCA=5.0, PE=0.58, DL=1.0, LAT=100.0, OV=60.0))
+    direct=(1, 1, 0),
+    early=(0, 0, 1),
+    own=("RS", "RS", "RE"), far=("SR", "EE", "EE"),
+    gd=("", "SSS", "SVS"),
+    gf="SVS",
+    gg=("HHH", "HSS", "SSS"),
+    sm=("bd", "fbdnxt", "fbdnxt"),
+    lead=(0.0, 15000.0, 10000.0),
+    flead=(-8000.0, 10000.0, 10000.0), glead=-8000.0,
+    keyed=3, tries=200, span=10000.0, weight=(1.3, 1.0, 0.5, 1.2), look=100.0, first=12, passes=82, wide=100, moves=300, heat=450.0, soft=1200.0, seed=7)
+COSTS = (dict(CY=0.83, GA=1.5, SCA=3.6, PE=0.42, DL=0.95, LAT=100.0, OV=52.0, RC=3000.0), dict(CY=0.92, GA=1.15, SCA=2.2, PE=0.48, DL=1.0, LAT=140.0, OV=55.0, RC=4500.0),
+         dict(CY=1.04, GA=1.5, SCA=3.0, PE=0.52, DL=1.4, LAT=80.0, OV=65.0, RC=3500.0), dict(CY=1.15, GA=1.85, SCA=5.0, PE=0.58, DL=1.0, LAT=100.0, OV=60.0, RC=2500.0))
 ORDER = {}
 SB = {
-    "flat": (16 * V, F), "ring": (RING, F), "ya": (V, F), "yb": (V, F), "xs": (V, B), "nb": (V, F), "nbp": (V, U),
-    "off": (V, U), "val": (1024, F), "ni": (832, I), "big": (8192, B), "mix": (4096, H), "r8": (1024, B),
+    "flat": (12 * V + RING, F), "ya": (V, F), "yb": (V, F), "xs": (V, B), "nb": (V, F), "nbp": (V, U),
+    "off": (V, U), "val": (1024, F), "ni": (832, I), "big": (6144 + WT, B), "mix": (4096, B), "gg": (1024, H), "eq": (1024, B),
+    "cf": (256, H), "s1": (288, F), "ee": (288, F), "r8": (1024, B),
     "xf": (384, B), "stall": (48, I), "p0": (48, U), "pr": (96, U), "ys": (128, F),
     "pi": (8, I), "col": (28, F), "ib": (128, B), "ibn": (128, B), "i3": (128, B), "iff": (128, F), "ifh": (128, F), "zb": (1152, B), "lam": (128, B),
-    "selc": (256, B), "sq": (640, B), "m17": (16, B), "b48": (48, B), "bp": (48, B), "bn": (48, B), "bp2": (48, B), "bn2": (48, B),
+    "selc": (256, B), "sq": (640, B), "m17": (8, B), "b48": (48, B), "bp": (48, B), "bn": (48, B), "bp2": (48, B), "bn2": (48, B),
     "bias": (384, B), "rf": (256, B), "rfs": (256, B), "rom": (256, B), "par": (256, B), "h2": (64, B),
-    "zero": (128, B), "ones": (128, B), "nones": (512, B), "dv": (128, H), "bc": (32, U), "pil": (112, U), "cw": (16, B),
-    "b8": (8, B), "b64": (8, B), "b64n": (8, B), "b128": (8, B), "kb": (288, B), "rst": (288, B), "dm": (144, B), "mt": (256, B), "negm": (128, B),
-    "d0": (256, B), "c16": (256, U), "nf": (288, B), "xx": (256, H),
+    "zero": (128, B), "ones": (128, B), "nones": (512, B), "dv": (384, H), "bc": (32, U), "pil": (112, U), "cw": (16, B),
+    "b8": (8, B), "b64": (8, B), "b64n": (8, B), "b128": (8, B), "kb": (144, B), "rst": (144, B), "dm": (144, B), "mt": (384, B), "negm": (128, B),
+    "d0": (768, B), "yy": (768, H), "c16": (256, U), "nf": (288, B), "xx": (256, H),
     "nbb": (128, H), "cq": (64, U), "fa": (128, U), "brep": (128, H), "nbrep": (128, H), "rl": (8, U),
     "dw": (256, B), "indp": (128, B), "fam": (256, H), "ot": (128, H), "o16": (64, U), "b16": (64, U), "wts": (128, B),
     "wrow": (128, B), "sl": (128, U), "thh": (128, H),
 }
-ALIAS = {"gw": ("big", 0, 1024), "ab": ("mix", 0, 1024), "xcq": ("mix", 1024, 1024), "gg": ("mix", 2048, 1024), "eq": ("mix", 3072, 1024), "iot": ("yb", 0, 256), "t1": ("yb", 256, 256), "t2": ("yb", 512, 256), "t3": ("yb", 768, 256),
-         "yy": ("xx", 0, 256), "nfx": ("thh", 0, 128), "rlx": ("ot", 0, 128), "mw": ("dw", 0, 256), "zz": ("fam", 0, 256),
-         "t4": ("yb", 1024, 256), "cf": ("fam", 0, 256), "s1": ("val", 256, 288), "ee": ("val", 544, 288),
-         "sc": ("big", 0, 2048), "rep": ("big", 2048, 2048), "wt": ("big", 4096, WT)}
+ALIAS = {"gw": ("big", 4096, 1024), "ab": ("mix", 0, 1024), "xcq": ("mix", 1024, 1024), "ring": ("flat", 16 * V, RING - 4 * V),
+         "iot": ("yb", 0, 256), "t1": ("yb", 256, 256), "t2": ("yb", 512, 256), "t3": ("yb", 768, 256), "t4": ("yb", 1024, 128),
+         "nfx": ("thh", 0, 128), "rlx": ("ot", 0, 128), "mw": ("dw", 0, 256), "zz": ("fam", 0, 256),
+         "sc": ("big", 6144, 2048), "rep": ("big", 4096, 2048), "wt": ("big", 6144, WT)}
 SCRATCH = dict((k, ("sbuf", [128, n], d)) for k, (n, d) in SB.items())
 SCRATCH["wz"] = ("dram", [128, WT], B)
 for _b in range(8):
@@ -99,8 +84,7 @@ def build(g, core, T, topo, costs):
     ops = []
     nsem = [0]
     vec, act, pe = g.vector, g.scalar, g.tensor
-    CY, GA, SCA, PE, DL = [costs[k] for k in ("CY", "GA", "SCA", "PE", "DL")]
-    OV = costs.get("OV", 55.0)
+    CY, GA, SCA, PE, DL, OV = [costs[k] for k in ("CY", "GA", "SCA", "PE", "DL", "OV")]
 
     def A(name, a=0, b=None, s=1, p=None):
         if name in ALIAS:
@@ -154,7 +138,19 @@ def build(g, core, T, topo, costs):
         return op("S", lambda: act.activation(out[0], a[0], f, **kw), cost(out, a, 1) + 15 + extra, [a] + list(k.values()), [out], after=after)
 
     def lin(out, a, m, c=0.0):
-        return ac(out, a, scale=m, bias=c) if PAR["cs"] == "S" else ts(out, a, m, AL.mult, c, AL.add)
+        return ac(out, a, scale=m, bias=c)
+
+    def either(e, s, v):
+        alt = ops.pop((v if e else s)())
+        i = (s if e else v)()
+        ops[i]["alt"] = alt
+        return i
+
+    def shift(e, out, a, m, c):
+        return either(e, lambda: lin(out, a, m, c), lambda: ts(out, a, m, AL.mult, c, AL.add))
+
+    def relu(out, a):
+        return either(False, lambda: ac(out, a, AF.Relu), lambda: ts(out, a, 0.0, AL.max))
 
     def mm(calls):
         def fn():
@@ -186,14 +182,14 @@ def build(g, core, T, topo, costs):
         a = A("ones", 0, out[4])
         return op("G", lambda: g.affine_select(out[0], a[0], pat, AL.is_equal, 0.0, base, 1), 190 + 2 * out[4] * CY, [a], [out])
 
-    def dma(eng, pairs, lat, xfer=100.0, **k):
+    def dma(eng, pairs, lat, xfer=100.0):
         sem = T.sem["d%d" % nsem[0]]
         nsem[0] += 1
         q = {"G": g, "Y": g.sync, "S": act}[eng]
 
         def fn():
             for o, i in pairs:
-                q.dma_start(ap(o), ap(i), **k).then_inc(sem, 16)
+                q.dma_start(ap(o), ap(i)).then_inc(sem, 16)
         j = op(eng, fn, (900 if eng == "G" else 70) * len(pairs) * DL, [i for o, i in pairs], [o for o, i in pairs if isinstance(o, tuple)],
                kind="d", lat=lat * DL, sem=sem, cnt=16 * len(pairs))
         ops[j]["xfer"] = xfer * len(pairs) * DL
@@ -218,16 +214,18 @@ def build(g, core, T, topo, costs):
     def row(s):
         return slice(s, 128, 16)
 
+    def FR(s):
+        return row(s % 8 if s < 8 else s - 8)
+
     Y0, Y1, Y2, Y3, D0, D1, KO, KF = ["ps%d" % i for i in range(8)]
-    TT = KF
     IB = A("ib")
     XV = lambda t, sd: A("xf", M * t, M * t + M) if sd else A("xs", V0 + M * t, V0 + M * t + M)
-    ST = lambda nm, t, sd: A(nm, 16 * t + 8 * sd, 16 * t + 8 * sd + 8)
+    ST = lambda nm, t, sd: A(nm, 8 * t + 24 * sd, 8 * t + 24 * sd + 8)
 
     ops[dma("Y", [(A("ni", 0, 104), T.nx0[0::8, :])], 2200)]["lead"] = 50000.0
     dma("S", [(A("ni", 416, 520), T.nx0[4::8, :])], 2200)
     dma("Y", [(A("ni", 104 * k, 104 * k + 104), T.nx0[k::8, :]) for k in (5, 1, 2, 3, 6, 7)], 3600)
-    dma("Y", [(ST("stall", t, 0), T.st[:, 8 * t:8 * t + 8]) for t in range(RO)], 2300)
+    dma("Y", [(A("stall", 0, 24), T.st[:])], 2300)
     dma("Y", [(A("xs"), T.x[:])], 3000)
     early = [iota(A("col", 0, 1), [[0, 1]], 0, 1), iota(A("pi", 0, 1), [[0, 1]], 0, 1), iota(A("iot"), [[1, 256]])]
     silu = ac(A("col", 17, 18), A("col", 0, 1), AF.Silu, extra=1400.0, scale=2.0, bias=V + OFF)
@@ -238,7 +236,7 @@ def build(g, core, T, topo, costs):
         ops[cp(A("nbp", 104 * a, 104 * b), A("ni", 104 * a, 104 * b))]["lead"] = 60000.0
     cv = PAR["cutv"]
     for k in range(8):
-        for a, b in (((0, 52), (52, 104)) if k % 4 == 0 else ((0, cv), (cv, 104)) if k == 3 and cv < 104 else ((0, 104),)):
+        for a, b in (((0, 52), (52, 104)) if k % 4 == 0 else ((0, cv), (cv, 104)) if k == 3 else ((0, 104),)):
             if (k, a) == (0, 52):
                 piece = len(ops) - 1
                 for c, d in ((5, 8), (1, 4)):
@@ -253,11 +251,11 @@ def build(g, core, T, topo, costs):
         ops[-1]["wr"] = [("nb%d" % (8 + k), 0, 1)]
         if k == 0:
             after = len(ops) - 2
-    cp(A("ring", 2048, 2048 + 832), A("ni"))
+    cp(A("val", 0, 832), A("ni"))
     ops[-1].update(lead=30000.0, after=[after])
-    dma("Y", [(A("nb", 0, V0, p=row(k)), A("ring", 2048 + 104 * k, 2152 + 104 * k)) for k in range(8)], 2500)
+    dma("Y", [(A("nb", 0, V0, p=row(k)), A("val", 104 * k, 104 * k + 104)) for k in range(8)], 2500)
     ops[-1]["wr"] = [("nb0", 0, 1)]
-    dma("Y", [(A("flat", k * V, k * V + V0, p=row(k)), A("ring", 2048 + 104 * k, 2152 + 104 * k)) for k in range(8)], 2500)
+    dma("Y", [(A("flat", k * V, k * V + V0, p=row(k)), A("val", 104 * k, 104 * k + 104)) for k in range(8)], 2500)
     NBS = [("nb%d" % s, 0, 1) for s in (0, 8, 9, 10, 11, 12, 13, 14, 15)]
 
     mk = start_masks(T, topo, rank)
@@ -268,7 +266,7 @@ def build(g, core, T, topo, costs):
             trs.append(RemoteDMATransfer(dst_ids=[DstId(rid=rid, pnc=pid)], dma_engine_mask=sum(1 << e for e in mk[t]), remote_sem=T.sem[name + str(t)],
                                          src=part(t, 0)[0], dst=part(t, 1)[0]))
         sent[0] += sum(len(m) for m in mk)
-        s = op("G", (lambda trs=trs: g.remote_dma_fused(trs, local_sem=T.sem.sent)), 2500, [part(t, 0) for t in range(RO)], [], kind="x", lat=3000.0)
+        s = op("G", (lambda trs=trs: g.remote_dma_fused(trs, local_sem=T.sem.sent)), costs["RC"], [part(t, 0) for t in range(RO)], [], kind="x", lat=3000.0)
         for t in range(RO):
             arrive(name + str(t), len(start_masks(T, topo, (rank - 1 - t) % n)[t]), part(t, 1), s)
     dma("G", [(A("ya", 0, V0), T.y0[:])], 4000)
@@ -296,35 +294,38 @@ def build(g, core, T, topo, costs):
     lin(SG, TOP, 2.0, -1.0)
     io = lambda w, a=0: A("iot", a, a + w)
     iota(A("ones"), [[0, 128]], 1)
-    iota(A("nones"), [[0, 512]], -1)
+    iota(A("t1", 0, 8), [[16, 8]])
+    iota(A("t4"), [[0, 8], [1, 16]])
+    iota(A("kb"), [[0, 8], [1, 18]])
+    iota(A("kb", 17, 144, 18), [[0, 8]], 1 << 20)
+    iota(A("m17"), [[0, 8]], -17)
+    iota(A("rst"), [[0, 144]])
+    iota(A("rst", 0, 144, 18), [[0, 8]], 1 << 23)
+    iota(A("nones", 0, 128), [[0, 128]], -1)
+    dma("Y", [(A("nones", c, c + 128), A("nones", 0, 128)) for c in (128, 256, 384)], 2500)
     lin(A("lam"), A("ones"), -0.5)
     ts(IB, io(128), P_, AL.is_equal)
     lin(A("ibn"), IB, -1.0)
     lin(A("i3"), IB, 3.0)
     lin(A("iff"), IB, 1.0)
     lin(A("ifh"), IB, 0.5)
-    iota(A("t1", 0, 8), [[16, 8]])
     ts(A("b8"), A("t1", 0, 8), GB, AL.is_equal)
     for nm, c in (("b64", 64.0), ("b64n", -64.0), ("b128", 128.0)):
         lin(A(nm), A("b8"), c)
-    iota(A("t4"), [[0, 16], [1, 16]])
-    ts(A("mt"), A("t4"), P16, AL.is_equal)
     MT = A("mt", 0, 128)
+    ts(MT, A("t4"), P16, AL.is_equal)
+    dma("Y", [(A("mt", c, c + 128), MT) for c in (128, 256)], 2500)
     lin(A("negm"), MT, 2.0 ** 98, -2.0 ** 98)
-    cp(A("bc", 0, 16), io(16))
-    ts(A("bc", 16, 32), io(16), 18.0, AL.mult, 17.0, AL.add)
-    iota(A("kb"), [[0, 16], [1, 18]])
-    iota(A("kb", 17, 288, 18), [[0, 16]], 1 << 20)
-    iota(A("m17"), [[0, 16]], -17)
-    iota(A("rst"), [[0, 288]])
-    iota(A("rst", 0, 288, 18), [[0, 16]], 1 << 23)
+    cp(A("bc", 0, 24), io(24))
+    ts(A("bc", 24, 32), io(8), 18.0, AL.mult, 17.0, AL.add)
     ts(A("t2", 0, 144), io(144), -2.0, AL.add, G18, AL.is_equal)
     ts(A("dm"), io(144), -1.0, AL.add, G18, AL.is_equal)
     tt(A("dm"), A("t2", 0, 144), A("dm"), AL.subtract)
-    iota(A("sq"), [[0, 640]])
+    op("V", lambda: vec.memset(A("wt")[0], 0.0), 45 + WT * 0.5 * CY, [], [A("wt")])
+    ops[-1]["lead"] = 90000.0
+    dma("Y", [(A(nm), A("wt", 0, A(nm)[4])) for nm in ("sq", "zb", "zero", "r8", "wz")], 2500)
     for q in range(4):
         pick(A("sq", 160 * q + 16 + 4 * q, 160 * q + 144 + 4 * q), [[-16, 8], [-1000, 4], [-1, 4]], -4 * q)
-    iota(A("zb"), [[0, 1152]])
     pick(A("zb", 0, 1152, 16), [[-1, 8], [-16, 9]], 8)
     for e in range(2):
         pick(A("rf", e, 256, 2), [[-1, 8], [-8, 2], [-16, 8]], 0)
@@ -342,7 +343,6 @@ def build(g, core, T, topo, costs):
     ts(A("par"), A("par"), P1, AL.is_equal)
     iota(A("bias", 0, 256), [[-1, 2], [0, 128]])
     lin(A("bias", 256, 384), A("par", 0, 128), 16384.0, -16384.0)
-    iota(A("zero"), [[0, 128]])
     iota(A("t2", 144, 208), [[1, 16], [256, 4]])
     iota(A("t2", 208, 256), [[1, 16], [256, 3]])
     ts(A("pil"), A("t2", 144, 256), P256, AL.add)
@@ -352,15 +352,19 @@ def build(g, core, T, topo, costs):
     op("V", lambda: vec.tensor_reduce(WC[0], A("t3", 0, 128)[0], AxisListType.X, AL.add), 200, [A("t3", 0, 128)], [WC])
     lin(TC, WC, 2.2)
     lin(A("cw"), A("ones", 0, 16), WC)
-    iota(A("r8"), [[16, 8], [0, 128]])
-    ts(A("r8"), A("r8"), GB, AL.is_equal)
+    dma("Y", [(A("r8", 128 * q, 128 * q + 128, p=slice(16 * q, 16 * q + 16)), A("ones", p=slice(16 * q, 16 * q + 16))) for q in range(8)], 2500)
     for k in range(8):
         pick(A("rom", 32 * k, 32 * k + 32), [[8, 2], [-16, 8], [0, 2]], -8 - k)
-    cp(A("p0"), A("stall"))
+    for sd in range(2):
+        cp(A("p0", 24 * sd, 24 * sd + 24), A("stall", 24 * sd, 24 * sd + 24))
+        d = A("d0", 384 * sd, 384 * sd + 384)
+        tt(d, IN(A("xs", 0, V0), A("p0", 24 * sd, 24 * sd + 24)), A("xf") if sd else A("xs", V0, V), AL.subtract)
+        ac(d, d, AF.Abs)
+        tt(A("yy", 384 * sd, 384 * sd + 384), IN(A("stall", 24 * sd, 24 * sd + 24), A("bc", 0, 24)), A("mt"), AL.mult)
+    for t in range(RO):
+        lin(C(20 + t), P_, 1.0, V0 + M * t - OFF)
+        shift("d" in PAR["sm"][t], A("dv", M * t, M * t + M), IB, C(20 + t), 1.0)
     iota(A("nb", V0, V), [[0, V - V0]], int(OFF))
-    op("V", lambda: vec.memset(A("wt")[0], 0.0), 45 + WT * 0.5 * CY, [], [A("wt")])
-    ops[-1]["lead"] = 90000.0
-    dma("Y", [(A("wz"), A("wt"))], 2500)
 
     xw = A("xs")
     SQ = lambda q, h: A("sq", 160 * q + 16 + 4 * q - 4 * h, 160 * q + 144 + 4 * q - 4 * h)
@@ -369,120 +373,111 @@ def build(g, core, T, topo, costs):
         ops[i]["rd"] += NBS
         return i
 
-    def search(t, sds, d0, d1, kb, ki):
+    def search(t, sd, d0, d1, kb):
         nbw = A("nb", 0, V0 + M * t)
-        lo, m = sds[0], len(sds)
-        io = 144 if m == 1 else 0
-        cs = lambda nm, sd=None: A(nm, 128 * lo, 128 * (lo + m)) if sd is None else A(nm, 128 * sd, 128 * sd + 128)
-        ks = lambda nm, a=0, s=1, sd=None: A(nm, 144 * lo + a, 144 * (lo + m), s) if sd is None else A(nm, 144 * sd + a, 144 * sd + 144, s)
-        big = lambda nm, sd, a, b, s=1: A("big", 4096 * sd + 2048 * (nm == "rep") + a, 4096 * sd + 2048 * (nm == "rep") + b, s)
-        for sd in sds:
-            for s in range(16):
-                gcopy(big("rep", sd, s, 2048, 16), XV(t, sd))
-            tt(cs("d0", sd), IN(A("xs", 0, V0), ST("p0", t, sd)), XV(t, sd), AL.subtract)
-        ac(cs("d0"), cs("d0"), AF.Abs)
-        p = A("p0", 16 * t + 8 * lo, 16 * t + 8 * (lo + m))
-        tt(cs("yy"), IN(A("stall", 16 * t + 8 * lo, 16 * t + 8 * (lo + m)), A("bc", 0, 8 * m)), A("mt", 0, 128 * m), AL.mult)
+        cs = lambda nm: A(nm, 128 * sd, 128 * sd + 128)
+        ks = lambda nm, a=0, s=1: A(nm, 144 * sd + a, 144 * sd + 144, s)
+        big = lambda nm, a, b, s=1: A("big", 4096 - 4096 * sd + 2048 * (nm == "sc") + a, 4096 - 4096 * sd + 2048 * (nm == "sc") + b, s)
+        at = lambda nm: A(nm, 384 * sd + M * t, 384 * sd + M * t + M)
+        for s in range(16):
+            gcopy(big("rep", s, 2048, 16), XV(t, sd))
+        p = ST("p0", t, sd)
         for h in range(2):
-            if "c" in PAR["sm"][t]:
-                nbg(ac(cs("cf"), IN(nbw, p), bias=TOFF))
-                ts(cs("c16"), cs("cf"), -OFF, AL.add)
-            elif "C" in PAR["sm"][t]:
-                nbg(ts(cs("cf"), IN(nbw, p), TOFF, AL.add))
+            if "cf"[sd] in PAR["sm"][t]:
+                nbg(shift(True, cs("cf"), IN(nbw, p), 1.0, TOFF))
                 ts(cs("c16"), cs("cf"), -OFF, AL.add)
             else:
                 nbg(ts(cs("c16"), IN(nbw, p), NOFF, AL.add))
-                nbg(ac(cs("cf"), IN(nbw, p), bias=TOFF))
-            for i, sd in enumerate(sds):
-                one = A(ki, io + 144 * i + 1, io + 144 * i + 144, 18)
-                grp([(A(ki, io + 144 * i, io + 144 * i + 144), cs("cf", sd), A("dm"))]
-                    + ([(one, cs("yy", sd), A("b8")), (one, MT, A("b64"))] if h == 0 else [(one, A("iff"), ks("ee", 17, 18, sd))]))
-            stay = [(A(kb, 144 * i, 144 * i + 144, 18), cs("d0", sd), A("b64")) for i, sd in enumerate(sds)] if h == 0 else [(A(kb, 0, 144 * m, 18), A("iff"), ks("s1", 17, 18)), (A(kb, 0, 144 * m, 18), IB, A("m17", 0, 8 * m))]
-            grp([(A(kb, 0, 144 * m), IB, A("kb", 0, 144 * m))] + stay, stop=False)
+                nbg(shift(True, cs("cf"), IN(nbw, p), 1.0, TOFF))
+            one = A(kb, 145, 288, 18)
+            grp([(A(kb, 144, 288), cs("cf"), A("dm"))] + ([(one, at("yy"), A("b8")), (one, MT, A("b64"))] if h == 0 else [(one, A("iff"), ks("ee", 17, 18))]))
+            stay = [(A(kb, 0, 144, 18), at("d0"), A("b64"))] if h == 0 else [(A(kb, 0, 144, 18), A("iff"), ks("s1", 17, 18)), (A(kb, 0, 144, 18), IB, A("m17"))]
+            grp([(A(kb, 0, 144), IB, A("kb"))] + stay, stop=False)
             last = []
-            for n, sd in enumerate(sds):
-                eng = PAR["far" if sd else "own"][t]
-                way = [eng[(2 * h + i) % len(eng)] for i in range(2)]
-                for hv in [[0], [1]] if (way[0] in "RE") != (way[1] in "RE") else [[0, 1]]:
-                    a, b = 1024 * hv[0], 1024 * hv[-1] + 1024
-                    sums = lambda w, stop, a=a, b=b, n=n, sd=sd: grp([(A(kb, 144 * n + 1 + s, 144 * n + 144, 18, p=slice(a // 16, b // 16)),
-                                                                       A("mix", 2048 * sd + a + s, 2048 * sd + b, 16) if w == "b128" and not lo else big("sc", sd, a + s, b, 16), A(w))
-                                                                      for s in range(16)], start=False, stop=stop)
-                    for i in hv:
-                        x, lst = big("sc", sd, 1024 * i, 1024 * i + 1024), IN(xw, A("c16", 128 * sd + 64 * i, 128 * sd + 64 * i + 64))
-                        if way[i] in "VR":
-                            tt(x, lst, big("rep", sd, 1024 * i, 1024 * i + 1024), AL.subtract)
-                        else:
-                            ac(x, lst, scale=-1.0)
-                        if way[i] in "DE":
-                            fold_dma(x, big("rep", sd, 1024 * i, 1024 * i + 1024))
-                        if way[i] in "VD":
-                            ac(x, x, AF.Abs)
-                        elif way[i] == "S":
-                            for u, bank in enumerate((d0, d1)):
-                                c = 1024 * i + 512 * u
-                                mm(acc(A(bank), [(IB, big("sc", sd, c, c + 512)), (IB, big("rep", sd, c, c + 512))]))
-                                ac(big("sc", sd, c, c + 512), A(bank), AF.Abs)
-                    if way[hv[0]] in "RE":
-                        sums("b64n", False)
-                        for u, v in ((a, b),) if way[hv[0]] == way[hv[-1]] else ((a, a + 1024), (a + 1024, b)):
-                            ts(big("sc", sd, u, v) if lo else A("mix", 2048 * sd + u, 2048 * sd + v), big("sc", sd, u, v), 0.0, AL.max)
-                    last.append((sums, "b128" if way[hv[0]] in "RE" else "b64", n == m - 1))
-            for sums, w, stop in last:
-                sums(w, stop)
-            scan(ks("s1"), A("rst", 0, 144 * m), A(kb, 0, 144 * m), 0.0, AL.add, AL.min)
-            tt(ks("nf"), ks("s1"), A(kb, 0, 144 * m), AL.not_equal)
-            scan(ks("ee"), A(ki, io, io + 144 * m), ks("nf"), 0.0, AL.add, AL.mult)
-            tt(cs("xx"), IN(ks("ee"), A("bc", 16, 16 + 8 * m)), A("mt", 0, 128 * m), AL.mult)
-            mm([(A(kb, 288 + 8 * i, 296 + 8 * i), cs("xx", sd), A("b8"), True, True) for i, sd in enumerate(sds)])
-            p = A("pr", 32 * t + 16 * h + 8 * lo, 32 * t + 16 * h + 8 * (lo + m))
-            ts(p, A(kb, 288, 288 + 8 * m), -OFF, AL.add)
-
-    def shift(e, out, a, m, c):
-        return ac(out, a, scale=m, bias=c) if e else ts(out, a, m, AL.mult, c, AL.add)
+            way = PAR["far" if sd else "own"][t]
+            for hv in [[0], [1]] if (way[0] == "S") != (way[1] == "S") else [[0, 1]]:
+                a, b = 1024 * hv[0], 1024 * hv[-1] + 1024
+                sums = lambda w, stop, a=a, b=b: grp([(A(kb, 1 + s, 144, 18, p=slice(a // 16, b // 16)),
+                                                       A("mix", a + s, b, 16) if w == "b128" and not sd else big("sc", a + s, b, 16), A(w))
+                                                      for s in range(16)], start=False, stop=stop)
+                for i in hv:
+                    x, lst = big("sc", 1024 * i, 1024 * i + 1024), IN(xw, A("c16", 128 * sd + 64 * i, 128 * sd + 64 * i + 64))
+                    if way[i] == "R":
+                        tt(x, lst, big("rep", 1024 * i, 1024 * i + 1024), AL.subtract)
+                    if way[i] == "E":
+                        shift(True, x, lst, -1.0, 0.0)
+                        fold_dma(x, big("rep", 1024 * i, 1024 * i + 1024))
+                    if way[i] == "S":
+                        for u, bank in enumerate((d0, d1)):
+                            c = 1024 * i + 512 * u
+                            shift(True, big("sc", c, c + 512), IN(xw, A("c16", 128 * sd + c // 16, 128 * sd + c // 16 + 32)), -1.0, 0.0)
+                            grp([(A(bank), IB, big("rep", c, c + 512))], stop=False)
+                            grp([(A(bank), IB, big("sc", c, c + 512))], start=False)
+                            ac(big("sc", c, c + 512), A(bank), AF.Abs)
+                if way[hv[0]] != "S":
+                    sums("b64n", False)
+                    for u, v in ((a, b),) if way[hv[0]] == way[hv[-1]] else ((a, a + 1024), (a + 1024, b)):
+                        relu(big("sc", u, v) if sd else A("mix", u, v), big("sc", u, v))
+                last.append((sums, "b64" if way[hv[0]] == "S" else "b128"))
+            for sums, w in last:
+                sums(w, True)
+            scan(ks("s1"), A("rst"), A(kb, 0, 144), 0.0, AL.add, AL.min)
+            tt(ks("nf"), ks("s1"), A(kb, 0, 144), AL.not_equal)
+            scan(ks("ee"), A(kb, 144, 288), ks("nf"), 0.0, AL.add, AL.mult)
+            tt(cs("xx"), IN(ks("ee"), A("bc", 24, 32)), MT, AL.mult)
+            mm([(A(kb, 288, 296), cs("xx"), A("b8"), True, True)])
+            p = A("pr", 32 * t + 16 * h + 8 * sd, 32 * t + 16 * h + 8 * sd + 8)
+            ts(p, A(kb, 288, 296), -OFF, AL.add)
 
     def nbrs(out, win, lst, e, off):
         for x, a, b in (("V", 0, 512), ("S", 512, 1024)) if e == "H" else ((e, 0, 1024),):
             shift(x == "S", A(out, a, b), IN(win, A(lst, a // 16, b // 16)), 1.0, off)
 
-    posf, posr = [PAR["s0"] * V], [0]
+    pos = [16 * V]
+
+    def room(w):
+        a = pos[0] if pos[0] + w <= 12 * V + RING else 12 * V
+        pos[0] = a + w
+        return a
+
     chain = {"V": [], "S": []}
-    made, mid = {"V": [], "S": []}, [0]
     for t in range(RO):
         old, have = V0 + M * t, V0 + M * (t + 1)
+        SEC = lambda s, t=t: V * (s - 4 if t and s >= 12 else s)
         nbw = A("nb", 0, old)
-        first = len(ops)
+        begun = len(ops)
         bl, pf = [A("pr", 32 * t + 16 + 8 * sd, 32 * t + 24 + 8 * sd) for sd in range(2)]
-        if PAR["both"][t]:
-            search(t, (0, 1), D0, D1, KO, KF)
-        else:
-            search(t, (1,), Y0, Y1, KF if t else Y3, KF if t else Y3)
-            for o in ops[first:]:
-                o["lead"] = PAR["flead"][t]
-            first = len(ops)
+        search(t, 1, Y0, Y1, KF if t else Y3)
+        for o in ops[begun:]:
+            o.update(lead=PAR["flead"][t], part=t)
+        first = len(ops)
         if PAR["early"][t]:
             shift("x" in PAR["sm"][t], A("xx", 128, 256), IN(nbw, pf), 1.0, TOFF)
             mm([c for z in range(2) for c in acc(A(KF, 296 + 64 * z, 360 + 64 * z), [(SQ(2 * z + u, 2 * h + u), A("xx", 128 + h, 256, 2)) for h in range(2) for u in range(2)])])
             ts(A("c16", 128, 256), A(KF, 296, 424), -OFF, AL.add)
-        if not PAR["both"][t]:
-            search(t, (0,), D0, D1, KO, KO)
+        search(t, 0, D0, D1, KO)
         iota(A("val", 0, 512), [[1, 128], [0, 4]], old + int(OFF))
-        VC = C(20 + t)
-        lin(VC, P_, 1.0, old - OFF)
-        shift("d" in PAR["sm"][t], A("dv"), IB, VC, 1.0)
-        wt = A("wt") if t else A("big", 6144, 8064)
+        DV = A("dv", M * t, M * t + M)
+        gd = PAR["gd"][t]
+        TT = D1 if t else KF
+        wt = A("wt") if t else A("big", 0, 1920)
         dma("Y", [(wt, A("wz", 0, wt[4]))], 2500)
         if t:
-            s0 = PAR["s0"] if PAR["inflat"][t - 1][1] else 16
-            dma("Y", [(A("flat", s * V + old - M, s * V + old, p=row(s)), A("nb", old - M, old, p=row(s))) for s in range(s0)], 2200, 50.0)
-            if s0 < 16:
-                dma("Y", [(A("flat", s * V, s * V + old, p=row(s)), A("nb", 0, old, p=row(s))) for s in range(s0, 16)], 1900 + 2.2 * old, 0.155 * old)
+            dma("Y", [(A("flat", SEC(s) + old - M, SEC(s) + old, p=FR(s)), A("nb", old - M, old, p=row(s))) for s in range(16) if s // 4 != 2 + t % 2], 2200, 50.0)
         XX = A("xx", 0, 128)
         shift("n" in PAR["sm"][t], A("nbb"), IN(nbw, bl), 1.0, TOFF)
         mm(acc(A(KO, 304, 368), [(A("selc", 128 * h, 128 * h + 128), A("nbb", h, 128, 2)) for h in range(2)]))
         ts(A("cq"), A(KO, 304, 368), -OFF, AL.add)
         nbrs("gg", nbw, "cq", PAR["gg"][t][0], TOFF)
-        ac(A("xcq"), IN(xw, A("cq")))
+        BC, BV, NG = (lambda a, b: A("rep", a, b)), (lambda a, b, s=1: A("mix", 2048 + a, 2048 + b, s)), (lambda a, b: A("mix", a, b))
+        if gd:
+            shift(gd[0] == "S", BC(0, 1024), IN(xw, A("cq")), 1.0, 0.0)
+            ops[gcopy(BC(1024, 2048), BC(0, 1024))].update(comm=False, urgent=True)
+            for k in range(8):
+                gcopy(BV(k, 1024, 8), XV(t, 0))
+            dma("Y", [(BV(1024, 2048), BV(0, 1024))], 2200, 500.0)
+        else:
+            shift(True, A("xcq"), IN(xw, A("cq")), 1.0, 0.0)
         GK = lambda k: A("gg", k, 1024, 8)
         RF = lambda nm, k, a, b, s=1: A(nm, 32 * k + a, 32 * k + b, s)
         mm([(A(KO, k, 256, 8), GK(k), RF("rf", k, 0, 32), True, True) for k in range(8)])
@@ -503,46 +498,53 @@ def build(g, core, T, topo, costs):
         grp([(A(D0, 0, 128), IB, A("negm"))] + [(A(D0, 16 * q, 16 * q + 16), EQ(q), A("cw")) for q in range(8)])
         ts(A("nfx"), A(D0, 0, 128), TC, AL.is_ge, JC if t else GB16, AL.mult)
         tt(A("rlx"), A("nfx"), XX, AL.max)
-        mm([(A(D1, 0, 8), A("rlx"), A("b8"), True, True)])
-        cp(A("rl"), A(D1, 0, 8))
-        grp([(A(TT, 0, 256), A("nbb"), A("selc")), (A(TT, 0, 256), A("dv"), A("nones", 0, 256))]
+        mm([(A(D1, 384, 392), A("rlx"), A("b8"), True, True)])
+        cp(A("rl"), A(D1, 384, 392))
+        grp([(A(TT, 0, 256), A("nbb"), A("selc")), (A(TT, 0, 256), DV, A("nones", 0, 256))]
             + [(A(TT, 120 * u + 8 + k, 128 * u + 128, 16), GK(k), RF("rf", k, 16 * u, 16 * u + 16, 2)) for k in range(8) for u in range(2)])
         mm([c for k in range(8) for c in acc(A(TT, 256 + k, 384, 8), [(GK(k), RF("rfs", k, 16 * u, 16 * u + 16)) for u in range(2)])])
         r8v = lambda a, b: A("rep", 2 * a, 2 * b, 2)
         keys = lambda nm, o, sg: [(A(KO, k, 384, 8), A(nm, o + k, o + 1024, 8), A(sg)) for k in range(8)]
-        far, both = PAR["gf"][t] == "S", PAR["gf"][t] == "B"
+        far = PAR["gf"][t] == "S" and not gd
         fl, al = IN(xw, A("fa", 0, 64)), IN(xw, A("fa", 64, 128))
         grp([(A(KO, 0, 384), IB, A("bias"))] + (keys("xcq", 0, "bp") + [(A(KO, k, 384, 8), XV(t, 0), A("bn")) for k in range(8)] if far else []), stop=False)
-        meet = dict((e, [made[e][mid[0] - PAR["meet"][t]]] if PAR["meet"][t] else []) for e in "VS")
         gains = len(ops)
-        def sizes(got, at, lst, to, after):
-            ac(A(got, at, at + 1024), lst, after=after)
-            for (o, c), sub in zip(to, (lambda u: A("xcq", 512 * u, 512 * u + 512), lambda u: r8v(512 * u, 512 * u + 512))):
-                for u, bank in enumerate((D0, D1)):
-                    mm(acc(A(bank), [(IB, A(got, at + 512 * u, at + 512 * u + 512)), (A("ibn"), sub(u))]))
-                    ac(A(o, c + 512 * u, c + 512 * u + 512), A(bank), AF.Abs)
-        if both:
-            sizes("sc", 1024, al, (("sc", 0), ("sc", 1024)), meet["S"])
+        if gd:
+            for u, lst in enumerate((fl, al)):
+                shift(gd[1 + u] == "S", NG(1024 * u, 1024 * u + 1024), lst, -1.0, 0.0)
+            parts = [(x, 1024 * u, 1024 * u + 1024) for u in range(2) for x in (BC, BV)]
+            for x, a, b in parts:
+                fold_dma(x(a, b), NG(a, b))
+            for x, a, b in parts:
+                relu(x(a, b), x(a, b))
+            for i, (nm, o, sg) in enumerate((("rep", 0, "bp"), ("mix", 2048, "bn"), ("rep", 1024, "bn"), ("mix", 3072, "bp"))):
+                grp(keys(nm, o, sg), start=False, stop=i == 3)
         else:
-            tt(A("sc", 1024, 2048), al, r8v(0, 1024), AL.max, after=[tt(A("sc", 0, 1024), al, A("xcq"), AL.max, after=meet["V"])])
-        if far or both:
-            sizes("ab", 0, fl, (("xcq", 0), ("ab", 0)), meet["S"])
-        else:
-            tt(A("ab"), fl, A("xcq"), AL.max)
-            tt(A("xcq"), fl, r8v(0, 1024), AL.max)
-        grp(keys("sc", 0, "bn2" if far else "bn"), start=False, stop=False)
-        grp(keys("sc", 1024, "bp2" if far else "bp"), start=False, stop=False)
-        grp(keys("xcq", 0, "bp" if far or both else "bn"), start=False, stop=False)
-        grp(keys("ab", 0, "bn" if far or both else "bp"), start=False)
+            tt(BV(1024, 2048), al, r8v(0, 1024), AL.max, after=[tt(BV(0, 1024), al, A("xcq"), AL.max)])
+            if far:
+                for u in range(2):
+                    ac(A("ab", 512 * u, 512 * u + 512), IN(xw, A("fa", 32 * u, 32 * u + 32)))
+                for o, sub in (("xcq", lambda u: A("xcq", 512 * u, 512 * u + 512)), ("ab", lambda u: r8v(512 * u, 512 * u + 512))):
+                    for u, bank in enumerate((D0, D0 if t else D1)):
+                        grp([(A(bank), A("ibn"), sub(u))], stop=False)
+                        grp([(A(bank), IB, A("ab", 512 * u, 512 * u + 512))], start=False)
+                        ac(A(o, 512 * u, 512 * u + 512), A(bank), AF.Abs)
+            else:
+                tt(A("ab"), fl, A("xcq"), AL.max)
+                tt(A("xcq"), fl, r8v(0, 1024), AL.max)
+            grp(keys("mix", 2048, "bn2" if far else "bn"), start=False, stop=False)
+            grp(keys("mix", 3072, "bp2" if far else "bp"), start=False, stop=False)
+            grp(keys("xcq", 0, "bp" if far else "bn"), start=False, stop=False)
+            grp(keys("ab", 0, "bn" if far else "bp"), start=False)
         ts(A("indp"), A(KO, 256, 384), 0.0, AL.is_ge)
         ts(A("dw"), A(KO, 0, 256), 0.0, AL.is_ge, WC, AL.mult)
         tt(A("ot"), A("indp"), A(TT, 256, 384), AL.mult)
         mm(acc(A(D0, 0, 64), [(A("fam", 128, 256), A("h2")), (A("ot"), A("h2"))]))
         ts(A("o16"), A(D0, 0, 64), -OFF, AL.add)
-        mm([(A(D1, 16 * q + 8 * z, 16 * q + 8 * z + 8), EQ(q), A("dw", 128 * z + 16 * q, 128 * z + 16 * q + 8), True, True) for q in range(8) for z in range(2)])
-        ac(A("wts"), A(D1, 0, 128))
-        mm([(A(D1, 128, 256), A("wts"), IB, True, True)])
-        ac(A("wrow"), A(D1, 128, 256))
+        mm([(A(D1, 384 + 16 * q + 8 * z, 392 + 16 * q + 8 * z), EQ(q), A("dw", 128 * z + 16 * q, 128 * z + 16 * q + 8), True, True) for q in range(8) for z in range(2)])
+        shift(True, A("wts"), A(D1, 384, 512), 1.0, 0.0)
+        mm([(A(D1, 384, 512), A("wts"), IB, True, True)])
+        shift(True, A("wrow"), A(D1, 384, 512), 1.0, 0.0)
         grp([(A(KO, 0, 256), A("zero"), A("nones", 0, 256))] + [(A(KO, 128 * z, 128 * z + 128), A("i3"), A("dw", 128 - 128 * z, 256 - 128 * z)) for z in range(2)]
             + [(A(KO, 16 * q, 16 * q + 16), EQ(q % 8), A("dw", 16 * q, 16 * q + 16)) for q in range(16)], stop=False)
         nbrs("gg", nbw, "o16", PAR["gg"][t][1], 0.0)
@@ -553,64 +555,66 @@ def build(g, core, T, topo, costs):
         grp([(A(KO, k, 256, 8), A("gw", k, 1024, 8), A("rom", 32 * k, 32 * k + 32)) for k in range(8)], start=False)
         ts(A("mw"), A(KO, 0, 256), TC, AL.is_lt)
         tt(A("zz"), A("mw"), A(TT, 0, 256), AL.mult)
-        mm(acc(A(D0, 128, 256), [(A("ones"), A("dv")), (A("zz", 0, 128), IB), (A("zz", 128, 256), IB)]))
+        mm(acc(A(D0, 128, 256), [(A("ones"), DV), (A("zz", 0, 128), IB), (A("zz", 128, 256), IB)]))
         shift("t" in PAR["sm"][t], A("thh"), A(D0, 128, 256), 1.0, -OFF)
         mm([c for q in range(4) for c in acc(A(D1, 32 * q, 32 * q + 32), [(SQ(q, h), A("thh", h, 128, 4)) for h in range(4)])])
         ts(A("sl"), A(D1, 0, 128), SV, AL.add)
-        hold = dict((e, made[e][-PAR["hold"][t]:][:1] if PAR["hold"][t] else []) for e in "VS")
-        for q in range(2):
-            ops[ts(IN(A("flat", 4 * q * V, 4 * q * V + 4 * V), A("sl", 32 * q, 32 * q + 32)), A("val", 0, 512), 1.0, AL.mult, -OFF, AL.add)]["after"] = hold["V"]
-            ac(IN(A("flat", (8 + 4 * q) * V, (12 + 4 * q) * V), A("sl", 64 + 32 * q, 96 + 32 * q)), A("val", 0, 512), AF.Silu, after=hold["S"])
-        nbg(mm(acc(A(D0, 256, 384), [(SQ(q, (q + 2) % 4), A("thh")) for q in range(4)])))
-        ac(A("nb", old, have), A(D0, 256, 384), bias=BOFF)
-        W = (64, 48 if have == 1792 else 64)
         direct = PAR["direct"][t]
-        if direct:
-            at = lambda s: 512 * (s % 8 < 4) + 256 * (s // 8) + 64 * (s % 4)
-            for z, ks in enumerate(((0,), (1, 2, 3), (4, 5, 6, 7))):
-                dma(PAR["dq"][t][z % 2], [(A("val", at(s), at(s) + 64), A("flat", s * V, s * V + 1024, p=row(s))) for k in ks for s in (8 + k, k)], 1900 + 400 * len(ks), 160.0)
-                for u in (8, 0):
-                    ts(A("off", 64 * (u + ks[0]), 64 * (u + ks[-1] + 1)), A("val", at(u + ks[0]), at(u + ks[-1]) + 64), -OFF if u else 0.0, AL.add)
+        back = lambda ss, a, b: ops[dma("Y", [(A("nb", a, b, p=row(s)), A("flat", SEC(s) + a, SEC(s) + b, p=FR(s))) for s in ss],
+                                        1900 + (0.275 if len(ss) > 4 else 0.2) * len(ss) * (b - a), 0.155 * (b - a))].update(comm=True)
+        at = lambda s: 512 * (s % 8 < 4) + 256 * (s // 8) + 64 * (s % 4)
+        for q in range(2):
+            ts(IN(A("flat", 4 * q * V, 4 * q * V + 4 * V), A("sl", 32 * q, 32 * q + 32)), A("val", 0, 512), 1.0, AL.mult, -OFF, AL.add)
+            u = 1 - q if t == 2 else q
+            ss = range(8 + 4 * u, 12 + 4 * u)
+            w = IN(A("flat", SEC(ss[0]), SEC(ss[0]) + 4 * V), A("sl", 64 + 32 * u, 96 + 32 * u))
+            j = either(True, lambda: ac(w, A("val", 0, 512), AF.Silu), lambda: cp(w, A("val", 0, 512)))
+            for ks in (((0,), (1, 2, 3)), ((4, 5, 6, 7),))[q] if direct else ():
+                dma("Y", [(A("val", at(s), at(s) + 64), A("flat", SEC(s), SEC(s) + 1024, p=FR(s))) for k in ks for s in (8 + k, k)], 1900 + 400 * len(ks), 160.0)
+                for z in (8, 0):
+                    ts(A("off", 64 * (z + ks[0]), 64 * (z + ks[-1] + 1)), A("val", at(z + ks[0]), at(z + ks[-1]) + 64), -OFF if z else 0.0, AL.add)
+            if t and q:
+                ops[j]["rd"].append(("turn", 0, 1))
+            elif t:
+                back(ss, 0, old)
+                i = dma("Y", [(A("flat", SEC(s), SEC(s) + old, p=FR(s)), A("nb", 0, old, p=row(s))) for s in range(12 - 4 * u, 16 - 4 * u)], 1900 + 0.8 * old, 0.155 * old)
+                ops[i].update(wr=[("turn", 0, 1)], rd=[], hard=[j])
+        nbg(mm(acc(A(D0, 256, 384), [(SQ(q, (q + 2) % 4), A("thh")) for q in range(4)])))
+        shift(True, A("nb", old, have), A(D0, 256, 384), 1.0, BOFF)
+        W = (64, 48 if have == 1792 else 64)
         for a, b in ((0, 1024), (1024, old))[::-1 if direct else 1]:
-            for z in range(2):
-                dma(PAR["dq"][t][z], [(A("nb", a, b, p=row(s)), A("flat", s * V + a, s * V + b, p=row(s))) for s in range(8 * z, 8 * z + 8)], 1900 + 2.2 * (b - a), 0.155 * (b - a))
-                ops[-1]["comm"] = True
+            back(range(8), a, b)
+            back(ss if t else range(8, 16), a, b)
         for r in range(direct, 2):
             a, w, l = 1024 * r, W[r], (0 if W[r] == 64 else 64)
-            if PAR["wrap"][t][r] == "S":
-                ac(A("mix", 2048 + a, 2048 + a + 16 * w), IN(A("nb", a, a + 16 * w), A("pil", l, l + w)), bias=NOFF)
-                cp(A("nbp", a, a + 16 * w), A("mix", 2048 + a, 2048 + a + 16 * w))
-            else:
-                ts(A("nbp", a, a + 16 * w), IN(A("nb", a, a + 16 * w), A("pil", l, l + w)), NOFF, AL.add)
-            ops[-1]["after"] = made["V"][-PAR["holdw"][t]:][:1] if r and PAR["holdw"][t] else []
-            for z, ks in enumerate(((0,), (1, 2), (3, 4), (5, 6, 7)) if r == 0 else ((0, 1, 2, 3), (4, 5, 6, 7))):
-                dma(PAR["dq"][t][z % 2], [(A("off", a + w * s, a + w * s + w), A("nbp", a, a + 16 * w, p=row(s))) for k in ks for s in (8 + k, k)], 1900 + 250 * len(ks))
+            ts(A("nbp", a, a + 16 * w), IN(A("nb", a, a + 16 * w), A("pil", l, l + w)), NOFF, AL.add)
+            for ks in ((0,), (1, 2), (3, 4), (5, 6, 7)) if r == 0 else ((0, 1, 2, 3), (4, 5, 6, 7)):
+                dma("Y", [(A("off", a + w * s, a + w * s + w), A("nbp", a, a + 16 * w, p=row(s))) for k in ks for s in (8 + k, k)], 1900 + 250 * len(ks))
         OL = lambda s, a, b: A("off", (a - a % 1024) + W[a // 1024] * s + a % 1024 // 16, (a - a % 1024) + W[a // 1024] * s + (b - a + a % 1024) // 16)
-        for o in ops[first:]:
-            o["lead"] = PAR["lead"][t]
-            o["round"] = t
-        for o in ops[first:gains]:
-            o["lead"] += PAR["haste"][t]
+        for i in range(first, len(ops)):
+            ops[i].update(lead=PAR["lead"][t], round=t, part=(4 if i < gains else 2) + t if t else -1)
+        for o in ops[begun:]:
+            if t and o["eng"] == "G" and o["kind"] == "c" and "urgent" not in o:
+                o.update(lead=PAR["glead"], part=7)
         if t + 1 == RO:
             dma("Y", [(T.nx[k::8, :], A("nb", p=row(k))) for k in range(8)], 3000)
         if PAR["early"][t]:
             yw = A("yb", 0, old)
-            ac(A("ys"), IN(yw, pf), scale=0.5)
-            ac(A("val"), IN(yw, A("c16", 192, 256)), scale=-0.0625)
-            tt(A("val"), IN(yw, A("c16", 128, 192)), A("val"), AL.mult)
-            mm(acc(A(D0, 0, 128), [(A("iff"), A("ys"))] + [(A("iff"), A("val", k, 1024, 8)) for k in range(8)]))
-            ac(A("ys"), A(D0, 0, 128), bias=0.5)
+            shift(True, A("ys"), IN(yw, pf), 0.5, 0.0)
+            c = room(1024)
+            shift(True, A("flat", c, c + 1024), IN(yw, A("c16", 192, 256)), -0.0625, 0.0)
+            tt(A("flat", c, c + 1024), IN(yw, A("c16", 128, 192)), A("flat", c, c + 1024), AL.mult)
+            mm(acc(A(KF, 0, 128), [(A("iff"), A("ys"))] + [(A("iff"), A("flat", c + k, c + 1024, 8)) for k in range(8)]))
+            shift(True, A("ys"), A(KF, 0, 128), 1.0, 0.5)
         else:
-            ac(A("ys"), IN(A("ya", 0, old), pf))
+            shift(True, A("ys"), IN(A("ya", 0, old), pf), 1.0, 0.0)
         to = T.cores[(rank - 1 - t) % n]
         rid, pid, _ = topo.addr(to)
         sent[0] += len(topo.engines(core, to))
         s = op("G", (lambda a=A("ya", old, have)[0], rid=rid, pid=pid, m=topo.mask(core, to), t=t:
                      g.remote_dma(a, A("ys")[0], T.sem["ay%d" % t], T.sem.sent, pid, rid, m)), 1500, [A("ys")], [], kind="x", sem=T.sem.sent, cnt=sent[0], lat=2500.0)
         arrive("ay%d" % t, len(topo.engines(T.cores[(rank + 1 + t) % n], core)), A("ya", old, have), s)
-        nch = 0
         for sw in range(2):
-            mid[0] = len(made["V"])
             src, dst = ("ya", "yb") if sw == 0 else ("yb", "ya")
             yw = A(src, 0, have)
             chunks, a = [], 0
@@ -637,12 +641,10 @@ def build(g, core, T, topo, costs):
                     ops[j]["grp"] = b["ops"][0]
                 b["ops"].append(j)
 
-            nl = PAR["late"][2 * t + sw]
-            late = [ci for ci, c in enumerate(chunks) if c[2][8] in "el"]
+            late = [ci for ci, c in enumerate(chunks) if c[2][8] == "e"]
             places = [[] for c in chunks]
-            for ci, ks in [(ci, range(8 - nl if ci in late else 8)) for ci in range(len(chunks))] + [(ci, (k,)) for k in range(8 - nl, 8) for ci in late]:
+            for ci, ks in [(ci, range(7 if ci in late else 8)) for ci in range(len(chunks))] + [(ci, (7,)) for ci in late]:
                 a, b, plan = chunks[ci]
-                w = b - a
                 parts = [(q, max(a, 512 * q), min(b, 512 * q + 512)) for q in range(a // 512, (b + 511) // 512)]
                 for q, lo, hi in parts if ks[0] == 0 else []:
                     if q not in banks:
@@ -654,50 +656,36 @@ def build(g, core, T, topo, costs):
                         term(q, 512 * q, top, A("ifh"), A(src, 512 * q, top))
                 place = places[ci]
                 for k in ks:
-                    rn, r0, rw, pos = ("flat", PAR["s0"] * V, 16 * V, posf) if PAR["inflat"][t][0] <= nch < PAR["inflat"][t][1] else ("ring", 0, RING, posr)
-                    nch += w
-                    if pos[0] + w > rw:
-                        pos[0] = r0
-                    place.append((rn, pos[0]))
-                    pos[0] += w
+                    place.append((dst, 1024 * k) if t == sw == ci == 0 and k < 2 else ("flat", room(b - a)))
                     pr = lambda i, lo=a, hi=b: A(place[i][0], place[i][1] + lo - a, place[i][1] + hi - a)
                     hd = PAR["head"][2 * t + sw] if ci == 0 and k == 0 else 0
                     for lo, hi in ((a, a + hd), (a + hd, b)) if hd else ((a, b),):
                         chain["S"] = [ac(pr(k, lo, hi), IN(yw, OL(8 + k, lo, hi)), after=chain["S"], scale=-0.0625)]
                         chain["V"] = [tt(pr(k, lo, hi), IN(yw, OL(k, lo, hi)), pr(k, lo, hi), AL.mult, after=chain["V"])]
                     ops[chain["S"][0]]["cut"] = ci == 0 and k == 0
-                    made["S"] += chain["S"]
-                    made["V"] += chain["V"]
-                    c = plan[k + 1]
-                    if c.isdigit():
-                        fold_dma(pr(int(c)), pr(k))
-                    elif c in "ABCDEFG":
-                        chain["V"] = [tt(pr(k), pr(k), pr(ord(c) - 65), AL.add, after=chain["V"])]
+                    if plan[k + 1].isdigit():
+                        fold_dma(pr(int(plan[k + 1])), pr(k))
                     for i in range(k + 1):
-                        mine = plan[i + 1] not in "e01234567" and chr(65 + i) not in plan[1:9]
-                        if mine and max(i, plan.rfind(str(i), 1, 9) - 1) == k:
+                        if plan[i + 1] == "p" and max(i, plan.rfind(str(i), 1, 9) - 1) == k:
                             for q, lo, hi in parts:
                                 term(q, lo, hi, A("iff"), pr(i) if direct and ci == 0 else pr(i, lo, hi), direct and ci == 0)
                 for q, lo, hi in parts if ks[-1] == 7 else []:
-                    banks[q]["ev"].append((lo, hi, plan[9], pr(7, lo, hi) if plan[8] == "e" else A(src, lo, hi)))
-                    if len(banks[q]["ev"]) == len(over(q)):
-                        ev = sorted(banks[q]["ev"], key=lambda e: e[0])
-                        if all(e[2] == ev[0][2] != "V" for e in ev):
-                            ev = [(ev[0][0], ev[-1][1], ev[0][2], None)]
-                        for lo, hi, e, more in ev:
+                    cut = hi - PAR["end"] if (t, sw, hi) == (RO - 1, 1, V) else hi
+                    banks[q]["ev"] += [(u, v, plan[9], pr(7, u, v)) for u, v in ((lo, cut), (cut, hi)) if u < v]
+                    if len(banks[q]["ev"]) >= len(over(q)):
+                        for lo, hi, e, more in sorted(banks[q]["ev"], key=lambda e: e[0]):
                             bk = A((Y0, Y1, Y2, Y3)[q], lo - 512 * q, hi - 512 * q)
                             if e != "V":
                                 shift(e == "S", A(dst, lo, hi), bk, 1.0, 0.5 - banks[q]["mu"])
                             else:
                                 tt(A(dst, lo, hi), bk, more, AL.add)
-                            ops[-1].update(lead=PAR["evl"], hard=list(banks[q]["ops"]))
+                            ops[-1]["hard"] = list(banks[q]["ops"])
                             if t == RO - 1 and sw == 1:
                                 dma("Y", [(T.y[:, lo:hi], A(dst, lo, hi))], 2000 + 1.0 * (hi - lo))
     return ops, sent[0]
 
 
-def schedule(ops, other):
-    LAT = PAR["LAT"]
+def depend(ops):
     hist = {}
     for i, o in enumerate(ops):
         deps = set(o["after"])
@@ -709,7 +697,7 @@ def schedule(ops, other):
                         continue
                     if nm[:2] == "ps" and o.get("grp", -1) == ops[j].get("grp", -2):
                         continue
-                    if j != i and ((nm[:2] == "ps" and (ops[j]["eng"] != o["eng"] or o["eng"] == "P")) or ((w or w2) and a < b2 and a2 < b)):
+                    if j != i and ((nm[:2] == "ps" and (ops[j]["eng"] != o["eng"] or o["eng"] == "P" or "alt" in o or "alt" in ops[j])) or ((w or w2) and a < b2 and a2 < b)):
                         deps.add(j)
                         soft.discard(j)
                         if "fold" in ops[j] and w2 and "cons" not in ops[j]:
@@ -739,258 +727,236 @@ def schedule(ops, other):
         o["known"] = known | sum(1 << j for j in deps if j not in soft and not o["eng"] == ops[j]["eng"] == "P")
         o["done"] = o["known"] | done | 1 << i
         o["deps"], o["soft"] = sorted(deps), soft
+
+
+def schedule(ops, other):
+    n, K = len(ops), range(len(other))
+    num = ["VSPGYR".index(o["eng"]) for o in ops]
+    link = [[(j, 0.0 if num[j] == num[i] and (num[i] == 2 or j in o["soft"]) else 1.0) for j in o["deps"]] for i, o in enumerate(ops)]
     succ = [[] for _ in ops]
-    for i, o in enumerate(ops):
-        for j in o["deps"]:
-            succ[j].append(i)
-    eng = [o["eng"] for o in ops]
-    link = [[(j, 0.0 if eng[j] == eng[i] and (eng[i] == "P" or j in o["soft"]) else 1.0) for j in o["deps"]] for i, o in enumerate(ops)]
+    for i, b in enumerate(link):
+        for j, h in b:
+            succ[j].append((i, h))
+    pre = [set(o["deps"]) for o in ops]
+    call = [[(num[i], [(j, c[3] * h) for j, h in b], c[0][i], c[1][i], c[2][i]) for i, b in enumerate(link)] for c in other]
+    rnd = np.random.RandomState(PAR["seed"])
+    home = num[:]
 
-    def begin(dur, lat, wake, lead, slow, look):
-        pre = [[(j, lat[j] + wake * h) for j, h in b] for b in link]
-        post = [[] for _ in ops]
-        for i, b in enumerate(pre):
-            for j, w in b:
-                post[j].append((i, w))
-        bl = [0.0] * len(ops)
-        for i in range(len(ops) - 1, -1, -1):
-            bl[i] = max([bl[j] + wake for j in succ[i]] + [0.0]) + dur[i] + lat[i] + (slow if ops[i].get("round") and eng[i] in "VS" else 0.0)
-        key = [bl[i] + o.get("lead", 0.0) + lead[o.get("round", 0)] for i, o in enumerate(ops)]
-        left = [len(b) for b in link]
-        rdy, end = [0.0] * len(ops), [0.0] * len(ops)
-        free = dict((e, 0.0) for e in "VSPGYR")
-        ready = dict((e, [i for i in range(len(ops)) if not left[i] and eng[i] == e]) for e in "VSPGYR")
-        for _ in ops:
-            now, e = min((max(free[e], min(rdy[i] for i in ready[e])), e) for e in ready if ready[e])
-            i = max((i for i in ready[e] if rdy[i] <= now + look), key=lambda i: (key[i], -i))
-            ready[e].remove(i)
-            end[i] = free[e] = max(now, rdy[i]) + dur[i]
-            for j, w in post[i]:
-                rdy[j] = max(rdy[j], end[i] + w)
-                left[j] -= 1
-                if not left[j]:
-                    ready[eng[j]].append(j)
-        back = place(rank([-x for x in end], post, pre), post, dur, lat)
-        end = place(rank([-x for x in back], pre, post), pre, dur, None)
-        seq = sorted(range(len(ops)), key=lambda i: (end[i], i))
-        end = run(seq, other[0])
-        at = [end[i] - other[0][1][i] - other[0][0][i] if eng[i] != "Y" else max([end[j] for j, _ in link[i]] + [0.0]) for i in range(len(ops))]
-        return rank(at, pre, post)
+    def flip(i):
+        num[i] = 1 - num[i]
+        for k in K:
+            call[k][i] = (num[i], call[k][i][1], other[k][0 if num[i] == home[i] else 4][i], 0.0, 0.0)
 
-    def place(seq, before, dur, tail):
-        busy = dict((e, ([], [])) for e in "VSPGYR")
-        end = [0.0] * len(ops)
-        for i in seq:
-            d = dur[i]
-            t = max([end[j] + w for j, w in before[i]] + [tail[i] if tail else 0.0])
-            st, en = busy[eng[i]]
-            k = len(st)
-            while k and en[k - 1] > t:
-                k -= 1
-            while k < len(st) and st[k] < t + d:
-                t = max(t, en[k])
-                k += 1
-            st.insert(k, t)
-            en.insert(k, t + d)
-            end[i] = t + d
-        return end
+    def assign(engines):
+        for i in range(n):
+            if num[i] != engines[i]:
+                flip(i)
 
-    def rank(key, before, behind):
-        wait = [len(b) for b in before]
-        top = list(key)
-        out = sorted((i for i in range(len(ops)) if not wait[i]), key=lambda i: key[i])
-        for i in out:
-            for j, _ in behind[i]:
-                top[j] = max(top[j], top[i])
-                wait[j] -= 1
-                if not wait[j]:
-                    out.append(j)
-        pos = dict((i, n) for n, i in enumerate(out))
-        return sorted(out, key=lambda i: (top[i], pos[i]))
+    def play(part, k, state, end):
+        free, cl = list(state), call[k]
+        for i in part:
+            e, ln, dur, lat, xfer = cl[i]
+            t = free[e]
+            for j, w in ln:
+                if end[j] + w > t:
+                    t = end[j] + w
+            free[e] = t = t + dur
+            if lat:
+                t += lat
+                if xfer:
+                    free[6] = t = max(t, min(free[6], t + 4000.0) + xfer)
+            end[i] = t
+        return free
 
-    def length(seq):
-        return sum(math.log(max(run(seq, c))) for c in other)
+    def length(seq, engines):
+        assign(engines)
+        x = 0.0
+        for k in K:
+            end = [0.0] * n
+            play(seq, k, [0.0] * 7, end)
+            x += math.log(max(end)) * PAR["weight"][k]
+        return x
 
-    def run(seq, c, why=None):
+    def listed(c, key):
         dur, lat, xfer, wake = c
-        free = dict((e, 0.0) for e in "VSPGYR")
-        last = dict((e, -1) for e in "VSPGYR")
-        end = [0.0] * len(ops)
-        moved = 0.0
-        for i in seq:
-            e = eng[i]
-            t, w = free[e], last[e]
-            for j, hard in link[i]:
-                if end[j] + wake * hard >= t:
-                    t, w = end[j] + wake * hard, -2 - j
-            free[e] = t = t + dur[i]
+        left, rdy, free, moved, seq = [len(b) for b in link], [0.0] * n, [0.0] * 6, 0.0, []
+        ready = [[i for i in range(n) if not left[i] and num[i] == e] for e in range(6)]
+        first = [0.0 if r else 1e18 for r in ready]
+        for _ in ops:
+            now, e = min((max(first[x], free[x]), x) for x in range(6))
+            i = max((i for i in ready[e] if rdy[i] <= now + PAR["look"]), key=lambda i: key[i])
+            ready[e].remove(i)
+            first[e] = min([rdy[j] for j in ready[e]] + [1e18])
+            t = free[e] = max(now, rdy[i]) + dur[i]
             t += lat[i]
             if xfer[i]:
                 moved = t = max(t, min(moved, t + 4000.0) + xfer[i])
-            end[i] = t
-            last[e] = i
-            if why is not None:
-                why[i] = w
-        return end
+            seq.append(i)
+            for j, h in succ[i]:
+                rdy[j] = max(rdy[j], t + wake * h)
+                left[j] -= 1
+                if not left[j]:
+                    ready[num[j]].append(j)
+                    first[num[j]] = min(first[num[j]], rdy[j])
+        return seq
 
-    rnd = np.random.RandomState(PAR["seed"])
-    starts = []
-    for n in range(PAR["starts"]):
-        mix = rnd.dirichlet([1.0] * len(other))
-        dur, lat = [[float(x) for x in sum(m * np.array(c[k]) for m, c in zip(mix, other))] for k in range(2)]
-        lat = [x * PAR["DL"] for x in lat]
-        seq = begin(dur, lat, LAT, [0.0] + [float(x) for x in PAR["span"] * (rnd.rand(2) - 0.5)], float(rnd.choice(PAR["slow"])), float(rnd.choice((100.0, 200.0))))
-        starts.append((length(seq), n, seq))
-    starts = [s[2] for s in sorted(starts)]
-    num = ["VSPGYR".index(e) for e in eng]
-    tied = [[[(j, c[3] * hard) for j, hard in b] for b in link] for c in other]
-    STEP = 32
+    def keyed():
+        c = rnd.dirichlet([4.0] * len(other))
+        c = [[float(x) for x in sum(m * np.array(y[k]) for m, y in zip(c, other))] for k in range(3)] + [100.0]
+        bl = [0.0] * n
+        for i in range(n - 1, -1, -1):
+            bl[i] = max([bl[j] + c[3] * h for j, h in succ[i]] + [0.0]) + c[0][i] + c[1][i]
+        now = 1e9
+        for m in range(PAR["tries"]):
+            if m < PAR["tries"] // 8:
+                lead = dict((p, PAR["span"] * (rnd.rand() - 0.5)) for p in range(8))
+                new = [bl[i] + o.get("lead", 0.0) + lead.get(o.get("part"), 0.0) for i, o in enumerate(ops)]
+            else:
+                a, w, d = rnd.randint(n), int(rnd.choice((1, 4, 10, 30, 80))), float(rnd.choice((1000, 3000, 10000)) * rnd.randn())
+                e = num[a] if rnd.rand() < 0.5 else -1
+                new = key[:a] + [x + d if e in (-1, num[a + i]) else x for i, x in enumerate(key[a:a + w])] + key[a + w:]
+            seq = listed(c, new)
+            x = length(seq, home)
+            if x <= now:
+                key, now, keep = new, x, seq
+        return keep, home
 
-    def rerun(seq, k, start, old, stop=99999):
-        dur, lat, xfer, _ = other[k]
-        m = start // STEP
-        end, marks, ln = old[0][:], old[1][:m + 1], tied[k]
-        free = list(marks[m])
-        for a in range(m * STEP, len(seq), STEP):
-            for i in seq[a:a + STEP]:
-                e = num[i]
-                t = free[e]
-                for j, w in ln[i]:
-                    if end[j] + w > t:
-                        t = end[j] + w
-                free[e] = t = t + dur[i]
-                t += lat[i]
-                if xfer[i]:
-                    free[6] = t = max(t, min(free[6], t + 4000.0) + xfer[i])
-                if t > free[7]:
-                    free[7] = t
-                free[8] += t
-                end[i] = t
-            marks.append(tuple(free))
-            if a >= stop and a + STEP < len(seq):
-                was = old[1][len(marks) - 1]
-                d, ago = free[0] - was[0], min(free[0], was[0]) - 7000.0
-                if (all(abs(free[e] - was[e] - d) < 1.0 or max(free[e], was[e]) < ago for e in (1, 2, 3, 4, 6))
-                        and all(abs(end[i] - old[0][i] - d) < 1.0 or max(end[i], old[0][i]) < ago for i in seq[max(0, a - 2 * STEP):a + STEP])):
-                    last = old[1][-1]
-                    return None, [last[:7] + (last[7] + d, last[8] - was[8] + free[8] + d * (len(seq) - a - STEP))]
-        return end, marks
+    def polish(start, passes):
+        W, tau = PAR["wide"], PAR["soft"]
+        seq, best = start[0], 1e18
+        assign(start[1])
+        for p in range(passes + 1):
+            free, end, at = [0.0] * 7, [0.0] * n, [0.0] * n
+            for i in seq:
+                free = play((i,), p % len(other), free, end)
+                at[i] = free[num[i]] - call[p % len(other)][i][2]
+            seq = sorted(seq, key=lambda i: at[i])
+            ends, tails, total = [[0.0] * n for k in K], [], []
+            for k in K:
+                free, eff, tail, nxt = [0.0] * 7, [0.0] * n, [0.0] * n, [0.0] * 6
+                for i in seq:
+                    free = play((i,), k, free, ends[k])
+                    eff[i] = ends[k][i] - free[num[i]]
+                for i in seq[::-1]:
+                    t = eff[i] + max([other[k][3] * h + tail[j] for j, h in succ[i]] + [0.0])
+                    tail[i] = nxt[num[i]] = call[k][i][2] + max(t, nxt[num[i]])
+                tails.append(tail)
+                total.append(max(ends[k]))
+            x = sum(math.log(t) * w for t, w in zip(total, PAR["weight"]))
+            if x < best:
+                best, keep = x, (seq, num[:])
+            if p == passes:
+                return keep
+            warm = PAR["heat"] * (1.0 - p / passes) ** 2
+            state, a, skew = [[0.0] * 7 for k in K], 0, int(rnd.randint(W // 2))
+            while a < n - 4:
+                b = min(n, (a or -skew) + W)
+                part = seq[a:b]
+                m, inside, behind, outs = len(part), set(part), {}, []
+                for i in seq[b:b + 400]:
+                    behind.setdefault(num[i], i)
+                for k in K:
+                    o = [(i, max([other[k][3] * h + tails[k][j] for j, h in succ[i] if j not in inside] + [0.0]) - total[k]) for i in part]
+                    outs.append(([x for x in o if ends[k][x[0]] + x[1] > -9000.0], [(e, tails[k][j] - total[k]) for e, j in behind.items()]))
+
+                def worth(part, k, v, marks):
+                    end, marks = ends[k], marks[:v // 8 + 1]
+                    for c in range(v // 8 * 8, m, 8):
+                        marks.append(play(part[c:c + 8], k, marks[-1], end))
+                    z = 1e-9 + sum([math.exp((end[i] + t) / tau) for i, t in outs[k][0]]) + sum([math.exp((marks[-1][e] + t) / tau) for e, t in outs[k][1]])
+                    return tau * math.log(z) * 2.6e5 / total[k] * PAR["weight"][k], marks
+
+                now = [worth(part, k, 0, [state[k]]) for k in K]
+                old = [[ends[k][i] for i in part] for k in K]
+                c = PAR["moves"]
+                for u, way, far, luck in zip(rnd.randint(m, size=c).tolist(), rnd.rand(c).tolist(), rnd.choice((1, 1, 1, 2, 2, 3, 5), size=c).tolist(), rnd.rand(c).tolist()):
+                    e, v, d = num[part[u]], u, -1 if way < 0.5 else 1
+                    turn = part[u] if far == 5 and other[0][4][part[u]] else -1
+                    while far and 0 <= v + d < m and turn < 0:
+                        v += d
+                        far -= num[part[v]] == e
+                    if turn >= 0:
+                        flip(turn)
+                        along, new = [], part
+                    elif num[part[v]] != e or v == u:
+                        continue
+                    elif d < 0:
+                        need, along, rest = set(pre[part[u]]), [part[u]], []
+                        for i in part[u - 1:v - 1 if v else None:-1]:
+                            if i in need:
+                                along.append(i)
+                                need |= pre[i]
+                            else:
+                                rest.append(i)
+                        new = part[:v] + along[::-1] + rest[::-1] + part[u + 1:]
+                    else:
+                        need, along, rest = {part[u]}, [part[u]], []
+                        for i in part[u + 1:v + 1]:
+                            if pre[i] & need:
+                                along.append(i)
+                                need.add(i)
+                            else:
+                                rest.append(i)
+                        new = part[:u] + rest + along + part[v + 1:]
+                    if part[v] in along:
+                        continue
+                    v, trial, d = min(u, v), [], 0.0
+                    for k in K:
+                        trial.append(worth(new, k, v, now[k][1]))
+                        d += trial[k][0] - now[k][0]
+                        if d > warm * luck + 100.0 * (len(other) - 1 - k):
+                            break
+                    if d <= warm * luck:
+                        part, now = new, trial
+                        old = [[ends[k][i] for i in part] for k in K]
+                    else:
+                        if turn >= 0:
+                            flip(turn)
+                        v = v // 8 * 8
+                        for k in range(len(trial)):
+                            for i, t in zip(part[v:], old[k][v:]):
+                                ends[k][i] = t
+                seq = seq[:a] + part + seq[b:]
+                c = b - W + W // 2 if b < n else n
+                state = [play(seq[a:c], k, state[k], ends[k]) for k in K]
+                a = c
 
     def cross(seqs):
         cuts = [i for i, o in enumerate(ops) if o.get("cut")]
-        back = [[(j, 0.0) for j in s] for s in succ]
-        best, top = seqs[0], length(seqs[0])
+        best, top = seqs[0], length(*seqs[0])
         for c in cuts[::-1] + cuts:
             for s in seqs:
                 for a, b in ((best, s), (s, best)):
-                    pa, pb = dict((i, k) for k, i in enumerate(a)), dict((i, k) for k, i in enumerate(b))
-                    new = rank([pa[i] if pa[i] < pa[c] else len(ops) + pb[i] for i in range(len(ops))], link, back)
-                    x = length(new)
+                    head = a[0][:a[0].index(c)]
+                    done = set(head)
+                    new = (head + [i for i in b[0] if i not in done], [(a if i in done else b)[1][i] for i in range(n)])
+                    x = length(*new)
                     if x < top:
                         best, top = new, x
         return best
 
-    starts = [cross(starts[k::PAR["kept"]]) for k in range(PAR["kept"])]
-
-    back = [[(j, 0.0) for j in s] for s in succ]
-    whole_ops = [i for i, o in enumerate(ops) if "round" in o]
-    worth = lambda x: math.log(x[1][-1][7]) + PAR["mean"] * math.log(x[1][-1][8])
-    stages = [PAR["first"]] * len(starts) + [PAR["swaps"]]
-    found, left = [], 0
-    for n in range(sum(stages) + 1):
-        if not left:
-            if n:
-                found.append((top, len(found), keep))
-            if len(found) == len(stages):
-                break
-            seq = keep = starts[len(found)] if len(found) < len(starts) else cross([f[2] for f in sorted(found)])
-            left = span = stages[len(found)]
-            state = [rerun(seq, k, 0, ([0.0] * len(ops), [(0.0,) * 9])) for k in range(len(other))]
-            now, top, fresh = sum(worth(x) for x in state), sum(math.log(x[1][-1][7]) for x in state), True
-        left -= 1
-        if n % 24 == 0 or fresh:
-            why, c = {}, other[rnd.randint(len(other))]
-            end = run(seq, c, why)
-            pos = dict((i, k) for k, i in enumerate(seq))
-            idle = [i for i in seq if why[i] < -1 and eng[i] in "VS"]
-            i, whole = max(range(len(ops)), key=lambda i: end[i]), []
-            while why[i] != -1:
-                if why[i] >= 0:
-                    whole.append((why[i], i))
-                i = why[i] if why[i] >= 0 else -2 - why[i]
-        fresh, arcs = False, whole
-        if rnd.rand() < PAR["block"]:
-            a = whole_ops[rnd.randint(len(whole_ops))]
-            b, d = a + int(rnd.choice((4, 10, 25, 60))), float(rnd.choice((-1, 1)) * rnd.choice((4, 10, 20, 40)))
-            new = rank([pos[i] + (d + 0.5 if a <= i < b and "round" in ops[i] else 0.0) for i in range(len(ops))], link, back)
-            trial = [rerun(new, k, 0, state[k]) for k in range(len(other))]
-            if sum(worth(y) for y in trial) <= now + PAR["heat"] * left / span * rnd.rand():
-                seq, now, fresh, state = new, sum(worth(y) for y in trial), True, trial
-            continue
-        if rnd.rand() < PAR["local"]:
-            i, arcs = idle[rnd.randint(len(idle))], []
-            stop = end[i] - 12000.0
-            while why[i] != -1 and end[i] > stop:
-                if why[i] >= 0:
-                    arcs.append((why[i], i))
-                i = why[i] if why[i] >= 0 else -2 - why[i]
-        if not arcs:
-            continue
-        a, b = arcs[rnd.randint(len(arcs))]
-        way = rnd.randint(3)
-        if way < 2:
-            line = [i for i in seq[max(0, pos[a] - 40):pos[a] + 1] if eng[i] == eng[a]]
-            a = line[max(0, len(line) - 1 - int(rnd.choice((0, 0, 0, 1, 2, 4))))]
-        else:
-            line = [i for i in seq[pos[b]:pos[b] + 40] if eng[i] == eng[b]]
-            b = line[min(len(line) - 1, int(rnd.choice((0, 0, 0, 1, 2, 4))))]
-        part = seq[pos[a]:pos[b] + 1]
-        if way < 2:
-            up, first = {b}, {eng[b]: False}
-            for i in part[-2::-1]:
-                if (way == 0 and first.get(eng[i])) or any(j in up for j in succ[i]):
-                    up.add(i)
-                    first[eng[i]] = True
-        else:
-            down = {a}
-            for i in part[1:]:
-                if any(j in down for j, _ in link[i]):
-                    down.add(i)
-            up = set(part) - down
-        if a in up or b not in up:
-            continue
-        new = seq[:pos[a]] + [i for i in part if i in up] + [i for i in part if i not in up] + seq[pos[b] + 1:]
-        trial, x = [], now
-        for k in range(len(other)):
-            trial.append(rerun(new, k, pos[a], state[k], pos[b]))
-            x += worth(trial[k]) - worth(state[k])
-            if x > now + 4 * PAR["heat"]:
-                break
-        if x <= now + PAR["heat"] * left / span * rnd.rand():
-            state = [y if y[0] else rerun(new, k, pos[a], state[k]) for k, y in enumerate(trial)]
-            seq, now, fresh = new, sum(worth(y) for y in state), True
-            x = sum(math.log(y[1][-1][7]) for y in state)
-            if x < top:
-                top, keep = x, new
-    seq = keep
-    return dict((e, [i for i in seq if ops[i]["eng"] == e]) for e in "VSPGYR")
+    found = []
+    for _ in range(PAR["keyed"]):
+        assign(home)
+        found.append(polish(keyed(), PAR["first"]))
+    seq, engines = polish(cross(found), PAR["passes"])
+    return dict((e, [i for i in seq if engines[i] == x]) for x, e in enumerate("VSPGYR"))
 
 
 def rank_program(g, core, T, topo):
     if T.rank_of(core) is None:
         return
-    ops, sent = build(g, core, T, topo, PAR)
-    other = []
-    for c in COSTS:
-        alt = build(g, core, T, topo, c)[0]
-        other.append(([o["dur"] for o in alt], [o["lat"] for o in alt], [o.get("xfer", 0.0) for o in alt], c["LAT"]))
-    key = repr(sorted(PAR.items()))
-    if key not in ORDER:
-        ORDER.clear()
-        ORDER[key] = (schedule(ops, other), [(o["deps"], o["soft"]) for o in ops])
-    order = ORDER[key][0]
-    for o, (d, s) in zip(ops, ORDER[key][1]):
-        o["deps"], o["soft"] = d, s
+    ops, sent = build(g, core, T, topo, COSTS[0])
+    depend(ops)
+    if not ORDER:
+        alts = [build(g, core, T, topo, c)[0] for c in COSTS]
+        ORDER.update(schedule(ops, [([o["dur"] for o in alt], [o["lat"] for o in alt], [o.get("xfer", 0.0) for o in alt], c["LAT"],
+                                     [o["alt"]["dur"] if "alt" in o else 0.0 for o in alt]) for alt, c in zip(alts, COSTS)]))
+    order = ORDER
+    for e in "VS":
+        for i in order[e]:
+            if ops[i]["eng"] != e:
+                ops[i].update(eng=e, fn=ops[i]["alt"]["fn"])
     total = {}
     for e in "VSPG":
         c = 0
@@ -1002,30 +968,39 @@ def rank_program(g, core, T, topo):
     for i, o in enumerate(ops):
         if o["kind"] != "c":
             o["key"] = "sent" if o["kind"] == "x" else o.get("key", i)
-    seen = {}
+    knows, place, waited, left = dict((e, {}) for e in order), dict((e, 0) for e in order), {}, len(ops)
+    while left:
+        for e in order:
+            while place[e] < len(order[e]) and all("knew" in ops[j] for j in ops[order[e][place[e]]]["deps"]):
+                o, know = ops[order[e][place[e]]], knows[e]
+                o["waits"] = []
+                for j in o["deps"][::-1] if e != "R" else ():
+                    d = ops[j]
+                    if j in o["soft"] or (e == "P" and d["eng"] == "P") or d["cnt"] <= know.get(d["key"], 0):
+                        continue
+                    o["waits"] = [w for w in o["waits"] if w[2] != d["key"]] + [(d["sem"], d["cnt"], d["key"])]
+                    for k, c in d["knew"].items():
+                        know[k] = max(know.get(k, 0), c)
+                for s, c, k in o["waits"]:
+                    waited[k] = max(waited.get(k, 0), c)
+                o["knew"] = dict(know)
+                o["knew"][o["key"]] = max(o["cnt"], know.get(o["key"], 0))
+                place[e] += 1
+                left -= 1
     for e, q in (("V", g.vector), ("S", g.scalar), ("P", g.tensor), ("Y", g.sync), ("G", g)):
-        seen = {}
         for i in order[e]:
             o = ops[i]
-            need = {}
-            for j in o["deps"]:
-                d = ops[j]
-                if j in o["soft"] or (e == "P" and d["eng"] == "P"):
-                    continue
-                if d["cnt"] > max(seen.get(d["key"], 0), need.get(d["key"], (0, None))[0]):
-                    need[d["key"]] = (d["cnt"], d["sem"])
-            for k, (c, s) in need.items():
+            for s, c, k in o["waits"]:
                 q.wait_ge(s, c)
-                seen[k] = c
             r = o["fn"]()
             if o["kind"] == "c":
                 r.then_inc(o["sem"], 1)
-    for e in "VSPG":
-        if total[e] > seen.get(e, 0):
-            g.wait_ge(T.sem["c" + e], total[e])
-    for o in ops[::-1]:
-        if o["kind"] in "dr" and o["cnt"] > seen.get(o["key"], 0):
-            g.wait_ge(o["sem"], o["cnt"])
-            seen[o["key"]] = o["cnt"]
-    if sent > seen.get("sent", 0):
+    last = dict((o["key"], o) for o in ops if o["kind"] in "dr")
+    if sent > waited.get("sent", 0):
         g.wait_ge(T.sem.sent, sent)
+    for e in "GPSV":
+        if total[e] > waited.get(e, 0):
+            g.wait_ge(T.sem["c" + e], total[e])
+    for o in last.values():
+        if o["cnt"] > waited.get(o["key"], 0):
+            g.wait_ge(o["sem"], o["cnt"])

import math
import numpy as np
from concourse.bass import DstId, RemoteDMATransfer
from concourse.mybir import AluOpType, AxisListType, ActivationFunctionType

AL = AluOpType
AF = ActivationFunctionType
V0, M, RO, V = 1664, 128, 3, 2048
H = "float16"
F, B, I, U = "float32", "bfloat16", "int32", "uint16"
OFF = 64.0
RING = 10752
WT = 2368
NF = 52
PAIRS, PV, E4, EL = "Pp0p2p4p6S", "Pp0p2p4p6v", "Pp0p2p4peV", "Pp0p2pppeV"
PAR = dict(
    plan=(((1024, PV), (768, E4)), ((1024, PAIRS), (768, EL)), ((1024, PV), (896, E4)), ((1024, PAIRS), (896, EL)),
          ((512, E4),) * 4, ((512, E4),) * 4),
    head=(256,) * 6,
    end=128,
    cutv=88,
    direct=(1, 1, 0),
    early=(0, 0, 1),
    own=("RS", "RS", "RE"), far=("SR", "EE", "EE"),
    gd=("", "SSS", "SVS"),
    gf="SVS",
    gg=("HHH", "HSS", "SSS"),
    sm=("bd", "fbdnxt", "fbdnxt"),
    lead=(0.0, 15000.0, 10000.0),
    flead=(-8000.0, 10000.0, 10000.0), glead=-8000.0,
    keyed=3, tries=200, span=10000.0, weight=(1.3, 1.0, 0.5, 1.2), look=100.0, first=12, passes=82, wide=100, moves=300, heat=450.0, soft=1200.0, seed=7)
COSTS = (dict(CY=0.83, GA=1.5, SCA=3.6, PE=0.42, DL=0.95, LAT=100.0, OV=52.0, RC=3000.0), dict(CY=0.92, GA=1.15, SCA=2.2, PE=0.48, DL=1.0, LAT=140.0, OV=55.0, RC=4500.0),
         dict(CY=1.04, GA=1.5, SCA=3.0, PE=0.52, DL=1.4, LAT=80.0, OV=65.0, RC=3500.0), dict(CY=1.15, GA=1.85, SCA=5.0, PE=0.58, DL=1.0, LAT=100.0, OV=60.0, RC=2500.0))
ORDER = {}
SB = {
    "flat": (12 * V + RING, F), "ya": (V, F), "yb": (V, F), "xs": (V, B), "nb": (V, F), "nbp": (V, U),
    "off": (V, U), "val": (1024, F), "ni": (832, I), "big": (6144 + WT, B), "mix": (4096, B), "gg": (1024, H), "eq": (1024, B),
    "cf": (256, H), "s1": (288, F), "ee": (288, F), "r8": (1024, B),
    "xf": (384, B), "stall": (48, I), "p0": (48, U), "pr": (96, U), "ys": (128, F),
    "pi": (8, I), "col": (28, F), "ib": (128, B), "ibn": (128, B), "i3": (128, B), "iff": (128, F), "ifh": (128, F), "zb": (1152, B), "lam": (128, B),
    "selc": (256, B), "sq": (640, B), "m17": (8, B), "b48": (48, B), "bp": (48, B), "bn": (48, B), "bp2": (48, B), "bn2": (48, B),
    "bias": (384, B), "rf": (256, B), "rfs": (256, B), "rom": (256, B), "par": (256, B), "h2": (64, B),
    "zero": (128, B), "ones": (128, B), "nones": (512, B), "dv": (384, H), "bc": (32, U), "pil": (112, U), "cw": (16, B),
    "b8": (8, B), "b64": (8, B), "b64n": (8, B), "b128": (8, B), "kb": (144, B), "rst": (144, B), "dm": (144, B), "mt": (384, B), "negm": (128, B),
    "d0": (768, B), "yy": (768, H), "c16": (256, U), "nf": (288, B), "xx": (256, H),
    "nbb": (128, H), "cq": (64, U), "fa": (128, U), "brep": (128, H), "nbrep": (128, H), "rl": (8, U),
    "dw": (256, B), "indp": (128, B), "fam": (256, H), "ot": (128, H), "o16": (64, U), "b16": (64, U), "wts": (128, B),
    "wrow": (128, B), "sl": (128, U), "thh": (128, H),
}
ALIAS = {"gw": ("big", 4096, 1024), "ab": ("mix", 0, 1024), "xcq": ("mix", 1024, 1024), "ring": ("flat", 16 * V, RING - 4 * V),
         "iot": ("yb", 0, 256), "t1": ("yb", 256, 256), "t2": ("yb", 512, 256), "t3": ("yb", 768, 256), "t4": ("yb", 1024, 128),
         "nfx": ("thh", 0, 128), "rlx": ("ot", 0, 128), "mw": ("dw", 0, 256), "zz": ("fam", 0, 256),
         "sc": ("big", 6144, 2048), "rep": ("big", 4096, 2048), "wt": ("big", 6144, WT)}
SCRATCH = dict((k, ("sbuf", [128, n], d)) for k, (n, d) in SB.items())
SCRATCH["wz"] = ("dram", [128, WT], B)
for _b in range(8):
    SCRATCH["ps%d" % _b] = ("psum", [128, 512], F)
SEMAPHORES = ["cV", "cS", "cP", "cG", "sent"] + ["d%d" % i for i in range(82)] + ["f%d" % i for i in range(NF)] + [k + str(t) for k in ("ax", "as", "ay") for t in range(RO)]


def start_masks(T, topo, rank):
    me = T.cores[rank]
    eng = [topo.engines(me, T.cores[(rank + 1 + t) % len(T.cores)]) for t in range(RO)]
    least = min(len(e) for e in eng)
    narrow = [t for t in range(RO) if len(eng[t]) == least]
    share = 1
    while share * 2 * len(narrow) <= least:
        share *= 2
    used, out = [], [None] * RO
    for t in narrow + [t for t in range(RO) if t not in narrow]:
        free = [e for e in eng[t] if e not in used]
        n = share
        if t not in narrow:
            while n * 2 <= len(free):
                n *= 2
        out[t] = free[:n]
        used += out[t]
    return out


def build(g, core, T, topo, costs):
    rank = T.rank_of(core)
    n = len(T.cores)
    ops = []
    nsem = [0]
    vec, act, pe = g.vector, g.scalar, g.tensor
    CY, GA, SCA, PE, DL, OV = [costs[k] for k in ("CY", "GA", "SCA", "PE", "DL", "OV")]

    def A(name, a=0, b=None, s=1, p=None):
        if name in ALIAS:
            name, o, w = ALIAS[name]
            a, b = a + o, (w if b is None else b) + o
        t = T[name]
        b = SCRATCH[name][1][1] if b is None else b
        cs = slice(a, b, s) if s > 1 else slice(a, b)
        return (t[slice(None) if p is None else p, cs], name, a, b, (b - a + s - 1) // s)

    def IN(win, off):
        return (win[0].indirect(off[0]), win[1], win[2], win[3], win[4], off)

    def op(eng, fn, dur, rd, wr, kind="c", lat=0.0, sem=None, cnt=0, after=()):
        r = [x[1:4] for x in rd if isinstance(x, tuple)] + [x[5][1:4] for x in list(rd) + list(wr) if isinstance(x, tuple) and len(x) > 5]
        ops.append(dict(eng=eng, fn=fn, dur=dur, rd=sorted(set(r)), wr=sorted(set(x[1:4] for x in wr)), kind=kind, lat=lat, sem=sem, cnt=cnt, after=list(after)))
        return len(ops) - 1

    def two(*xs):
        return all(SCRATCH[x[1]][2] in (B, H, U) for x in xs)

    def cost(out, a, per):
        if len(out) > 5:
            return OV + 16 * out[5][4] * SCA * CY
        if len(a) > 5:
            return OV + out[4] * GA * CY
        return OV + max(64, out[4] * per) * CY

    def ap(x):
        return x[0] if isinstance(x, tuple) else x

    def cp(out, a):
        return op("V", lambda: vec.tensor_copy(out[0], a[0]), cost(out, a, .5 if two(out, a) else 1), [a], [out])

    def tt(out, a, b, o, **k):
        per = 1 if (a[1][:2] == "ps" or b[1][:2] == "ps") else 2
        return op("V", lambda: vec.tensor_tensor(out[0], a[0], b[0], o), cost(out, a, per), [a, b], [out], **k)

    def ts(out, a, s1, o1, s2=None, o2=None):
        if o2 is None:
            fn = lambda: vec.tensor_scalar(out[0], a[0], ap(s1), None, o1)
        else:
            fn = lambda: vec.tensor_scalar(out[0], a[0], ap(s1), ap(s2), o1, o2)
        return op("V", fn, cost(out, a, .5 if two(out, a) else 1), [a, s1, s2], [out])

    def scan(out, a, b, first, o0, o1):
        return op("V", lambda: vec.tensor_tensor_scan(out[0], a[0], b[0], first, o0, o1), cost(out, a, 1), [a, b], [out])

    def ac(out, a, f=AF.Identity, extra=0.0, after=(), **k):
        kw = dict((x, ap(y)) for x, y in k.items())
        return op("S", lambda: act.activation(out[0], a[0], f, **kw), cost(out, a, 1) + 15 + extra, [a] + list(k.values()), [out], after=after)

    def lin(out, a, m, c=0.0):
        return ac(out, a, scale=m, bias=c)

    def either(e, s, v):
        alt = ops.pop((v if e else s)())
        i = (s if e else v)()
        ops[i]["alt"] = alt
        return i

    def shift(e, out, a, m, c):
        return either(e, lambda: lin(out, a, m, c), lambda: ts(out, a, m, AL.mult, c, AL.add))

    def relu(out, a):
        return either(False, lambda: ac(out, a, AF.Relu), lambda: ts(out, a, 0.0, AL.max))

    def mm(calls):
        def fn():
            for c in calls:
                r = pe.matmul(c[0][0], c[1][0], c[2][0], c[3], c[4])
            return r
        d = 60 + sum(max(64, c[2][4]) * (4 if SB[c[2][1]][1] == F else 1) * PE for c in calls)
        return op("P", fn, d, [x for c in calls for x in c[1:3]], [c[0] for c in calls])

    def acc(out, pairs):
        return [(out, l, r, i == 0, i == len(pairs) - 1) for i, (l, r) in enumerate(pairs)]

    def grp(calls, start=True, stop=True):
        return mm([c + (start and i == 0, stop and i == len(calls) - 1) for i, c in enumerate(calls)])

    def iota(out, pat, base=0, cm=0):
        if SB[out[1]][1] == I:
            fn = lambda: g.iota(out[0], pat, base, cm)
        else:
            fn = lambda: g.iota(out[0], pat, base, cm, allow_small_or_imprecise_dtypes=True)
        return op("G", fn, 150 + 2 * out[4] * CY, [], [out])

    def gcopy(out, a):
        i = op("G", lambda: g.affine_select(out[0], a[0], [[0, a[4]]], AL.is_equal, 0.0, 0, 0), 190 + 2 * out[4] * CY, [a], [out])
        ops[i]["comm"] = True
        return i

    def pick(out, pat, base):
        a = A("ones", 0, out[4])
        return op("G", lambda: g.affine_select(out[0], a[0], pat, AL.is_equal, 0.0, base, 1), 190 + 2 * out[4] * CY, [a], [out])

    def dma(eng, pairs, lat, xfer=100.0):
        sem = T.sem["d%d" % nsem[0]]
        nsem[0] += 1
        q = {"G": g, "Y": g.sync, "S": act}[eng]

        def fn():
            for o, i in pairs:
                q.dma_start(ap(o), ap(i)).then_inc(sem, 16)
        j = op(eng, fn, (900 if eng == "G" else 70) * len(pairs) * DL, [i for o, i in pairs], [o for o, i in pairs if isinstance(o, tuple)],
               kind="d", lat=lat * DL, sem=sem, cnt=16 * len(pairs))
        ops[j]["xfer"] = xfer * len(pairs) * DL
        return j

    folds = []

    def fold_dma(out, a):
        i = len(folds)
        sem = T.sem["f%d" % (i % NF)]
        x = (100 + (0.85 if two(out) else 1.7) * out[4]) * DL
        op("G", lambda: g.dma_start(out[0], a[0], accum_op=AL.add).then_inc(sem, 16), 900 * DL, [a, out], [out], kind="d",
           lat=1700 * DL + x, sem=sem, cnt=16 * (i // NF + 1))
        ops[-1].update(xfer=x, key="f%d" % (i % NF), fold=folds[i - NF] if i >= NF else -1)
        folds.append(len(ops) - 1)

    sent = [0]

    def arrive(name, cnt, reg, after):
        return op("R", None, 0.0, [], [reg], kind="r", lat=1000.0 * DL, sem=T.sem[name], cnt=cnt, after=[after])

    def row(s):
        return slice(s, 128, 16)

    def FR(s):
        return row(s % 8 if s < 8 else s - 8)

    Y0, Y1, Y2, Y3, D0, D1, KO, KF = ["ps%d" % i for i in range(8)]
    IB = A("ib")
    XV = lambda t, sd: A("xf", M * t, M * t + M) if sd else A("xs", V0 + M * t, V0 + M * t + M)
    ST = lambda nm, t, sd: A(nm, 8 * t + 24 * sd, 8 * t + 24 * sd + 8)

    ops[dma("Y", [(A("ni", 0, 104), T.nx0[0::8, :])], 2200)]["lead"] = 50000.0
    dma("S", [(A("ni", 416, 520), T.nx0[4::8, :])], 2200)
    dma("Y", [(A("ni", 104 * k, 104 * k + 104), T.nx0[k::8, :]) for k in (5, 1, 2, 3, 6, 7)], 3600)
    dma("Y", [(A("stall", 0, 24), T.st[:])], 2300)
    dma("Y", [(A("xs"), T.x[:])], 3000)
    early = [iota(A("col", 0, 1), [[0, 1]], 0, 1), iota(A("pi", 0, 1), [[0, 1]], 0, 1), iota(A("iot"), [[1, 256]])]
    silu = ac(A("col", 17, 18), A("col", 0, 1), AF.Silu, extra=1400.0, scale=2.0, bias=V + OFF)
    ops[-1]["lead"] = 90000.0
    for h in range(2):
        ops[iota(A("ring", 832 * h, 832 * h + 832), [[1, 52], [104, 16]], int(OFF) + 52 * h)]["after"] = early
    for a, b in ((4, 5), (0, 1)):
        ops[cp(A("nbp", 104 * a, 104 * b), A("ni", 104 * a, 104 * b))]["lead"] = 60000.0
    cv = PAR["cutv"]
    for k in range(8):
        for a, b in (((0, 52), (52, 104)) if k % 4 == 0 else ((0, cv), (cv, 104)) if k == 3 else ((0, 104),)):
            if (k, a) == (0, 52):
                piece = len(ops) - 1
                for c, d in ((5, 8), (1, 4)):
                    ops[cp(A("nbp", 104 * c, 104 * d), A("ni", 104 * c, 104 * d))]["after"] = [piece]
            w = IN(A("flat", (8 + k) * V, (8 + k) * V + V0), A("nbp", 104 * k + a, 104 * k + b))
            if k < 3 or (k, a) == (3, 0):
                ops[cp(w, A("ring", 16 * a, 16 * b))]["lead"] = 40000.0 if k == 0 else 0.0
            else:
                j = ac(w, A("ring", 16 * a, 16 * b), AF.Silu, after=[silu])
                silu = j if k == 4 else silu
        dma("Y", [(A("nb", 0, V0, p=row(8 + k)), A("flat", (8 + k) * V, (8 + k) * V + V0, p=row(k)))], 2500, 400.0)
        ops[-1]["wr"] = [("nb%d" % (8 + k), 0, 1)]
        if k == 0:
            after = len(ops) - 2
    cp(A("val", 0, 832), A("ni"))
    ops[-1].update(lead=30000.0, after=[after])
    dma("Y", [(A("nb", 0, V0, p=row(k)), A("val", 104 * k, 104 * k + 104)) for k in range(8)], 2500)
    ops[-1]["wr"] = [("nb0", 0, 1)]
    dma("Y", [(A("flat", k * V, k * V + V0, p=row(k)), A("val", 104 * k, 104 * k + 104)) for k in range(8)], 2500)
    NBS = [("nb%d" % s, 0, 1) for s in (0, 8, 9, 10, 11, 12, 13, 14, 15)]

    mk = start_masks(T, topo, rank)
    for name, part in (("ax", XV), ("as", lambda t, sd: ST("stall", t, sd))):
        trs = []
        for t in range(RO):
            rid, pid, _ = topo.addr(T.cores[(rank + 1 + t) % n])
            trs.append(RemoteDMATransfer(dst_ids=[DstId(rid=rid, pnc=pid)], dma_engine_mask=sum(1 << e for e in mk[t]), remote_sem=T.sem[name + str(t)],
                                         src=part(t, 0)[0], dst=part(t, 1)[0]))
        sent[0] += sum(len(m) for m in mk)
        s = op("G", (lambda trs=trs: g.remote_dma_fused(trs, local_sem=T.sem.sent)), costs["RC"], [part(t, 0) for t in range(RO)], [], kind="x", lat=3000.0)
        for t in range(RO):
            arrive(name + str(t), len(start_masks(T, topo, (rank - 1 - t) % n)[t]), part(t, 1), s)
    dma("G", [(A("ya", 0, V0), T.y0[:])], 4000)

    def C(i):
        return A("col", i, i + 1)
    P_, P16, P8, GB, P1, PH, T0, TOP, BOT, FST, GB16, T1, SV, P256, WC, TC, SW, JC, G18, SG = [C(i) for i in range(20)]
    for i, (c, o) in enumerate(((15, AL.bitwise_and), (3, AL.bitwise_and), (112, AL.bitwise_and), (1, AL.bitwise_and), (1, AL.arith_shift_right))):
        ts(A("pi", i + 1, i + 2), A("pi", 0, 1), c, o)
    cp(A("col", 1, 6), A("pi", 1, 6))
    ts(TOP, P16, 8.0, AL.is_lt)
    ts(BOT, P16, 8.0, AL.is_ge)
    ts(FST, P16, 0.0, AL.is_equal)
    TOFF, NOFF, BOFF = C(23), C(24), C(25)
    lin(TOFF, TOP, OFF)
    lin(NOFF, BOT, -OFF)
    lin(BOFF, BOT, OFF)
    lin(SW, FST, 8.0, P_)
    lin(T0, SW, 1.0, -1.0)
    lin(T1, SW, 1.0, 7.0)
    lin(SV, P8, float(V))
    lin(P256, P16, 16.0)
    lin(GB16, P_, 1.0, V0 + M)
    lin(G18, GB, 0.125, P_)
    lin(SG, TOP, 2.0, -1.0)
    io = lambda w, a=0: A("iot", a, a + w)
    iota(A("ones"), [[0, 128]], 1)
    iota(A("t1", 0, 8), [[16, 8]])
    iota(A("t4"), [[0, 8], [1, 16]])
    iota(A("kb"), [[0, 8], [1, 18]])
    iota(A("kb", 17, 144, 18), [[0, 8]], 1 << 20)
    iota(A("m17"), [[0, 8]], -17)
    iota(A("rst"), [[0, 144]])
    iota(A("rst", 0, 144, 18), [[0, 8]], 1 << 23)
    iota(A("nones", 0, 128), [[0, 128]], -1)
    dma("Y", [(A("nones", c, c + 128), A("nones", 0, 128)) for c in (128, 256, 384)], 2500)
    lin(A("lam"), A("ones"), -0.5)
    ts(IB, io(128), P_, AL.is_equal)
    lin(A("ibn"), IB, -1.0)
    lin(A("i3"), IB, 3.0)
    lin(A("iff"), IB, 1.0)
    lin(A("ifh"), IB, 0.5)
    ts(A("b8"), A("t1", 0, 8), GB, AL.is_equal)
    for nm, c in (("b64", 64.0), ("b64n", -64.0), ("b128", 128.0)):
        lin(A(nm), A("b8"), c)
    MT = A("mt", 0, 128)
    ts(MT, A("t4"), P16, AL.is_equal)
    dma("Y", [(A("mt", c, c + 128), MT) for c in (128, 256)], 2500)
    lin(A("negm"), MT, 2.0 ** 98, -2.0 ** 98)
    cp(A("bc", 0, 24), io(24))
    ts(A("bc", 24, 32), io(8), 18.0, AL.mult, 17.0, AL.add)
    ts(A("t2", 0, 144), io(144), -2.0, AL.add, G18, AL.is_equal)
    ts(A("dm"), io(144), -1.0, AL.add, G18, AL.is_equal)
    tt(A("dm"), A("t2", 0, 144), A("dm"), AL.subtract)
    op("V", lambda: vec.memset(A("wt")[0], 0.0), 45 + WT * 0.5 * CY, [], [A("wt")])
    ops[-1]["lead"] = 90000.0
    dma("Y", [(A(nm), A("wt", 0, A(nm)[4])) for nm in ("sq", "zb", "zero", "r8", "wz")], 2500)
    for q in range(4):
        pick(A("sq", 160 * q + 16 + 4 * q, 160 * q + 144 + 4 * q), [[-16, 8], [-1000, 4], [-1, 4]], -4 * q)
    pick(A("zb", 0, 1152, 16), [[-1, 8], [-16, 9]], 8)
    for e in range(2):
        pick(A("rf", e, 256, 2), [[-1, 8], [-8, 2], [-16, 8]], 0)
    lin(A("rfs"), A("rf"), SG)
    ts(A("selc", 0, 128), io(128), T0, AL.is_equal, TOP, AL.mult)
    ts(A("selc", 128, 256), io(128), T1, AL.is_equal, TOP, AL.mult)
    ts(A("h2"), io(64), PH, AL.is_equal)
    iota(A("t1", 16, 64), [[0, 3], [16, 8], [0, 2]])
    ts(A("b48"), A("t1", 16, 64), GB, AL.is_equal)
    lin(A("bp"), A("b48"), 1.0)
    lin(A("bp", 16, 32), A("b48", 16, 32), -1.0)
    for nm, c in (("bn", -1.0), ("bp2", 2.0), ("bn2", -2.0)):
        lin(A(nm), A("bp"), c)
    iota(A("par"), [[0, 16], [1, 2], [0, 8]])
    ts(A("par"), A("par"), P1, AL.is_equal)
    iota(A("bias", 0, 256), [[-1, 2], [0, 128]])
    lin(A("bias", 256, 384), A("par", 0, 128), 16384.0, -16384.0)
    iota(A("t2", 144, 208), [[1, 16], [256, 4]])
    iota(A("t2", 208, 256), [[1, 16], [256, 3]])
    ts(A("pil"), A("t2", 144, 256), P256, AL.add)
    lin(A("t3", 0, 128), A("ones"), 1.0 / 3.0)
    scan(A("t3", 128, 256), A("t3", 0, 128), A("zero"), float(3.0 ** 62), AL.mult, AL.add)
    tt(A("t3", 0, 128), A("t3", 128, 256), A("iff"), AL.mult)
    op("V", lambda: vec.tensor_reduce(WC[0], A("t3", 0, 128)[0], AxisListType.X, AL.add), 200, [A("t3", 0, 128)], [WC])
    lin(TC, WC, 2.2)
    lin(A("cw"), A("ones", 0, 16), WC)
    dma("Y", [(A("r8", 128 * q, 128 * q + 128, p=slice(16 * q, 16 * q + 16)), A("ones", p=slice(16 * q, 16 * q + 16))) for q in range(8)], 2500)
    for k in range(8):
        pick(A("rom", 32 * k, 32 * k + 32), [[8, 2], [-16, 8], [0, 2]], -8 - k)
    for sd in range(2):
        cp(A("p0", 24 * sd, 24 * sd + 24), A("stall", 24 * sd, 24 * sd + 24))
        d = A("d0", 384 * sd, 384 * sd + 384)
        tt(d, IN(A("xs", 0, V0), A("p0", 24 * sd, 24 * sd + 24)), A("xf") if sd else A("xs", V0, V), AL.subtract)
        ac(d, d, AF.Abs)
        tt(A("yy", 384 * sd, 384 * sd + 384), IN(A("stall", 24 * sd, 24 * sd + 24), A("bc", 0, 24)), A("mt"), AL.mult)
    for t in range(RO):
        lin(C(20 + t), P_, 1.0, V0 + M * t - OFF)
        shift("d" in PAR["sm"][t], A("dv", M * t, M * t + M), IB, C(20 + t), 1.0)
    iota(A("nb", V0, V), [[0, V - V0]], int(OFF))

    xw = A("xs")
    SQ = lambda q, h: A("sq", 160 * q + 16 + 4 * q - 4 * h, 160 * q + 144 + 4 * q - 4 * h)

    def nbg(i):
        ops[i]["rd"] += NBS
        return i

    def search(t, sd, d0, d1, kb):
        nbw = A("nb", 0, V0 + M * t)
        cs = lambda nm: A(nm, 128 * sd, 128 * sd + 128)
        ks = lambda nm, a=0, s=1: A(nm, 144 * sd + a, 144 * sd + 144, s)
        big = lambda nm, a, b, s=1: A("big", 4096 - 4096 * sd + 2048 * (nm == "sc") + a, 4096 - 4096 * sd + 2048 * (nm == "sc") + b, s)
        at = lambda nm: A(nm, 384 * sd + M * t, 384 * sd + M * t + M)
        for s in range(16):
            gcopy(big("rep", s, 2048, 16), XV(t, sd))
        p = ST("p0", t, sd)
        for h in range(2):
            if "cf"[sd] in PAR["sm"][t]:
                nbg(shift(True, cs("cf"), IN(nbw, p), 1.0, TOFF))
                ts(cs("c16"), cs("cf"), -OFF, AL.add)
            else:
                nbg(ts(cs("c16"), IN(nbw, p), NOFF, AL.add))
                nbg(shift(True, cs("cf"), IN(nbw, p), 1.0, TOFF))
            one = A(kb, 145, 288, 18)
            grp([(A(kb, 144, 288), cs("cf"), A("dm"))] + ([(one, at("yy"), A("b8")), (one, MT, A("b64"))] if h == 0 else [(one, A("iff"), ks("ee", 17, 18))]))
            stay = [(A(kb, 0, 144, 18), at("d0"), A("b64"))] if h == 0 else [(A(kb, 0, 144, 18), A("iff"), ks("s1", 17, 18)), (A(kb, 0, 144, 18), IB, A("m17"))]
            grp([(A(kb, 0, 144), IB, A("kb"))] + stay, stop=False)
            last = []
            way = PAR["far" if sd else "own"][t]
            for hv in [[0], [1]] if (way[0] == "S") != (way[1] == "S") else [[0, 1]]:
                a, b = 1024 * hv[0], 1024 * hv[-1] + 1024
                sums = lambda w, stop, a=a, b=b: grp([(A(kb, 1 + s, 144, 18, p=slice(a // 16, b // 16)),
                                                       A("mix", a + s, b, 16) if w == "b128" and not sd else big("sc", a + s, b, 16), A(w))
                                                      for s in range(16)], start=False, stop=stop)
                for i in hv:
                    x, lst = big("sc", 1024 * i, 1024 * i + 1024), IN(xw, A("c16", 128 * sd + 64 * i, 128 * sd + 64 * i + 64))
                    if way[i] == "R":
                        tt(x, lst, big("rep", 1024 * i, 1024 * i + 1024), AL.subtract)
                    if way[i] == "E":
                        shift(True, x, lst, -1.0, 0.0)
                        fold_dma(x, big("rep", 1024 * i, 1024 * i + 1024))
                    if way[i] == "S":
                        for u, bank in enumerate((d0, d1)):
                            c = 1024 * i + 512 * u
                            shift(True, big("sc", c, c + 512), IN(xw, A("c16", 128 * sd + c // 16, 128 * sd + c // 16 + 32)), -1.0, 0.0)
                            grp([(A(bank), IB, big("rep", c, c + 512))], stop=False)
                            grp([(A(bank), IB, big("sc", c, c + 512))], start=False)
                            ac(big("sc", c, c + 512), A(bank), AF.Abs)
                if way[hv[0]] != "S":
                    sums("b64n", False)
                    for u, v in ((a, b),) if way[hv[0]] == way[hv[-1]] else ((a, a + 1024), (a + 1024, b)):
                        relu(big("sc", u, v) if sd else A("mix", u, v), big("sc", u, v))
                last.append((sums, "b64" if way[hv[0]] == "S" else "b128"))
            for sums, w in last:
                sums(w, True)
            scan(ks("s1"), A("rst"), A(kb, 0, 144), 0.0, AL.add, AL.min)
            tt(ks("nf"), ks("s1"), A(kb, 0, 144), AL.not_equal)
            scan(ks("ee"), A(kb, 144, 288), ks("nf"), 0.0, AL.add, AL.mult)
            tt(cs("xx"), IN(ks("ee"), A("bc", 24, 32)), MT, AL.mult)
            mm([(A(kb, 288, 296), cs("xx"), A("b8"), True, True)])
            p = A("pr", 32 * t + 16 * h + 8 * sd, 32 * t + 16 * h + 8 * sd + 8)
            ts(p, A(kb, 288, 296), -OFF, AL.add)

    def nbrs(out, win, lst, e, off):
        for x, a, b in (("V", 0, 512), ("S", 512, 1024)) if e == "H" else ((e, 0, 1024),):
            shift(x == "S", A(out, a, b), IN(win, A(lst, a // 16, b // 16)), 1.0, off)

    pos = [16 * V]

    def room(w):
        a = pos[0] if pos[0] + w <= 12 * V + RING else 12 * V
        pos[0] = a + w
        return a

    chain = {"V": [], "S": []}
    for t in range(RO):
        old, have = V0 + M * t, V0 + M * (t + 1)
        SEC = lambda s, t=t: V * (s - 4 if t and s >= 12 else s)
        nbw = A("nb", 0, old)
        begun = len(ops)
        bl, pf = [A("pr", 32 * t + 16 + 8 * sd, 32 * t + 24 + 8 * sd) for sd in range(2)]
        search(t, 1, Y0, Y1, KF if t else Y3)
        for o in ops[begun:]:
            o.update(lead=PAR["flead"][t], part=t)
        first = len(ops)
        if PAR["early"][t]:
            shift("x" in PAR["sm"][t], A("xx", 128, 256), IN(nbw, pf), 1.0, TOFF)
            mm([c for z in range(2) for c in acc(A(KF, 296 + 64 * z, 360 + 64 * z), [(SQ(2 * z + u, 2 * h + u), A("xx", 128 + h, 256, 2)) for h in range(2) for u in range(2)])])
            ts(A("c16", 128, 256), A(KF, 296, 424), -OFF, AL.add)
        search(t, 0, D0, D1, KO)
        iota(A("val", 0, 512), [[1, 128], [0, 4]], old + int(OFF))
        DV = A("dv", M * t, M * t + M)
        gd = PAR["gd"][t]
        TT = D1 if t else KF
        wt = A("wt") if t else A("big", 0, 1920)
        dma("Y", [(wt, A("wz", 0, wt[4]))], 2500)
        if t:
            dma("Y", [(A("flat", SEC(s) + old - M, SEC(s) + old, p=FR(s)), A("nb", old - M, old, p=row(s))) for s in range(16) if s // 4 != 2 + t % 2], 2200, 50.0)
        XX = A("xx", 0, 128)
        shift("n" in PAR["sm"][t], A("nbb"), IN(nbw, bl), 1.0, TOFF)
        mm(acc(A(KO, 304, 368), [(A("selc", 128 * h, 128 * h + 128), A("nbb", h, 128, 2)) for h in range(2)]))
        ts(A("cq"), A(KO, 304, 368), -OFF, AL.add)
        nbrs("gg", nbw, "cq", PAR["gg"][t][0], TOFF)
        BC, BV, NG = (lambda a, b: A("rep", a, b)), (lambda a, b, s=1: A("mix", 2048 + a, 2048 + b, s)), (lambda a, b: A("mix", a, b))
        if gd:
            shift(gd[0] == "S", BC(0, 1024), IN(xw, A("cq")), 1.0, 0.0)
            ops[gcopy(BC(1024, 2048), BC(0, 1024))].update(comm=False, urgent=True)
            for k in range(8):
                gcopy(BV(k, 1024, 8), XV(t, 0))
            dma("Y", [(BV(1024, 2048), BV(0, 1024))], 2200, 500.0)
        else:
            shift(True, A("xcq"), IN(xw, A("cq")), 1.0, 0.0)
        GK = lambda k: A("gg", k, 1024, 8)
        RF = lambda nm, k, a, b, s=1: A(nm, 32 * k + a, 32 * k + b, s)
        mm([(A(KO, k, 256, 8), GK(k), RF("rf", k, 0, 32), True, True) for k in range(8)])
        tt(A("fam"), A(KO, 0, 256), A("par"), AL.mult)
        mm([(A(KO, 360 + 64 * u, 424 + 64 * u), A("fam", 128 * u, 128 * u + 128), A("h2"), True, True) for u in range(2)])
        ts(A("fa"), A(KO, 360, 488), -OFF, AL.add)
        mm([(A(D1, 384, 512), XX, IB, True, True)])
        shift("b" in PAR["sm"][t], A("brep"), A(D1, 384, 512), 1.0, 0.0)
        shift("b" in PAR["sm"][t], A("nbrep"), A("brep"), -1.0, 0.0)
        for u, bank in enumerate((D0, D1)):
            c = []
            for q in range(4):
                rg = A("r8", 128 * (4 * u + q), 128 * (4 * u + q) + 128)
                c += acc(A(bank, 128 * q, 128 * q + 128), [(rg, A("brep")), (A("nbrep"), rg)])
            mm(c)
            ts(A("eq", 512 * u, 512 * u + 512), A(bank), 0.0, AL.is_equal)
        EQ = lambda q: A("eq", 128 * q, 128 * q + 128)
        grp([(A(D0, 0, 128), IB, A("negm"))] + [(A(D0, 16 * q, 16 * q + 16), EQ(q), A("cw")) for q in range(8)])
        ts(A("nfx"), A(D0, 0, 128), TC, AL.is_ge, JC if t else GB16, AL.mult)
        tt(A("rlx"), A("nfx"), XX, AL.max)
        mm([(A(D1, 384, 392), A("rlx"), A("b8"), True, True)])
        cp(A("rl"), A(D1, 384, 392))
        grp([(A(TT, 0, 256), A("nbb"), A("selc")), (A(TT, 0, 256), DV, A("nones", 0, 256))]
            + [(A(TT, 120 * u + 8 + k, 128 * u + 128, 16), GK(k), RF("rf", k, 16 * u, 16 * u + 16, 2)) for k in range(8) for u in range(2)])
        mm([c for k in range(8) for c in acc(A(TT, 256 + k, 384, 8), [(GK(k), RF("rfs", k, 16 * u, 16 * u + 16)) for u in range(2)])])
        r8v = lambda a, b: A("rep", 2 * a, 2 * b, 2)
        keys = lambda nm, o, sg: [(A(KO, k, 384, 8), A(nm, o + k, o + 1024, 8), A(sg)) for k in range(8)]
        far = PAR["gf"][t] == "S" and not gd
        fl, al = IN(xw, A("fa", 0, 64)), IN(xw, A("fa", 64, 128))
        grp([(A(KO, 0, 384), IB, A("bias"))] + (keys("xcq", 0, "bp") + [(A(KO, k, 384, 8), XV(t, 0), A("bn")) for k in range(8)] if far else []), stop=False)
        gains = len(ops)
        if gd:
            for u, lst in enumerate((fl, al)):
                shift(gd[1 + u] == "S", NG(1024 * u, 1024 * u + 1024), lst, -1.0, 0.0)
            parts = [(x, 1024 * u, 1024 * u + 1024) for u in range(2) for x in (BC, BV)]
            for x, a, b in parts:
                fold_dma(x(a, b), NG(a, b))
            for x, a, b in parts:
                relu(x(a, b), x(a, b))
            for i, (nm, o, sg) in enumerate((("rep", 0, "bp"), ("mix", 2048, "bn"), ("rep", 1024, "bn"), ("mix", 3072, "bp"))):
                grp(keys(nm, o, sg), start=False, stop=i == 3)
        else:
            tt(BV(1024, 2048), al, r8v(0, 1024), AL.max, after=[tt(BV(0, 1024), al, A("xcq"), AL.max)])
            if far:
                for u in range(2):
                    ac(A("ab", 512 * u, 512 * u + 512), IN(xw, A("fa", 32 * u, 32 * u + 32)))
                for o, sub in (("xcq", lambda u: A("xcq", 512 * u, 512 * u + 512)), ("ab", lambda u: r8v(512 * u, 512 * u + 512))):
                    for u, bank in enumerate((D0, D0 if t else D1)):
                        grp([(A(bank), A("ibn"), sub(u))], stop=False)
                        grp([(A(bank), IB, A("ab", 512 * u, 512 * u + 512))], start=False)
                        ac(A(o, 512 * u, 512 * u + 512), A(bank), AF.Abs)
            else:
                tt(A("ab"), fl, A("xcq"), AL.max)
                tt(A("xcq"), fl, r8v(0, 1024), AL.max)
            grp(keys("mix", 2048, "bn2" if far else "bn"), start=False, stop=False)
            grp(keys("mix", 3072, "bp2" if far else "bp"), start=False, stop=False)
            grp(keys("xcq", 0, "bp" if far else "bn"), start=False, stop=False)
            grp(keys("ab", 0, "bn" if far else "bp"), start=False)
        ts(A("indp"), A(KO, 256, 384), 0.0, AL.is_ge)
        ts(A("dw"), A(KO, 0, 256), 0.0, AL.is_ge, WC, AL.mult)
        tt(A("ot"), A("indp"), A(TT, 256, 384), AL.mult)
        mm(acc(A(D0, 0, 64), [(A("fam", 128, 256), A("h2")), (A("ot"), A("h2"))]))
        ts(A("o16"), A(D0, 0, 64), -OFF, AL.add)
        mm([(A(D1, 384 + 16 * q + 8 * z, 392 + 16 * q + 8 * z), EQ(q), A("dw", 128 * z + 16 * q, 128 * z + 16 * q + 8), True, True) for q in range(8) for z in range(2)])
        shift(True, A("wts"), A(D1, 384, 512), 1.0, 0.0)
        mm([(A(D1, 384, 512), A("wts"), IB, True, True)])
        shift(True, A("wrow"), A(D1, 384, 512), 1.0, 0.0)
        grp([(A(KO, 0, 256), A("zero"), A("nones", 0, 256))] + [(A(KO, 128 * z, 128 * z + 128), A("i3"), A("dw", 128 - 128 * z, 256 - 128 * z)) for z in range(2)]
            + [(A(KO, 16 * q, 16 * q + 16), EQ(q % 8), A("dw", 16 * q, 16 * q + 16)) for q in range(16)], stop=False)
        nbrs("gg", nbw, "o16", PAR["gg"][t][1], 0.0)
        mm(acc(A(D0, 64, 128), [(A("zb", 144 * ((r + 1) % 8) + 16 - r, 144 * ((r + 1) % 8) + 144 - r), A("gg", r, 1024, 16)) for r in range(16)]))
        cp(A("b16"), A(D0, 64, 128))
        cp(IN(wt, A("rl")), A("wrow"))
        nbrs("gw", wt, "b16", PAR["gg"][t][2], 0.0)
        grp([(A(KO, k, 256, 8), A("gw", k, 1024, 8), A("rom", 32 * k, 32 * k + 32)) for k in range(8)], start=False)
        ts(A("mw"), A(KO, 0, 256), TC, AL.is_lt)
        tt(A("zz"), A("mw"), A(TT, 0, 256), AL.mult)
        mm(acc(A(D0, 128, 256), [(A("ones"), DV), (A("zz", 0, 128), IB), (A("zz", 128, 256), IB)]))
        shift("t" in PAR["sm"][t], A("thh"), A(D0, 128, 256), 1.0, -OFF)
        mm([c for q in range(4) for c in acc(A(D1, 32 * q, 32 * q + 32), [(SQ(q, h), A("thh", h, 128, 4)) for h in range(4)])])
        ts(A("sl"), A(D1, 0, 128), SV, AL.add)
        direct = PAR["direct"][t]
        back = lambda ss, a, b: ops[dma("Y", [(A("nb", a, b, p=row(s)), A("flat", SEC(s) + a, SEC(s) + b, p=FR(s))) for s in ss],
                                        1900 + (0.275 if len(ss) > 4 else 0.2) * len(ss) * (b - a), 0.155 * (b - a))].update(comm=True)
        at = lambda s: 512 * (s % 8 < 4) + 256 * (s // 8) + 64 * (s % 4)
        for q in range(2):
            ts(IN(A("flat", 4 * q * V, 4 * q * V + 4 * V), A("sl", 32 * q, 32 * q + 32)), A("val", 0, 512), 1.0, AL.mult, -OFF, AL.add)
            u = 1 - q if t == 2 else q
            ss = range(8 + 4 * u, 12 + 4 * u)
            w = IN(A("flat", SEC(ss[0]), SEC(ss[0]) + 4 * V), A("sl", 64 + 32 * u, 96 + 32 * u))
            j = either(True, lambda: ac(w, A("val", 0, 512), AF.Silu), lambda: cp(w, A("val", 0, 512)))
            for ks in (((0,), (1, 2, 3)), ((4, 5, 6, 7),))[q] if direct else ():
                dma("Y", [(A("val", at(s), at(s) + 64), A("flat", SEC(s), SEC(s) + 1024, p=FR(s))) for k in ks for s in (8 + k, k)], 1900 + 400 * len(ks), 160.0)
                for z in (8, 0):
                    ts(A("off", 64 * (z + ks[0]), 64 * (z + ks[-1] + 1)), A("val", at(z + ks[0]), at(z + ks[-1]) + 64), -OFF if z else 0.0, AL.add)
            if t and q:
                ops[j]["rd"].append(("turn", 0, 1))
            elif t:
                back(ss, 0, old)
                i = dma("Y", [(A("flat", SEC(s), SEC(s) + old, p=FR(s)), A("nb", 0, old, p=row(s))) for s in range(12 - 4 * u, 16 - 4 * u)], 1900 + 0.8 * old, 0.155 * old)
                ops[i].update(wr=[("turn", 0, 1)], rd=[], hard=[j])
        nbg(mm(acc(A(D0, 256, 384), [(SQ(q, (q + 2) % 4), A("thh")) for q in range(4)])))
        shift(True, A("nb", old, have), A(D0, 256, 384), 1.0, BOFF)
        W = (64, 48 if have == 1792 else 64)
        for a, b in ((0, 1024), (1024, old))[::-1 if direct else 1]:
            back(range(8), a, b)
            back(ss if t else range(8, 16), a, b)
        for r in range(direct, 2):
            a, w, l = 1024 * r, W[r], (0 if W[r] == 64 else 64)
            ts(A("nbp", a, a + 16 * w), IN(A("nb", a, a + 16 * w), A("pil", l, l + w)), NOFF, AL.add)
            for ks in ((0,), (1, 2), (3, 4), (5, 6, 7)) if r == 0 else ((0, 1, 2, 3), (4, 5, 6, 7)):
                dma("Y", [(A("off", a + w * s, a + w * s + w), A("nbp", a, a + 16 * w, p=row(s))) for k in ks for s in (8 + k, k)], 1900 + 250 * len(ks))
        OL = lambda s, a, b: A("off", (a - a % 1024) + W[a // 1024] * s + a % 1024 // 16, (a - a % 1024) + W[a // 1024] * s + (b - a + a % 1024) // 16)
        for i in range(first, len(ops)):
            ops[i].update(lead=PAR["lead"][t], round=t, part=(4 if i < gains else 2) + t if t else -1)
        for o in ops[begun:]:
            if t and o["eng"] == "G" and o["kind"] == "c" and "urgent" not in o:
                o.update(lead=PAR["glead"], part=7)
        if t + 1 == RO:
            dma("Y", [(T.nx[k::8, :], A("nb", p=row(k))) for k in range(8)], 3000)
        if PAR["early"][t]:
            yw = A("yb", 0, old)
            shift(True, A("ys"), IN(yw, pf), 0.5, 0.0)
            c = room(1024)
            shift(True, A("flat", c, c + 1024), IN(yw, A("c16", 192, 256)), -0.0625, 0.0)
            tt(A("flat", c, c + 1024), IN(yw, A("c16", 128, 192)), A("flat", c, c + 1024), AL.mult)
            mm(acc(A(KF, 0, 128), [(A("iff"), A("ys"))] + [(A("iff"), A("flat", c + k, c + 1024, 8)) for k in range(8)]))
            shift(True, A("ys"), A(KF, 0, 128), 1.0, 0.5)
        else:
            shift(True, A("ys"), IN(A("ya", 0, old), pf), 1.0, 0.0)
        to = T.cores[(rank - 1 - t) % n]
        rid, pid, _ = topo.addr(to)
        sent[0] += len(topo.engines(core, to))
        s = op("G", (lambda a=A("ya", old, have)[0], rid=rid, pid=pid, m=topo.mask(core, to), t=t:
                     g.remote_dma(a, A("ys")[0], T.sem["ay%d" % t], T.sem.sent, pid, rid, m)), 1500, [A("ys")], [], kind="x", sem=T.sem.sent, cnt=sent[0], lat=2500.0)
        arrive("ay%d" % t, len(topo.engines(T.cores[(rank + 1 + t) % n], core)), A("ya", old, have), s)
        for sw in range(2):
            src, dst = ("ya", "yb") if sw == 0 else ("yb", "ya")
            yw = A(src, 0, have)
            chunks, a = [], 0
            for w, plan in PAR["plan"][2 * t + sw]:
                chunks.append((a, a + w, plan))
                a += w
            over = lambda q: [c for c in chunks if c[0] < 512 * q + 512 and c[1] > 512 * q]
            banks = {}

            def term(q, lo, hi, lhs, rhs, turn=False):
                b, bank = banks[q], (Y0, Y1, Y2, Y3)[q]
                calls = [(A(bank, lo - 512 * q, hi - 512 * q), rhs)]
                if turn:
                    calls = [(A(bank, 64 * i, 64 * i + 64), A(rhs[1], rhs[2] + 8 * q + i, rhs[3], 16)) for i in range(8)]

                def fn(b=b, first=not b["ops"]):
                    b["left"] -= 1
                    for c in calls:
                        r = pe.matmul(c[0][0], lhs[0], c[1][0], first, b["left"] == 0 and c is calls[-1])
                    return r
                b["left"] += 1
                j = op("P", fn, 40 + max(64, hi - lo) * (4 if SB[rhs[1]][1] == F else 1) * PE, [lhs, rhs], [A(bank, lo - 512 * q, hi - 512 * q)])
                if b["ops"]:
                    ops[j]["grp"] = b["ops"][0]
                b["ops"].append(j)

            late = [ci for ci, c in enumerate(chunks) if c[2][8] == "e"]
            places = [[] for c in chunks]
            for ci, ks in [(ci, range(7 if ci in late else 8)) for ci in range(len(chunks))] + [(ci, (7,)) for ci in late]:
                a, b, plan = chunks[ci]
                parts = [(q, max(a, 512 * q), min(b, 512 * q + 512)) for q in range(a // 512, (b + 511) // 512)]
                for q, lo, hi in parts if ks[0] == 0 else []:
                    if q not in banks:
                        top = min(have, 512 * q + 512)
                        banks[q] = dict(ops=[], left=0, mu=0.0, ev=[])
                        if any(c[2][9] == "V" for c in over(q)):
                            banks[q]["mu"] = 0.5
                            term(q, 512 * q, top, A("lam", p=slice(0, 1)), A("nones", 0, top - 512 * q, p=slice(0, 1)))
                        term(q, 512 * q, top, A("ifh"), A(src, 512 * q, top))
                place = places[ci]
                for k in ks:
                    place.append((dst, 1024 * k) if t == sw == ci == 0 and k < 2 else ("flat", room(b - a)))
                    pr = lambda i, lo=a, hi=b: A(place[i][0], place[i][1] + lo - a, place[i][1] + hi - a)
                    hd = PAR["head"][2 * t + sw] if ci == 0 and k == 0 else 0
                    for lo, hi in ((a, a + hd), (a + hd, b)) if hd else ((a, b),):
                        chain["S"] = [ac(pr(k, lo, hi), IN(yw, OL(8 + k, lo, hi)), after=chain["S"], scale=-0.0625)]
                        chain["V"] = [tt(pr(k, lo, hi), IN(yw, OL(k, lo, hi)), pr(k, lo, hi), AL.mult, after=chain["V"])]
                    ops[chain["S"][0]]["cut"] = ci == 0 and k == 0
                    if plan[k + 1].isdigit():
                        fold_dma(pr(int(plan[k + 1])), pr(k))
                    for i in range(k + 1):
                        if plan[i + 1] == "p" and max(i, plan.rfind(str(i), 1, 9) - 1) == k:
                            for q, lo, hi in parts:
                                term(q, lo, hi, A("iff"), pr(i) if direct and ci == 0 else pr(i, lo, hi), direct and ci == 0)
                for q, lo, hi in parts if ks[-1] == 7 else []:
                    cut = hi - PAR["end"] if (t, sw, hi) == (RO - 1, 1, V) else hi
                    banks[q]["ev"] += [(u, v, plan[9], pr(7, u, v)) for u, v in ((lo, cut), (cut, hi)) if u < v]
                    if len(banks[q]["ev"]) >= len(over(q)):
                        for lo, hi, e, more in sorted(banks[q]["ev"], key=lambda e: e[0]):
                            bk = A((Y0, Y1, Y2, Y3)[q], lo - 512 * q, hi - 512 * q)
                            if e != "V":
                                shift(e == "S", A(dst, lo, hi), bk, 1.0, 0.5 - banks[q]["mu"])
                            else:
                                tt(A(dst, lo, hi), bk, more, AL.add)
                            ops[-1]["hard"] = list(banks[q]["ops"])
                            if t == RO - 1 and sw == 1:
                                dma("Y", [(T.y[:, lo:hi], A(dst, lo, hi))], 2000 + 1.0 * (hi - lo))
    return ops, sent[0]


def depend(ops):
    hist = {}
    for i, o in enumerate(ops):
        deps = set(o["after"])
        soft = set(o["after"])
        for regs, w in ((o["rd"], False), (o["wr"], True)):
            for nm, a, b in regs:
                for j, a2, b2, w2 in hist.get(nm, ()):
                    if w and w2 and o.get("comm") and ops[j].get("comm"):
                        continue
                    if nm[:2] == "ps" and o.get("grp", -1) == ops[j].get("grp", -2):
                        continue
                    if j != i and ((nm[:2] == "ps" and (ops[j]["eng"] != o["eng"] or o["eng"] == "P" or "alt" in o or "alt" in ops[j])) or ((w or w2) and a < b2 and a2 < b)):
                        deps.add(j)
                        soft.discard(j)
                        if "fold" in ops[j] and w2 and "cons" not in ops[j]:
                            ops[j]["cons"] = i
        for regs, w in ((o["rd"], False), (o["wr"], True)):
            for nm, a, b in regs:
                h = hist.setdefault(nm, [])
                if w and nm[:2] != "ps" and not o.get("comm"):
                    h[:] = [e for e in h if not (a <= e[1] and e[2] <= b)]
                if nm[:2] == "ps":
                    h[:] = [e for e in h if e[0] != i][-12:]
                h.append((i, a, b, w))
        deps |= set(o.get("hard", ())) | set([o["grp"]] if "grp" in o else []) | set([o["fold"]] if o.get("fold", -1) >= 0 else [])
        for j in list(deps):
            while "fold" in ops[j] and ops[j]["cons"] != i:
                deps.discard(j)
                j = ops[j]["cons"]
                deps.add(j)
        known = done = 0
        for j in deps:
            if j not in soft and not o["eng"] == ops[j]["eng"] == "P":
                known |= ops[j]["done"] ^ 1 << j
            elif o["kind"] == ops[j]["kind"] == "c":
                known |= ops[j]["known"]
                done |= ops[j]["done"]
        deps = [j for j in deps if not known >> j & 1]
        o["known"] = known | sum(1 << j for j in deps if j not in soft and not o["eng"] == ops[j]["eng"] == "P")
        o["done"] = o["known"] | done | 1 << i
        o["deps"], o["soft"] = sorted(deps), soft


def schedule(ops, other):
    n, K = len(ops), range(len(other))
    num = ["VSPGYR".index(o["eng"]) for o in ops]
    link = [[(j, 0.0 if num[j] == num[i] and (num[i] == 2 or j in o["soft"]) else 1.0) for j in o["deps"]] for i, o in enumerate(ops)]
    succ = [[] for _ in ops]
    for i, b in enumerate(link):
        for j, h in b:
            succ[j].append((i, h))
    pre = [set(o["deps"]) for o in ops]
    call = [[(num[i], [(j, c[3] * h) for j, h in b], c[0][i], c[1][i], c[2][i]) for i, b in enumerate(link)] for c in other]
    rnd = np.random.RandomState(PAR["seed"])
    home = num[:]

    def flip(i):
        num[i] = 1 - num[i]
        for k in K:
            call[k][i] = (num[i], call[k][i][1], other[k][0 if num[i] == home[i] else 4][i], 0.0, 0.0)

    def assign(engines):
        for i in range(n):
            if num[i] != engines[i]:
                flip(i)

    def play(part, k, state, end):
        free, cl = list(state), call[k]
        for i in part:
            e, ln, dur, lat, xfer = cl[i]
            t = free[e]
            for j, w in ln:
                if end[j] + w > t:
                    t = end[j] + w
            free[e] = t = t + dur
            if lat:
                t += lat
                if xfer:
                    free[6] = t = max(t, min(free[6], t + 4000.0) + xfer)
            end[i] = t
        return free

    def length(seq, engines):
        assign(engines)
        x = 0.0
        for k in K:
            end = [0.0] * n
            play(seq, k, [0.0] * 7, end)
            x += math.log(max(end)) * PAR["weight"][k]
        return x

    def listed(c, key):
        dur, lat, xfer, wake = c
        left, rdy, free, moved, seq = [len(b) for b in link], [0.0] * n, [0.0] * 6, 0.0, []
        ready = [[i for i in range(n) if not left[i] and num[i] == e] for e in range(6)]
        first = [0.0 if r else 1e18 for r in ready]
        for _ in ops:
            now, e = min((max(first[x], free[x]), x) for x in range(6))
            i = max((i for i in ready[e] if rdy[i] <= now + PAR["look"]), key=lambda i: key[i])
            ready[e].remove(i)
            first[e] = min([rdy[j] for j in ready[e]] + [1e18])
            t = free[e] = max(now, rdy[i]) + dur[i]
            t += lat[i]
            if xfer[i]:
                moved = t = max(t, min(moved, t + 4000.0) + xfer[i])
            seq.append(i)
            for j, h in succ[i]:
                rdy[j] = max(rdy[j], t + wake * h)
                left[j] -= 1
                if not left[j]:
                    ready[num[j]].append(j)
                    first[num[j]] = min(first[num[j]], rdy[j])
        return seq

    def keyed():
        c = rnd.dirichlet([4.0] * len(other))
        c = [[float(x) for x in sum(m * np.array(y[k]) for m, y in zip(c, other))] for k in range(3)] + [100.0]
        bl = [0.0] * n
        for i in range(n - 1, -1, -1):
            bl[i] = max([bl[j] + c[3] * h for j, h in succ[i]] + [0.0]) + c[0][i] + c[1][i]
        now = 1e9
        for m in range(PAR["tries"]):
            if m < PAR["tries"] // 8:
                lead = dict((p, PAR["span"] * (rnd.rand() - 0.5)) for p in range(8))
                new = [bl[i] + o.get("lead", 0.0) + lead.get(o.get("part"), 0.0) for i, o in enumerate(ops)]
            else:
                a, w, d = rnd.randint(n), int(rnd.choice((1, 4, 10, 30, 80))), float(rnd.choice((1000, 3000, 10000)) * rnd.randn())
                e = num[a] if rnd.rand() < 0.5 else -1
                new = key[:a] + [x + d if e in (-1, num[a + i]) else x for i, x in enumerate(key[a:a + w])] + key[a + w:]
            seq = listed(c, new)
            x = length(seq, home)
            if x <= now:
                key, now, keep = new, x, seq
        return keep, home

    def polish(start, passes):
        W, tau = PAR["wide"], PAR["soft"]
        seq, best = start[0], 1e18
        assign(start[1])
        for p in range(passes + 1):
            free, end, at = [0.0] * 7, [0.0] * n, [0.0] * n
            for i in seq:
                free = play((i,), p % len(other), free, end)
                at[i] = free[num[i]] - call[p % len(other)][i][2]
            seq = sorted(seq, key=lambda i: at[i])
            ends, tails, total = [[0.0] * n for k in K], [], []
            for k in K:
                free, eff, tail, nxt = [0.0] * 7, [0.0] * n, [0.0] * n, [0.0] * 6
                for i in seq:
                    free = play((i,), k, free, ends[k])
                    eff[i] = ends[k][i] - free[num[i]]
                for i in seq[::-1]:
                    t = eff[i] + max([other[k][3] * h + tail[j] for j, h in succ[i]] + [0.0])
                    tail[i] = nxt[num[i]] = call[k][i][2] + max(t, nxt[num[i]])
                tails.append(tail)
                total.append(max(ends[k]))
            x = sum(math.log(t) * w for t, w in zip(total, PAR["weight"]))
            if x < best:
                best, keep = x, (seq, num[:])
            if p == passes:
                return keep
            warm = PAR["heat"] * (1.0 - p / passes) ** 2
            state, a, skew = [[0.0] * 7 for k in K], 0, int(rnd.randint(W // 2))
            while a < n - 4:
                b = min(n, (a or -skew) + W)
                part = seq[a:b]
                m, inside, behind, outs = len(part), set(part), {}, []
                for i in seq[b:b + 400]:
                    behind.setdefault(num[i], i)
                for k in K:
                    o = [(i, max([other[k][3] * h + tails[k][j] for j, h in succ[i] if j not in inside] + [0.0]) - total[k]) for i in part]
                    outs.append(([x for x in o if ends[k][x[0]] + x[1] > -9000.0], [(e, tails[k][j] - total[k]) for e, j in behind.items()]))

                def worth(part, k, v, marks):
                    end, marks = ends[k], marks[:v // 8 + 1]
                    for c in range(v // 8 * 8, m, 8):
                        marks.append(play(part[c:c + 8], k, marks[-1], end))
                    z = 1e-9 + sum([math.exp((end[i] + t) / tau) for i, t in outs[k][0]]) + sum([math.exp((marks[-1][e] + t) / tau) for e, t in outs[k][1]])
                    return tau * math.log(z) * 2.6e5 / total[k] * PAR["weight"][k], marks

                now = [worth(part, k, 0, [state[k]]) for k in K]
                old = [[ends[k][i] for i in part] for k in K]
                c = PAR["moves"]
                for u, way, far, luck in zip(rnd.randint(m, size=c).tolist(), rnd.rand(c).tolist(), rnd.choice((1, 1, 1, 2, 2, 3, 5), size=c).tolist(), rnd.rand(c).tolist()):
                    e, v, d = num[part[u]], u, -1 if way < 0.5 else 1
                    turn = part[u] if far == 5 and other[0][4][part[u]] else -1
                    while far and 0 <= v + d < m and turn < 0:
                        v += d
                        far -= num[part[v]] == e
                    if turn >= 0:
                        flip(turn)
                        along, new = [], part
                    elif num[part[v]] != e or v == u:
                        continue
                    elif d < 0:
                        need, along, rest = set(pre[part[u]]), [part[u]], []
                        for i in part[u - 1:v - 1 if v else None:-1]:
                            if i in need:
                                along.append(i)
                                need |= pre[i]
                            else:
                                rest.append(i)
                        new = part[:v] + along[::-1] + rest[::-1] + part[u + 1:]
                    else:
                        need, along, rest = {part[u]}, [part[u]], []
                        for i in part[u + 1:v + 1]:
                            if pre[i] & need:
                                along.append(i)
                                need.add(i)
                            else:
                                rest.append(i)
                        new = part[:u] + rest + along + part[v + 1:]
                    if part[v] in along:
                        continue
                    v, trial, d = min(u, v), [], 0.0
                    for k in K:
                        trial.append(worth(new, k, v, now[k][1]))
                        d += trial[k][0] - now[k][0]
                        if d > warm * luck + 100.0 * (len(other) - 1 - k):
                            break
                    if d <= warm * luck:
                        part, now = new, trial
                        old = [[ends[k][i] for i in part] for k in K]
                    else:
                        if turn >= 0:
                            flip(turn)
                        v = v // 8 * 8
                        for k in range(len(trial)):
                            for i, t in zip(part[v:], old[k][v:]):
                                ends[k][i] = t
                seq = seq[:a] + part + seq[b:]
                c = b - W + W // 2 if b < n else n
                state = [play(seq[a:c], k, state[k], ends[k]) for k in K]
                a = c

    def cross(seqs):
        cuts = [i for i, o in enumerate(ops) if o.get("cut")]
        best, top = seqs[0], length(*seqs[0])
        for c in cuts[::-1] + cuts:
            for s in seqs:
                for a, b in ((best, s), (s, best)):
                    head = a[0][:a[0].index(c)]
                    done = set(head)
                    new = (head + [i for i in b[0] if i not in done], [(a if i in done else b)[1][i] for i in range(n)])
                    x = length(*new)
                    if x < top:
                        best, top = new, x
        return best

    found = []
    for _ in range(PAR["keyed"]):
        assign(home)
        found.append(polish(keyed(), PAR["first"]))
    seq, engines = polish(cross(found), PAR["passes"])
    return dict((e, [i for i in seq if engines[i] == x]) for x, e in enumerate("VSPGYR"))


def rank_program(g, core, T, topo):
    if T.rank_of(core) is None:
        return
    ops, sent = build(g, core, T, topo, COSTS[0])
    depend(ops)
    if not ORDER:
        alts = [build(g, core, T, topo, c)[0] for c in COSTS]
        ORDER.update(schedule(ops, [([o["dur"] for o in alt], [o["lat"] for o in alt], [o.get("xfer", 0.0) for o in alt], c["LAT"],
                                     [o["alt"]["dur"] if "alt" in o else 0.0 for o in alt]) for alt, c in zip(alts, COSTS)]))
    order = ORDER
    for e in "VS":
        for i in order[e]:
            if ops[i]["eng"] != e:
                ops[i].update(eng=e, fn=ops[i]["alt"]["fn"])
    total = {}
    for e in "VSPG":
        c = 0
        for i in order[e]:
            if ops[i]["kind"] == "c":
                c += 1
                ops[i]["sem"], ops[i]["cnt"], ops[i]["key"] = T.sem["c" + e], c, e
        total[e] = c
    for i, o in enumerate(ops):
        if o["kind"] != "c":
            o["key"] = "sent" if o["kind"] == "x" else o.get("key", i)
    knows, place, waited, left = dict((e, {}) for e in order), dict((e, 0) for e in order), {}, len(ops)
    while left:
        for e in order:
            while place[e] < len(order[e]) and all("knew" in ops[j] for j in ops[order[e][place[e]]]["deps"]):
                o, know = ops[order[e][place[e]]], knows[e]
                o["waits"] = []
                for j in o["deps"][::-1] if e != "R" else ():
                    d = ops[j]
                    if j in o["soft"] or (e == "P" and d["eng"] == "P") or d["cnt"] <= know.get(d["key"], 0):
                        continue
                    o["waits"] = [w for w in o["waits"] if w[2] != d["key"]] + [(d["sem"], d["cnt"], d["key"])]
                    for k, c in d["knew"].items():
                        know[k] = max(know.get(k, 0), c)
                for s, c, k in o["waits"]:
                    waited[k] = max(waited.get(k, 0), c)
                o["knew"] = dict(know)
                o["knew"][o["key"]] = max(o["cnt"], know.get(o["key"], 0))
                place[e] += 1
                left -= 1
    for e, q in (("V", g.vector), ("S", g.scalar), ("P", g.tensor), ("Y", g.sync), ("G", g)):
        for i in order[e]:
            o = ops[i]
            for s, c, k in o["waits"]:
                q.wait_ge(s, c)
            r = o["fn"]()
            if o["kind"] == "c":
                r.then_inc(o["sem"], 1)
    last = dict((o["key"], o) for o in ops if o["kind"] in "dr")
    if sent > waited.get("sent", 0):
        g.wait_ge(T.sem.sent, sent)
    for e in "GPSV":
        if total[e] > waited.get(e, 0):
            g.wait_ge(T.sem["c" + e], total[e])
    for o in last.values():
        if o["cnt"] > waited.get(o["key"], 0):
            g.wait_ge(o["sem"], o["cnt"])
